import numpy as np, ml_dtypes
CORES = [40,41,42,43,44,45,46,47]
N = 8
BF = ml_dtypes.bfloat16
W, C, RO, SH = 8192, 256, 4, 5
def parts(rng):
    cov = np.where(rng.random((N, 8, 1, W)) < 0.15, 0, rng.integers(0, 256, (N, 8, 16, W)))
    share = rng.choice(np.array([0.0, 0.1, 0.2, 0.3, 0.5, 0.8]), (N, 8, 1, C))
    tst = np.where(rng.random((N, 8, 16, C)) < share, 256, rng.integers(0, 256, (N, 8, 16, C)))
    return cov, tst, rng.integers(0, 160, (N, 8, 16, C)), rng.integers(200, 2000, (N, 8))
def pack(cov, tst, pr, th):
    return {"cov": np.ascontiguousarray(cov.reshape(N, 128, W)).astype(np.float32).astype(BF), "tst": np.ascontiguousarray(tst.reshape(N, 128, C)).astype(np.int32),
            "pr": np.ascontiguousarray(pr.reshape(N, 128, C)).astype(np.float32).astype(BF), "th": np.ascontiguousarray(th.reshape(N, 8, 1)).astype(np.int32)}
def setup_inputs(rng):
    return pack(*parts(rng))
def setup_inputs_corners(rng):
    cov, tst, pr, th = parts(rng)
    c = np.arange(C); lane = np.arange(16)[:, None]; full = rng.integers(0, 256, (N, 8, 16, C))
    th = rng.choice(np.array([0, 1, 500, 4080]), (N, 8))
    for r in range(N):
        for g in range(8):
            k = (g + r) % 8; x = full[r, g]
            if k == 1: x = np.full((16, C), 256)
            elif k == 2: x = np.where(lane == c % 16, 256, x)
            elif k == 3: x = np.where((lane + c) % 2 == 1, 256, x)
            elif k == 4:
                x = np.repeat(x[:, :1], C, axis=1); pr[r, g] = np.repeat(pr[r, g][:, :1], C, axis=1); th[r, g] = 0
            elif k == 5: x = np.where((lane == c % 16) | (lane == (c + 1) % 16), x, 256)
            elif k == 6:
                cov[r, g][:, rng.random(W) < 0.7] = 0; th[r, g] = 0
            elif k == 7: pr[r, g] = 255 * rng.integers(0, 2, (1, C))
            tst[r, g] = x
    q = rng.permutation(N); th[q[0]] = 0; th[q[1]] = 4080
    r = int(q[0]); g = (8 - r) % 8
    cov[r, g, 0] = 0; cov[r, g, 1:] = rng.integers(1, 256, (15, W))
    pr[r, g, :, 0::2] = 255; pr[r, g, :, 1::2] = 0
    k = np.arange(C // 2); p = 1 + k % 14; v = rng.integers(0, 256, (2, C // 2)); x = np.full((16, C), 256)
    for odd in range(2):
        x[p, 2 * k + odd] = v[0]; x[p + 1, 2 * k + odd] = v[1]
    tst[r, g] = x
    return pack(cov, tst, pr, th)
def pairs(rng, low):
    x = rng.integers(0, 256, 2 ** 15); y = rng.integers(0, 256, 2 ** 15); i = rng.integers(0, 16, 2 ** 15)
    col, at = np.unique(((((2 * x + 1) * (2 * y + 1)) >> 4) + 613 * i) & (W - 1), return_index=True)
    at = rng.permutation(at[col >= low])
    return x[at], y[at], i[at]
def lone(rng, x, y, i):
    k = len(x); c = np.arange(k); v = np.full((16, k), 256)
    v[i, c] = x; v[(i + 1) & 15, c] = y
    for d in range(3, 15, 2): v[(i + d) & 15, c] = rng.integers(0, 256, k)
    return v
def setup_inputs_crowd(rng):
    cov, tst, pr, th = parts(rng)
    a = int(rng.integers(0, N)); b = (a + 1) % N; d = (a + 2) % N
    v = rng.integers(0, 256, (8, 16, C)); v[:, [1, 5, 7, 9, 11, 13, 15]] = 256
    tst[a] = v; th[a] = rng.integers(511, 1500, 8); th[b] = 0; th[d] = 0
    cov[b] = rng.integers(1, 256, (8, 16, W)); cov[d] = rng.integers(1, 256, (8, 16, W))
    c = np.arange(C); second = ((c % 2 == 0) & (c > 0)) | (c == C - 1)
    for g in range(8):
        p = np.append(rng.permutation(C - 1)[:31], C - 1)
        few = ((((2 * v[g, 2, p] + 1) * (2 * v[g, 3, p] + 1)) >> 4) + 613 * 2) & (W - 1)
        most = ((((2 * v[g, 3, p] + 1) * (2 * v[g, 4, p] + 1)) >> 4) + 613 * 3) & (W - 1)
        cov[a, g][:, few] = 255; cov[a, g][int(rng.integers(0, 16)), few] = 254; cov[a, g][:, most] = 255
        x, y, i = pairs(rng, 0)
        tst[b, g] = lone(rng, x[:C], y[:C], i[:C])
        x, y, i = pairs(rng, W - 254 if g == 7 else 0)
        o = (c + 1) // 2; o[C - 1] = 0; o = np.where(o > 0, 1 + (o - 1) % (len(x) - 1), 0)
        tst[d, g] = lone(rng, x[o], y[o], i[o])
        lev = rng.integers(0, 16, C // 2)[o]; lev = np.where(second, (lev + rng.integers(1, 16, C)) & 15, lev)
        pr[d, g] = np.where(np.arange(16)[:, None] == lev[None, :], 0, 255)
    return pack(cov, tst, pr, th)
def setup_inputs_ties(rng):
    unit = np.where(np.arange(8) % 4 == 1, 1, 85).reshape(1, 8, 1, 1)
    cov = unit * np.where(rng.random((N, 8, 1, W)) < 0.5, rng.integers(0, 4, (N, 8, 1, W)), rng.integers(0, 4, (N, 8, 16, W)))
    pr = unit * np.where(rng.random((N, 8, 1, C)) < 0.5, rng.integers(0, 2, (N, 8, 1, C)), rng.integers(0, 2, (N, 8, 16, C)))
    few = rng.choice(np.array([0, 1, 64, 128, 255, 256]), (N, 8, 16, C)); many = np.where(rng.random((N, 8, 16, C)) < 0.2, 256, rng.integers(0, 256, (N, 8, 16, C)))
    tst = np.where(rng.random((N, 8, 1, C)) < 0.5, few, many)
    return pack(cov, tst, pr, unit[..., 0, 0] * rng.integers(0, 24, (N, 8)))
def setup_inputs_spread(rng):
    cov = np.minimum((np.exp2(8 * rng.random((N, 8, 1, W))) * rng.random((N, 8, 16, W)) * 1.01).astype(np.int64), 255)
    pr = np.minimum((np.exp2(8 * rng.random((N, 8, 16, C))) * rng.random((N, 8, 1, C))).astype(np.int64), 255)
    tst = np.minimum((256 * rng.random((N, 8, 16, C)) ** rng.choice(np.array([0.25, 1.0, 4.0]), (N, 8, 16, 1))).astype(np.int64), 255)
    tst = np.where(rng.random((N, 8, 16, C)) < rng.random((N, 8, 1, C)) * 0.6, 256, tst)
    th = np.minimum(np.exp2(12 * rng.random((N, 8))).astype(np.int64) - 1, 4080)
    return pack(cov, tst, pr, th)
def setup_inputs_ends(rng):
    kind = rng.integers(0, 3, (N, 8, 1, W)); cov = 255 * np.where(kind == 2, rng.integers(0, 2, (N, 8, 16, W)), kind)
    lane = np.arange(16)
    for t in range(RO):
        z = (613 * lane + 77 * t) & (W - 1); f = ((511 * 511 >> 4) + 613 * lane + 77 * t) & (W - 1)
        cov[..., z] = 255; cov[..., f] = 0; cov[..., f[15]] = 255; cov[:, ::2, :, f[6]] = 255
    u = rng.random((N, 8, 16, C))
    tst = np.where(u < 0.5, 0, np.where(u < 0.7, 256, np.where(u < 0.9, 255, rng.integers(0, 256, (N, 8, 16, C)))))
    tst[..., [2, C - 1]] = 0; tst[..., [5, C - 2]] = 255; tst[..., [1, C - 3]] = 256
    pr = 255 * rng.integers(0, 2, (N, 8, 16, C))
    pr[..., [2, 5, C - 2, C - 1]] = 255; pr[:, :, 15, [2, 5, C - 2, C - 1]] = 0; pr[:, 1::2, 4, [2, C - 1]] = 0
    o = np.argsort(rng.random((N, 8)), axis=1); th = 4080 * (o < rng.integers(3, 6, (N, 1))).astype(np.int64)
    th[N - 1, 7] = 4080; th[N - 1, 0] = 0
    return pack(cov, tst, pr, th)
def check_inputs(d):
    bad = []
    for k, lo, hi in (("cov", 0, 255), ("tst", 0, 256), ("pr", 0, 255), ("th", 0, 4080)):
        v = np.asarray(d[k]).astype(np.float64)
        if not (np.min(v) >= lo and np.max(v) <= hi): bad.append("range of " + k)
        elif np.any(v != np.floor(v)): bad.append("whole numbers in " + k)
    return bad
def reference(cov, tst, pr, th):
    U = cov.astype(np.float32).astype(np.int64).reshape(N, 8, 16, W); T = tst.astype(np.int64).reshape(N, 8, 16, C)
    price = pr.astype(np.float32).astype(np.int64).reshape(N, 8, 16, C); lim = th.astype(np.int64).reshape(N, 8, 1)
    lane = np.arange(16).reshape(1, 16, 1); last = np.zeros(N, np.int64)
    for t in range(RO):
        rho = (5 * t) & 15; now = np.zeros(N, np.int64)
        for r in range(N):
            s = (r + t) % N
            x = T[r]; y = np.roll(x, -(1 + t), axis=1)
            live = (x != 256) & (y != 256)
            code = ((((2 * x + 1) * (2 * y + 1)) >> 4) + 613 * lane + 77 * t) & (W - 1)
            got = np.take_along_axis(U[s], code.reshape(8, 1, 16 * C), 2).reshape(8, 16, 16, C)
            gain = np.add.reduce(np.where(live[:, None], np.maximum(got - price[s][:, :, None, :], 0), 0), axis=2)
            lev = np.argmax(gain, axis=1); best = np.max(gain, axis=1)
            useful = best >= lim[s] + (last[s] & 255); now[s] = np.sum(~useful)
            some = np.any(live, axis=1)
            vote = np.argmax(np.where(live, np.add.reduce(got, axis=1), -1), axis=1)
            taken = np.take_along_axis(code, vote[:, None, :], 1)[:, 0] >> SH
            most = np.argmax(np.where(live, np.take_along_axis(got, lev[:, None, None, :], 1)[:, 0], -1), axis=1)
            credit = np.take_along_axis(code, most[:, None, :], 1)[:, 0]
            none = x == 256; first = np.argmax(none, axis=1)
            new = np.array(x)
            g, c = np.nonzero(~useful & some & np.any(none, axis=1))
            new[g, first[g, c], c] = taken[g, c]
            new[:, rho] = np.where(useful, 16 * lev + (best & 15), 256)
            for g in range(8):
                c = np.nonzero(useful[g] & some[g])[0]
                col, at = np.unique(credit[g, c], return_index=True)
                U[s, g, lev[g, c[at]], col] = 0
            T[r] = new
        last = now
    left = np.add.reduce(U.reshape(N, 128, W // 16, 16), axis=3)
    return {"yt": T.reshape(N, 128, C).astype(np.float32), "yc": left.astype(np.float32)}

@@ -1,0 +1,541 @@
+from concourse.mybir import AluOpType as A, AxisListType, ActivationFunctionType as F
+
+NONE = 2.0 ** 19
+W = 8192
+TR = 8192
+VOID = 8448
+UW = 8464
+SQ = 20480.0
+NS = 32
+K1R, K2R = 56, 48
+RHO = [0, 5, 10, 15]
+
+SCRATCH = {}
+
+
+def _b(name, cols, dtype, where="sbuf"):
+    SCRATCH[name] = (where, [128] + (list(cols) if isinstance(cols, (list, tuple)) else [cols]), dtype)
+
+
+for _n, _c in (("U", UW), ("got", 4096), ("Mx", 4096), ("PX", 4096), ("D0C", 512), ("BLKN", 128), ("D0G", 128), ("D0V", 128), ("segm", 256),
+               ("T0", 256), ("T1", 256), ("T2", 256), ("T3", 256), ("T4", 256), ("Tn0", 256), ("Tn1", 256), ("Tn2", 256), ("Tn3", 256),
+               ("Tt", 256), ("Nn", 256), ("prb", 256), ("prb2", 128), ("FT", 256), ("FT2", 256), ("rhs", 256), ("lhs", 256),
+               ("lhsE", 256), ("lhsO", 256), ("Xs", 256), ("vals", 256), ("mt0", 512), ("mt1", 512), ("mt2", 512), ("mt3", 512),
+               ("mt4", 512), ("mt5", 512), ("onesb", 256), ("I1", 128), ("I256", 128), ("nI", 128), ("nI16", 128), ("Ind", 8), ("MQ", 256),
+               ("SEL", 240), ("CC", 128), ("CTa", 128), ("CP", 128), ("CX", 128), ("zb", 128), ("m16", 4),
+               ("RT", 512), ("TNb", 128), ("TN", 512), ("CT", 512), ("FE", (2, K1R)), ("FE2", (2, K2R))):
+    _b(_n, _c, "bfloat16")
+for _n, _c in (("xx", 256), ("pd", 256), ("GKs", (2, 128)), ("VKs", (2, 128)), ("TH0", (2, 8)),
+               ("TH", (2, 8)), ("TH20", (2, 8)), ("TH2", (2, 8)), ("Z", 256), ("dm", 256), ("D1", 256),
+               ("BLK", 128), ("TM", 256), ("mif", 256), ("mf", 256), ("mgf", 128), ("w8", 8), ("colsf", 40), ("pw", 16), ("pw2", 16),
+               ("half", 16), ("msum", 4), ("junk", 16), ("yt32", 256), ("yc32", 512), ("ysc", 2048), ("mi2", 128), ("q1", 128), ("q2", 128), ("s0", 128), ("s1", 128), ("s2", 128), ("s3", 128)):
+    _b(_n, _c, "float32")
+for _n, _c in (("tsti", 256), ("z", 256), ("ci", 256), ("GKi", (2, 8)), ("DEC", (2, 24)), ("VKi", (2, 8)), ("tki", (2, 8)),
+               ("A1", 256), ("A2", 256), ("thr", 8), ("thb", 8), ("mi", 128), ("ri", 128), ("pc", 8)):
+    _b(_n, _c, "int32")
+for _n, _c in (("K1", 4096), ("R", 256), ("If", 128), ("nIf", 128), ("hib", 256)):
+    _b(_n, _c, "float16")
+for _n, _c in (("off", 256), ("l2u", 16)):
+    _b(_n, _c, "uint16")
+for _n in "ABCDEFGH":
+    _b("b" + _n, 512, "float32", "psum")
+
+SEMAPHORES = ["cv", "cs", "ct", "cg", "loc"] + ["d%d" % k for k in range(10)] + ["a%d" % k for k in range(1, 5)]
+
+
+def rank_program(g, core, T, topo):
+    rank = T.rank_of(core)
+    if rank is None:
+        return
+    N = len(T.cores)
+    eng = {"v": g.vector, "s": g.scalar, "t": g.tensor, "g": g, "y": g.sync}
+    cnt = {"v": 0, "s": 0, "t": 0, "g": 0}
+    known = {q: {} for q in eng}
+    clk = {}
+    wr, rd, bank = {}, {}, {}
+    ndma = [0]
+
+    def sem_of(e):
+        return T.sem["c" + e] if e in cnt else T.sem[e]
+
+    def need(q, deps):
+        best = {}
+        for e, n in deps:
+            if known[q].get(e, 0) < n and best.get(e, 0) < n:
+                best[e] = n
+        for e in list(best):
+            for e2 in list(best):
+                if e2 != e and e in best and e2 in best and clk.get((e2, best[e2]), {}).get(e, 0) >= best[e]:
+                    del best[e]
+        for e, n in best.items():
+            eng[q].wait_ge(sem_of(e), n)
+            for k, v in clk.get((e, n), {}).items():
+                if known[q].get(k, 0) < v:
+                    known[q][k] = v
+            known[q][e] = n
+
+    def deps_of(q, reads, writes):
+        deps = []
+        for t in list(reads) + list(writes):
+            if t[0] == "b":
+                for e, n in bank.get(t, {}).items():
+                    if e != q:
+                        deps.append((e, n))
+        for t in reads:
+            w = wr.get(t)
+            if w is not None and not (t[0] == "b" and w[0] != q):
+                deps.append(w)
+        for t in writes:
+            if t[0] != "b":
+                w = wr.get(t.rstrip("+"))
+                if w is not None and not (t[-1] == "+" and w[0] == q):
+                    deps.append(w)
+                deps.extend(rd.get(t.rstrip("+"), {}).items())
+        return deps
+
+    def note(q, e, n, reads, writes):
+        c = dict(known[q])
+        c[e] = n
+        clk[(e, n)] = c
+        for t in reads:
+            if t[0] == "b":
+                bank.setdefault(t, {})[e] = n
+            else:
+                rd.setdefault(t, {})[e] = n
+        for t in writes:
+            t = t.rstrip("+")
+            if t[0] == "b":
+                bank.setdefault(t, {})[e] = n
+            else:
+                rd[t] = {}
+            wr[t] = (e, n)
+
+    def op(q, fn, reads, writes):
+        reads = reads.split()
+        writes = writes.split()
+        need(q, deps_of(q, reads, writes))
+        ins = fn()
+        cnt[q] += 1
+        ins.then_inc(T.sem["c" + q], 1)
+        note(q, q, cnt[q], reads, writes)
+
+    def dma(q, out, in_, reads, writes):
+        reads = reads.split()
+        writes = writes.split()
+        need(q, deps_of("dma", reads, writes))
+        name = "d%d" % ndma[0]
+        ndma[0] += 1
+        eng[q].dma_start(out, in_).then_inc(T.sem[name], 16)
+        note(q, name, 16, reads, writes)
+
+    V, S, P = g.vector, g.scalar, g.tensor
+
+    def ts(out, in0, s1, s2, op0, op1, r, w):
+        if op1 is None:
+            op("v", lambda: V.tensor_scalar(out, in0, s1, None, op0), r, w)
+        else:
+            op("v", lambda: V.tensor_scalar(out, in0, s1, s2, op0, op1), r, w)
+
+    def tt(out, a, b, o, r, w):
+        op("v", lambda: V.tensor_tensor(out, a, b, o), r, w)
+
+    def cp(out, in_, r, w):
+        op("v", lambda: V.tensor_copy(out, in_), r, w)
+
+    def scan(out, d0, d1, o0, o1, r, w, init=0.0):
+        op("v", lambda: V.tensor_tensor_scan(out, d0, d1, init, o0, o1), r, w)
+
+    def act(out, in_, func, r, w, **k):
+        op("s", lambda: S.activation(out, in_, func, **k), r, w)
+
+    def mm(out, l, x, st, sp, r, w):
+        op("t", lambda: P.matmul(out, l, x, st, sp), r, w)
+
+    def ms(ap, c, w):
+        op("v", lambda: V.memset(ap, c), "", w)
+
+    def sel(out, in_, pat, cmp, fill, base, cm, r, w):
+        op("g", lambda: g.affine_select(out, in_, pat, cmp, fill, base, cm), r, w)
+
+    dma("y", T.tsti[:], T.tst[:], "", "tsti")
+    dma("s", T.prb[:], T.pr[:], "", "prb")
+    dma("y", T.thr[0:1, 0:8], T.th[:], "", "thr")
+    dma("y", T.U[:, 0:4096], T.cov[:, 0:4096], "", "Ua")
+    dma("s", T.U[:, 4096:W], T.cov[:, 4096:W], "", "Ub")
+    UALL = "Ua Ub Uc"
+
+    PI, PG, PP, OD, EV, SK, BK, CL, CR, N14, R14, R15, HB, PH = range(14)
+    KC, RC_ = 16, 20
+    BP = [[-1, 8], [0, 16]]
+    FL = {"allow_small_or_imprecise_dtypes": True}
+
+    def col(k):
+        return T.colsf[:, k:k + 1]
+
+    def iota(out, pat, base, cm, w, **k):
+        op("g", lambda: g.iota(out, pat, base, cm, **k), "", w)
+
+    iota(T.pc[:, 0:1], [[0, 1]], 0, 1, "pc0")
+    iota(T.ri[:], [[1, 128]], 1, 0, "ri")
+    iota(T.mgf[:], [[1, 8], [0, 16]], 0, 0, "mgf", **FL)
+    iota(T.mif[:], [[0, 16], [1, 16]], 0, 0, "mif", **FL)
+    iota(col(PP), [[0, 1]], 0, 1, "f2", **FL)
+    iota(T.mf[:], [[1, 256]], 0, 0, "mf", **FL)
+    iota(T.q1[:], [[0, 8], [-1, 16]], 7, 0, "q1", **FL)
+    iota(T.w8[:], [[1, 8]], 0, 0, "w8", **FL)
+    iota(col(PH), [[0, 1]], 128, 1, "f13", **FL)
+    op("g", lambda: g.partition_broadcast(T.thb[:], T.thr[0:1, 0:8], 128), "thr", "thb")
+
+    ms(T.onesb[:], 1.0, "onesb")
+    ms(T.zb[:], 0.0, "zb")
+    ms(T.CTa[:], 0.0, "CTa")
+    ms(T.CC[:], 0.0, "CC")
+    ts(T.pc[:, 1:2], T.pc[:, 0:1], 15, None, A.bitwise_and, None, "pc0", "pc1")
+    ts(T.pc[:, 2:3], T.pc[:, 0:1], 4, None, A.arith_shift_right, None, "pc0", "pc2")
+    ts(T.pc[:, 3:4], T.pc[:, 0:1], 4, 1, A.arith_shift_right, A.bitwise_and, "pc0", "pc3")
+    cp(col(PI), T.pc[:, 1:2], "pc1", "f0")
+    cp(col(PG), T.pc[:, 2:3], "pc2", "f1")
+    cp(col(OD), T.pc[:, 3:4], "pc3", "f3")
+    ts(T.BLK[:], T.mgf[:], col(PG), None, A.is_equal, None, "mgf f1", "BLK")
+    ts(T.mi[:], T.ri[:], 15, None, A.bitwise_and, None, "ri", "mi")
+    ts(T.mi2[:], T.mi[:], col(PI), 2.0, A.is_equal, A.mult, "mi f0", "mi2")
+    tt(T.RT[:, 0:128], T.mi2[:], T.BLK[:], A.mult, "mi2 BLK", "RT0")
+
+    def rot(t):
+        s, n = 1 + t, "RT%d" % t
+        b = T.RT[:, 128 * t:128 * t + 128]
+        sel(b, T.zb[:], [[-16, 8], [-1, 16]], A.not_equal, 2.0, -s, 1, "zb", n)
+        sel(b, b, [[-16, 8], [-1, 16]], A.not_equal, 2.0, 16 - s, 1, n, n)
+        sel(b, b, [[-16, 8], [0, 16]], A.is_ge, 0.0, 0, 1, n, n)
+        sel(b, b, [[16, 8], [0, 16]], A.is_ge, 0.0, 15, -1, n, n)
+
+    def codes_start():
+        mm(T.bA[:, 0:256], T.onesb[0:1, 0:128], T.onesb[0:1, 0:256], True, False, "onesb", "bA")
+
+    def codes_y(t):
+        src = "T%d" % t
+        mm(T.bA[:, 0:256], T.RT[:, 128 * t:128 * t + 128], T[src][:], False, True, "RT%d %s" % (t, src), "bA")
+
+    def codes_x(t):
+        src = "T%d" % t
+        act(T.xx[:], T[src][:], F.Identity, src, "xx", scale=2.0, bias=1.0)
+
+    HALVES = [(h, slice(128 * h, 128 * h + 128)) for h in range(2)]
+
+    def codes(t):
+        for h, c in HALVES:
+            tt(T.pd[:, c], T.bA[:, c], T.xx[:, c], A.mult, "bA xx", "pd%d" % h)
+        for h, c in HALVES:
+            ts(T.z[:, c], T.pd[:, c], col(KC + t), 2.0 ** 30, A.add, A.min, "pd%d fk%d" % (h, t), "z%d" % h)
+        for h, c in HALVES:
+            ts(T.ci[:, c], T.z[:, c], 4, 8191 | 0x7FFF8000, A.arith_shift_right, A.bitwise_and, "z%d" % h, "ci%d" % h)
+
+    def offsets():
+        for h, c in HALVES:
+            ts(T.off[:, c], T.ci[:, c], float(VOID), None, A.min, None, "ci%d" % h, "off+")
+
+    codes_start()
+    m128 = T.mf[:, 0:128]
+    ts(T.segm[:], T.mif[:], 0.0, None, A.is_gt, None, "mif", "segm")
+    ts(col(KC), col(PI), 16.0 * 613, None, A.mult, None, "f0", "fk0")
+    ts(T.I1[:], m128, col(PP), None, A.is_equal, None, "mf f2", "I1")
+    ts(T.If[:], m128, col(PP), None, A.is_equal, None, "mf f2", "If")
+    ts(T.nIf[:], m128, col(PP), -1.0, A.is_equal, A.mult, "mf f2", "nIf")
+    act(T.BLKN[:], T.BLK[:], F.Copy, "BLK", "BLKN", scale=NONE)
+    for k in range(2):
+        act(T.D0C[:, 256 * k:256 * k + 256], T.segm[:], F.Identity, "segm", "D0C+", scale=2.0 ** 20 + 1, bias=-2.0 ** 20)
+    act(T.s0[:], T.q1[:], F.Copy, "q1", "s0", scale=16384.0)
+    act(T.q2[:], T.q1[:], F.Square, "q1", "q2", bias=8.0)
+    act(T.s2[:], T.q1[:], F.Copy, "q1", "s2", scale=-512.0)
+    act(T.s1[:], T.q2[:], F.Identity, "q2", "s1", scale=-8192.0, bias=8192.0 * 65)
+    ts(T.pd[:], T.tsti[:], 256.0, NONE, A.is_ge, A.mult, "tsti", "pd0 pd1")
+    tt(T.T0[:], T.pd[:], T.tsti[:], A.max, "pd0 pd1 tsti", "T0")
+    codes_y(0)
+    codes_x(0)
+    act(T.s3[:], T.q2[:], F.Identity, "q2", "s3", scale=256.0, bias=-16384.0)
+    act(T.dm[:], T.mf[:], F.Copy, "mf", "dm", scale=1.0 / 1024)
+    act(T.I256[:], T.I1[:], F.Copy, "I1", "I256", scale=256.0)
+    act(T.nI[:], T.I1[:], F.Copy, "I1", "nI", scale=-4096.0)
+    codes(0)
+    offsets()
+    for i in range(16):
+        if i < 6:
+            act(T.PX[:, i:4096:16], T.prb[:], F.Copy, "prb", "PXs+")
+        else:
+            cp(T.PX[:, i:4096:16], T.prb[:], "prb", "PXv+")
+    act(T.nI16[:], T.I1[:], F.Copy, "I1", "nI16", scale=-16.0)
+    act(T.D0G[:], T.segm[:, 0:128], F.Identity, "segm", "D0G", scale=2.0 ** 25 + 16, bias=-2.0 ** 25)
+    act(T.D0V[:], T.segm[:, 0:128], F.Identity, "segm", "D0V", scale=2.0 ** 27 + 256, bias=-2.0 ** 27)
+    ms(T.U[:, W:VOID], 0.0, "Uc+")
+    ms(T.U[:, VOID:UW], -128.0, "Uc+")
+    cp(T.prb2[:, 0:128 - NS], T.prb[:, 128:256 - NS], "prb", "prb2+")
+    ms(T.prb2[:, 128 - NS:128], 0.0, "prb2+")
+    ts(T.Ind[:], T.w8[:], col(PG), 256.0, A.is_equal, A.mult, "w8 f1", "Ind")
+    for h in range(2):
+        ts(T.TH0[:, h, :], T.thb[:], 256.0, -SQ, A.mult, A.add, "thb", "TH0+")
+    act(T.TH20[:], T.TH0[:], F.Identity, "TH0", "TH20", bias=SQ)
+    ts(col(RC_), col(PI), float(RHO[0]), NONE, A.is_equal, A.mult, "f0", "fr0")
+    ms(T.FE[:, :, 48:56], 1.0, "F6")
+    ms(T.FE2[:, :, 40:48], 1.0, "E5")
+
+    def fills(n, rows, items):
+        for f, v in items:
+            sel(T[n][0:rows, :], T[n][0:rows, :], BP, A.not_equal, v, -8 * f, 1, n, n)
+
+    def tn(t):
+        sel(T.TN[:, 128 * t:128 * t + 128], T.TNb[:], [[0, 8], [1, 16]], A.not_equal, 0.0, -RHO[t], 0, "TNb", "TN%d" % t)
+
+    def ct(t):
+        n, a = "CT%d" % t, 128 * t
+        sel(T.CT[0:K2R, a:a + 128], T.CTa[0:K2R, :], [[0, 8], [1, 16]], A.not_equal, 0.0, -RHO[t], 0, "CTa", n)
+        c = T.CT[0:K2R, a + RHO[t]:a + 128:16]
+        for f, v in ((0, -16.0), (1, 1.0), (2, NONE), (5, 240.0)):
+            sel(c, c, [[-1, 8]], A.not_equal, v, -8 * f, 1, n, n)
+
+    sel(T.s0[0:K1R, :], T.s0[0:K1R, :], BP, A.is_equal, 0.0, 0, 1, "s0", "s0")
+    sel(T.s1[0:K1R, :], T.s1[0:K1R, :], BP, A.is_equal, 0.0, -8 * 6, 1, "s1", "s1")
+    sel(T.s2[0:K1R, :], T.s2[0:K1R, :], BP, A.is_equal, 0.0, -8, 1, "s2", "s2")
+    sel(T.s3[0:K1R, :], T.s3[0:K1R, :], BP, A.is_equal, 0.0, -8 * 6, 1, "s3", "s3")
+    fills("s0", K1R, [(2, -8192.0)])
+    fills("s2", K1R, [(3, 256.0)])
+    fills("CTa", K2R, [(4, 1.0)])
+    fills("s0", K1R, [(4, -8192.0)])
+    fills("CTa", K2R, [(2, -NONE)])
+    fills("CC", K1R, [(2, 2.0 ** 17)])
+    fills("CTa", K2R, [(3, NONE)])
+    fills("CC", K1R, [(0, 2.0 ** 17)])
+    fills("CTa", K2R, [(5, 2 * NONE)])
+    fills("CC", K1R, [(4, 2.0 ** 17)])
+    sel(T.TNb[:], T.BLKN[:], [[1, 128]], A.is_gt, 0.0, 0, -1, "BLKN", "TNb")
+    sel(T.TNb[:], T.TNb[:], [[1, 128]], A.not_equal, -NONE, 0, -1, "TNb", "TNb")
+    tn(0)
+    fills("CC", K1R, [(5, 1.0)])
+    ct(0)
+    fills("CC", K1R, [(6, 201.0 * 8192)])
+
+    def late_columns():
+        ms(T.half[:], 0.5, "half")
+        ms(T.pw2[:], 0.0, "pw2")
+        ts(col(R14), col(PI), 14.0, None, A.is_equal, None, "f0", "f10")
+        ts(col(R15), col(PI), 15.0, None, A.is_equal, None, "f0", "f11")
+        ts(col(HB), col(PI), 14.0, 0.5, A.is_lt, A.mult, "f0", "f12")
+        scan(T.pw[:], T.half[:], T.pw2[:], A.mult, A.add, "half pw2", "pw", 2.0)
+        tt(col(CL), col(HB), col(R14), A.subtract, "f12 f10", "f7")
+        tt(col(CR), col(HB), col(R15), A.subtract, "f12 f11", "f8")
+        ts(T.pw2[:], T.mif[:, 0:16], col(PI), None, A.is_equal, None, "mif f0", "pw2")
+        ts(col(N14), col(R14), -1.0, None, A.mult, None, "f10", "f9")
+        tt(T.pw[:], T.pw[:], T.pw2[:], A.mult, "pw pw2", "pw")
+        op("v", lambda: V.tensor_reduce(col(SK), T.pw[:, 0:14], AxisListType.X, A.add), "pw", "f5")
+        ts(T.bH[:, 0:256], T.dm[:], col(R15), col(CL), A.mult, A.add, "dm f11 f7", "bH")
+        ts(T.bH[:, 256:512], T.dm[:], col(N14), col(CR), A.mult, A.add, "dm f9 f8", "bH")
+        ts(col(BK), col(SK), 0.5, -0.5, A.mult, A.add, "f5", "f6")
+
+    def late_tiles():
+        for k in range(1, 4):
+            ts(col(KC + k), col(PI), 16.0 * 613, 16.0 * 77 * k, A.mult, A.add, "f0", "fk%d" % k)
+            ts(col(RC_ + k), col(PI), float(RHO[k]), NONE, A.is_equal, A.mult, "f0", "fr%d" % k)
+        ts(T.MQ[:], T.mif[:], col(PI), None, A.is_equal, None, "mif f0", "MQ")
+        ts(T.TM[:], T.mf[:], float(TR), None, A.add, None, "mf", "TM")
+        ms(T.SEL[:, 0:112], 0.0, "SEL+")
+        ms(T.SEL[:, 128:240], 0.0, "SEL+")
+        ms(T.SEL[:, 112:128], 2.0 ** 24, "SEL+")
+        tt(T.TM[:], T.TM[:], T.MQ[:], A.mult, "TM MQ", "TM")
+
+    late_columns()
+
+    def fe(f, n=1):
+        return T.FE[:, :, 8 * f:8 * (f + n)]
+
+    def fe2(f, n=1):
+        return T.FE2[:, :, 8 * f:8 * (f + n)]
+
+    ALLF = " ".join("F%d" % k for k in range(7)) + " I1"
+    ALLE = " ".join("E%d" % k for k in range(6)) + " I1"
+    GB, VB = [T.bA, T.bB], [T.bC, T.bD]
+    GN, VN = ["bA", "bB"], ["bC", "bD"]
+    win = T.U[:, 0:UW]
+    FT, FT2 = T.FT[0:K1R, :], T.FT2[0:K2R, :]
+    X0 = 4096 - 16 * NS
+
+    def gains(h, t):
+        a, b = 2048 * h, 2048 * h + 2048
+        mm(GB[h][:, 0:128], T.prb[:, 0:128] if h == 0 else T.prb2[:], T.nI[:], True, False, ("prb" if h == 0 else "prb2") + " nI", GN[h])
+        for i in range(16):
+            mm(GB[h][:, 0:128], T.Mx[:, a + i:b:16], T.I256[:], False, False, ("Mx0" if h == 0 else "Mx1 Mx2") + " I256", GN[h])
+
+    def votes(h):
+        a, b = 2048 * h, 2048 * h + 2048
+        mm(VB[h][:, 0:128], T.hib[:, 128 * h:128 * h + 128], T.If[:], True, False, "hib If", VN[h])
+        for i in range(16):
+            mm(VB[h][:, i:128:16], T.got[:, a + i:b:16], T.Ind[:], False, i == 15, ("got0" if h == 0 else "got1 got2") + " Ind", VN[h])
+
+    for t in range(4):
+        src = "T%d" % t
+        for k, a, b in ((2, X0, 4096), (0, 0, 2048), (1, 2048, X0)):
+            act(T.got[:, a:b], win.indirect(T.off[:, a // 16:b // 16]), F.Identity, "off " + UALL, "got%d" % k, scale=16.0, bias=-2048.0)
+            if k == 0:
+                mm(T.bG[:], T.nI16[:], T.PX[:, X0:4096], True, False, "nI16 PXs PXv", "bG")
+                mm(T.bG[:], T.I1[:], T.got[:, X0:4096], False, True, "I1 got2", "bG")
+                act(T.Mx[:, X0:4096], T.bG[:], F.Relu, "bG", "Mx2", scale=1.0 / 16, bias=128.0)
+        op("v", lambda: V.tensor_tensor(T.Mx[:, 0:2048], win.indirect(T.off[:, 0:128]), T.PX[:, 0:2048], A.max),
+           "off PXs PXv " + UALL, "Mx0")
+        ts(T.hib[:], T.off[:], 1.0 / 32, 1024.0 - 0.484375, A.mult, A.add, "off", "hib")
+        op("v", lambda: V.tensor_tensor(T.Mx[:, 2048:X0], win.indirect(T.off[:, 128:256 - NS]), T.PX[:, 2048:X0], A.max),
+           "off PXs PXv " + UALL, "Mx1")
+        gains(0, t)
+        votes(0)
+        gains(1, t)
+        votes(1)
+        act(T.Nn[:], T[src][:], F.Relu, src, "Nn", bias=1.0 - NONE)
+        act(T.Tt[:], T[src][:], F.Identity, src + " fr%d" % t, "Tt", bias=col(RC_ + t))
+        def payload(h):
+            c = slice(2048 * h + 15, 2048 * h + 2048, 16)
+            ts(T.R[:, 128 * h:128 * h + 128], T.K1[:, c], SQ - 7.5, SQ - 2288.0, A.add, A.max, "K1%d" % h, "R%d" % h)
+            mm(GB[h][:, 0:128], T.K1[:, c], T.If[:], False, False, "K1%d If" % h, GN[h])
+            mm(GB[h][:, 0:128], T.R[:, 128 * h:128 * h + 128], T.nIf[:], False, True, "R%d nIf" % h, GN[h])
+
+        def best(h):
+            scan(T.GKs[:, h, :], T.D0G[:], GB[h][:, 0:128], A.add, A.max, "D0G " + GN[h], "GKs+")
+
+        for h in (0, 1, 2, 3, 7, 4, 5, 6):
+            a, b = 512 * h, 512 * h + 512
+            scan(T.K1[:, a:b], T.D0C[:], T.got[:, a:b], A.add, A.max, "D0C got%d" % (2 if h == 7 else h // 4), "K1%d+" % (h // 4))
+            if h == 7:
+                payload(0)
+        best(0)
+        payload(1)
+        mm(T.bF[:, 0:256], T.TN[:, 128 * t:128 * t + 128], T.Nn[:], True, False, "TN%d Nn" % t, "bF")
+        best(1)
+        gk = T.GKs[:, :, 15:128:16]
+        th, thn = (T.TH0, "TH0") if t == 0 else (T.TH, "TH")
+        th2, thn2 = (T.TH20, "TH20") if t == 0 else (T.TH2, "TH2")
+        ts(T.GKi[:], gk, SQ, 240.0, A.add, A.max, "GKs", "GKi")
+        tt(fe(4), gk, th[:], A.is_lt, "GKs " + thn, "F4")
+        ts(T.DEC[:, :, 0:8], T.GKi[:], 15, None, A.bitwise_and, None, "GKi", "DEC0")
+        ts(T.DEC[:, :, 8:16], T.GKi[:], 4, 15, A.arith_shift_right, A.bitwise_and, "GKi", "DEC1")
+        cp(fe(0, 2), T.DEC[:, :, 0:16], "DEC0 DEC1", "F0 F1")
+        act(T.FE[:, 0, 40:48], T.FE[:, 0, 32:40], F.Copy, "F4 f2", "F5+", scale=col(PP))
+        act(T.FE[:, 1, 40:48], T.FE[:, 1, 32:40], F.Copy, "F4 f13", "F5+", scale=col(PH))
+        act(fe(2, 2), fe(0, 2), F.Square, "F0 F1", "F2 F3", bias=-8.0)
+        mm(T.bE[0:K1R, 0:128], T.FE[:, 0, :], T.I1[:], True, True, ALLF, "bE")
+        mm(T.bB[0:K1R, 0:128], T.FE[:, 1, :], T.I1[:], True, True, ALLF, "bB")
+        act(T.FT[0:K1R, 0:128], T.bE[0:K1R, 0:128], F.Copy, "bE", "FTa")
+        for h in range(2):
+            scan(T.VKs[:, h, :], T.D0V[:], VB[h][:, 0:128], A.add, A.max, "D0V " + VN[h], "VKs+")
+        vk = T.VKs[:, :, 15:128:16]
+        cp(T.FT[0:K1R, 128:256], T.bB[0:K1R, 0:128], "bB", "FTb")
+        if t == 0:
+            tt(T.CP[0:K1R, :], T.s0[0:K1R, :], T.s1[0:K1R, :], A.add, "s0 s1", "CP")
+            tt(T.CX[0:K1R, :], T.s2[0:K1R, :], T.s3[0:K1R, :], A.add, "s2 s3", "CX")
+        tt(fe2(2), T.GKi[:], th2[:], A.is_lt, "GKi " + thn2, "E2")
+        ts(fe2(3), vk, -2.0 ** 23, None, A.is_lt, None, "VKs", "E3")
+        ts(T.VKi[:], vk, 2.0 ** 23 - 1024, None, A.add, None, "VKs", "VKi")
+        ts(T.DEC[:, :, 16:24], T.GKi[:], 8, 15, A.arith_shift_right, A.bitwise_and, "GKi", "DEC2")
+        ts(T.tki[:], T.VKi[:], 255, None, A.bitwise_and, None, "VKi", "tki")
+        cp(fe2(0, 2), T.DEC[:, :, 8:24], "DEC1 DEC2", "E0 E1")
+        cp(fe2(4), T.tki[:], "tki", "E4")
+        mm(T.bA[:, 0:256], T.CP[0:K1R, :], FT, True, True, "CP FTa FTb", "bA")
+        colA = [(T.bG[:, 256:384], "bG"), (T.bD[:, 0:128], "bD")]
+        for h, c in HALVES:
+            mm(colA[h][0], T.CC[0:K1R, :], T.FT[0:K1R, c], True, False, "CC FT" + "ab"[h], colA[h][1])
+        for h in range(2):
+            mm(T.bC[0:K2R, 128 * h:128 * h + 128], T.FE2[:, h, :], T.I1[:], True, True, ALLE, "bC")
+        if t < 3:
+            for h in range(2):
+                mm(T.bC[:, 256 + 8 * h:264 + 8 * h], T.onesb[:, 0:128], T.FE2[:, h, 16:24], True, True, "onesb E2", "bC")
+        act(FT2, T.bC[0:K2R, 0:256], F.Copy, "bC", "FT2")
+        for h, c in HALVES:
+            tt(T.Z[:, c], T.bA[:, c], T.ci[:, c], A.min, "bA ci%d" % h, "Z%d" % h)
+            mm(colA[h][0], T.BLK[:], T.Z[:, c], False, True, "BLK Z%d" % h, colA[h][1])
+        mm(T.bF[:, 0:256], T.CT[0:K2R, 128 * t:128 * t + 128], FT2, False, True, "CT%d FT2" % t, "bF")
+        mm(T.bE[:, 256:512], T.CX[0:K1R, :], FT, True, True, "CX FTa FTb", "bE")
+        for h, c in HALVES:
+            ts(T.A1[:, c], colA[h][0], col(SK), col(BK), A.mult, A.add, colA[h][1] + " f5 f6", "A1%d" % h)
+        mm(T.bG[:, 0:256], T.CC[0:K1R, :], FT, True, False, "CC FTa FTb", "bG")
+        mm(T.bG[:, 0:256], T.BLK[:], T.Z[:], False, False, "BLK Z0 Z1", "bG")
+        tt(T["Tn%d" % t][:], T.bF[:, 0:256], T.Tt[:], A.min, "bF Tt", "Tn%d" % t)
+        if t < 3:
+            act(T.junk[:], T.bC[:, 256:272], F.Copy, "bC", "junk msum", accum_out=T.msum[:, 0:1])
+        act(T.Xs[:], T.bE[:, 256:512], F.Copy, "bE", "Xs")
+        dst = T.cores[(rank + 1) % N] if t < 3 else T.cores[(rank - 3) % N]
+        es = topo.engines(core, dst)[::2]
+        need("g", deps_of("g", ["Tn%d" % t], []))
+        rid, pid, _s = topo.addr(dst)
+        g.remote_dma(T["T%d" % (t + 1)][:], T["Tn%d" % t][:], T.sem["a%d" % (t + 1)], T.sem.loc, pid, rid, sum(1 << e for e in es))
+        wr["T%d" % (t + 1)] = ("a%d" % (t + 1), len(es))
+        nloc = len(es)
+        if t < 3:
+            rot(t + 1)
+            tn(t + 1)
+            ct(t + 1)
+        for h, c in HALVES:
+            ts(T.A2[:, c], T.A1[:, c], 1, None, A.bitwise_and, None, "A1%d" % h, "A2%d" % h)
+        for h, c in HALVES:
+            tt(T.lhs[:, c], T.A2[:, c], T.bH[:, c], A.subtract, "A2%d bH" % h, "lhs+")
+        tt(T.rhs[:], T.A2[:], T.bH[:, 256:512], A.subtract, "A20 A21 bH", "rhs")
+        ts(T.lhsO[:], T.lhs[:], col(OD), None, A.mult, None, "lhs f3", "lhsO")
+
+        def gram(bn, pos, gr, half):
+            ba = 32 * (gr // 2)
+            l, ln, k = (T.lhs, "lhs", 16) if gr % 2 == 0 else (T.lhsO, "lhsO", 32)
+            n, c0 = (256, 0) if half == 0 else (128, 128)
+            mm(T[bn][:, pos:pos + n], l[ba:ba + k, c0:c0 + 128], T.rhs[ba:ba + k, c0:256], True, True, ln + " rhs", bn)
+
+        for gr in (0, 2, 1, 3, 4, 5, 6, 7):
+            gram("b" + "ABCD"[gr // 2], 256 * (gr % 2), gr, 0)
+        last = {}
+        for bn, pair in (("bE", 0), ("bF", 2), ("bE", 1), ("bF", 3)):
+            if bn in last:
+                need("t", [("t", last[bn])])
+            for k in range(2):
+                gram(bn, 256 * (pair % 2) + 128 * k, 2 * pair + k, 1)
+            last[bn] = cnt["t"]
+        if t == 0:
+            late_tiles()
+        for k, bn, q in ((0, "bA", "v"), (1, "bB", "s"), (2, "bC", "v"), (3, "bD", "s"), (4, "bE", "v"), (5, "bF", "s")):
+            mt = T["mt%d" % k]
+            if k == 5 and t < 3:
+                codes_x(t + 1)
+            if q == "s":
+                act(mt[:], T[bn][:], F.Relu, bn, "mt%d" % k, bias=-3.5)
+            else:
+                ts(mt[:], T[bn][:], -3.5, 0.0, A.add, A.max, bn, "mt%d" % k)
+        for gr in range(8):
+            if gr == 4 and t < 3:
+                codes_start()
+                codes_y(t + 1)
+            mm(T.bG[:, 0:256], T.SEL[:, 112 - 16 * gr:240 - 16 * gr], T["mt%d" % (gr // 2)][:, 256 * (gr % 2):256 * (gr % 2) + 256],
+               False, False, "SEL mt%d" % (gr // 2), "bG")
+        for gr in range(8):
+            mm(T.bG[:, 128:256], T.SEL[:, 112 - 16 * gr:240 - 16 * gr], T["mt%d" % (4 + gr // 4)][:, 128 * (gr % 4):128 * (gr % 4) + 128],
+               False, gr == 7, "SEL mt%d" % (4 + gr // 4), "bG")
+        if t < 3:
+            codes(t + 1)
+            act(T.m16[:, 0:1], T.msum[:, 0:1], F.Identity, "msum", "m16", bias=49152.0 - 127.5)
+            act(T.msum[:, 1:2], T.msum[:, 0:1], F.Identity, "msum", "mb", scale=256.0, bias=256.0 * 49152)
+            act(T.msum[:, 2:3], T.m16[:, 0:1], F.Identity, "m16 mb", "mc", scale=-256.0, bias=T.msum[:, 1:2])
+            act(T.TH[:], T.TH0[:], F.Identity, "TH0 mc", "TH", bias=T.msum[:, 2:3])
+            act(T.TH2[:], T.TH20[:], F.Identity, "TH20 mc", "TH2", bias=T.msum[:, 2:3])
+        for h, c in HALVES:
+            tt(T.dm[:, c], T.bG[:, c], T.TM[:, c], A.min, "bG TM", "dm%d" % h)
+        if t < 3:
+            offsets()
+        for h, c in HALVES:
+            scan(T.D1[:, c], T.segm[:, c], T.dm[:, c], A.mult, A.add, "segm dm%d" % h, "D1%d" % h)
+        for h in range(2):
+            cp(T.l2u[:, 8 * h:8 * h + 8], T.D1[:, 128 * h + 15:128 * h + 128:16], "D1%d" % h, "l2u+")
+        op("v", lambda: V.tensor_tensor(T.vals[:], win.indirect(T.l2u[:]), T.Xs[:], A.min), "l2u Xs " + UALL, "vals")
+        op("v", lambda: V.tensor_copy(win.indirect(T.l2u[:]), T.vals[:]), "l2u vals", UALL)
+
+    for k in range(16):
+        mm(T.bA[:, 0:384], T.I1[:], T.U[:, k:6144:16], k == 0, k == 15, "I1 " + UALL, "bA")
+    for k in range(8):
+        scan(T.ysc[:, 256 * k:256 * k + 256], T.segm[:], T.U[:, 6144 + 256 * k:6400 + 256 * k], A.mult, A.add, "segm " + UALL, "ysc+")
+    cp(T.yc32[:, 384:512], T.ysc[:, 15:2048:16], "ysc", "yc1")
+    ts(T.yt32[:], T.T4[:], 256.0, None, A.min, None, "T4", "yt32")
+    act(T.yc32[:, 0:384], T.bA[:, 0:384], F.Copy, "bA", "yc0")
+    dma("s", T.yt[:], T.yt32[:], "yt32", "yt")
+    dma("y", T.yc[:], T.yc32[:], "yc0 yc1", "yc")
+    fin = [(q, n) for q, n in cnt.items() if n] + [("d%d" % k, 16) for k in range(ndma[0])]
+    need("g", fin)
+    g.wait_ge(T.sem.loc, 4 * nloc)

@@ -1,14 +1,18 @@
-from concourse.mybir import AluOpType as A, AxisListType, ActivationFunctionType as F
+from concourse.mybir import AluOpType as A, ActivationFunctionType as F
 
 NONE = 2.0 ** 19
 W = 8192
-TR = 8192
-VOID = 8448
-UW = 8464
+PAD = 16
+TR = PAD + W
+UW = TR + 32
+TOP = 32768 + W - 1 + PAD
 SQ = 20480.0
-NS = 32
-K1R, K2R = 56, 48
+KR = 64
 RHO = [0, 5, 10, 15]
+RAW = "ssvvvvss"
+TERM = "ssvvsvss"
+BANK = {0: 0, 1: 1, 6: 0, 7: 1}
+YT = 4608
 
 SCRATCH = {}
 
@@ -17,30 +21,32 @@ def _b(name, cols, dtype, where="sbuf"):
     SCRATCH[name] = (where, [128] + (list(cols) if isinstance(cols, (list, tuple)) else [cols]), dtype)
 
 
-for _n, _c in (("U", UW), ("got", 4096), ("Mx", 4096), ("PX", 4096), ("D0C", 512), ("BLKN", 128), ("D0G", 128), ("D0V", 128), ("segm", 256),
+for _n, _c in (("U", UW), ("Mx", 4096), ("gb", 2048), ("D0G", 128), ("D0V", 128), ("segm", 128), ("seg8", 512), ("one8", 512),
                ("T0", 256), ("T1", 256), ("T2", 256), ("T3", 256), ("T4", 256), ("Tn0", 256), ("Tn1", 256), ("Tn2", 256), ("Tn3", 256),
-               ("Tt", 256), ("Nn", 256), ("prb", 256), ("prb2", 128), ("FT", 256), ("FT2", 256), ("rhs", 256), ("lhs", 256),
-               ("lhsE", 256), ("lhsO", 256), ("Xs", 256), ("vals", 256), ("mt0", 512), ("mt1", 512), ("mt2", 512), ("mt3", 512),
-               ("mt4", 512), ("mt5", 512), ("onesb", 256), ("I1", 128), ("I256", 128), ("nI", 128), ("nI16", 128), ("Ind", 8), ("MQ", 256),
-               ("SEL", 240), ("CC", 128), ("CTa", 128), ("CP", 128), ("CX", 128), ("zb", 128), ("m16", 4),
-               ("RT", 512), ("TNb", 128), ("TN", 512), ("CT", 512), ("FE", (2, K1R)), ("FE2", (2, K2R))):
+               ("Tt", 256), ("Nn", 256), ("prb", 256), ("FT", 256), ("Xs", 256), ("old", 256), ("hot", 256),
+               ("onesb", 128), ("I1", 128), ("I256", 128), ("I64k", 128), ("BLKN", 128), ("TNb", 128), ("CTa", 128),
+               ("CQ", 128), ("CX", 128), ("zb", 128), ("m16", 4), ("M1", 208), ("M2", (12, 16)), ("DK", 208), ("DKp", 128), ("MP", 128),
+               ("c15", 208), ("c16", 128), ("E", (2, 192)), ("RT", 512), ("TN", 512), ("CT", 512), ("FE", (2, KR))):
     _b(_n, _c, "bfloat16")
-for _n, _c in (("xx", 256), ("pd", 256), ("GKs", (2, 128)), ("VKs", (2, 128)), ("TH0", (2, 8)),
-               ("TH", (2, 8)), ("TH20", (2, 8)), ("TH2", (2, 8)), ("Z", 256), ("dm", 256), ("D1", 256),
-               ("BLK", 128), ("TM", 256), ("mif", 256), ("mf", 256), ("mgf", 128), ("w8", 8), ("colsf", 40), ("pw", 16), ("pw2", 16),
-               ("half", 16), ("msum", 4), ("junk", 16), ("yt32", 256), ("yc32", 512), ("ysc", 2048), ("mi2", 128), ("q1", 128), ("q2", 128), ("s0", 128), ("s1", 128), ("s2", 128), ("s3", 128)):
+for _n, _c in (("xx", 256), ("pd", 256), ("GKs", (2, 128)), ("VKs", (2, 128)), ("TH0", 8), ("TH", 8), ("TH20", 8), ("TH2", 8),
+               ("Z", (8, 3, 16)), ("S10", 208), ("S11", 208), ("DD0", 192), ("DD1", 192), ("S20", 192), ("S21", 192), ("SP", 128),
+               ("BLK", 128), ("BLKs", 128), ("GM", 128), ("mif", 128), ("mf", 128), ("mgf", 128), ("w8", 8), ("OH", 8), ("OHN", 16),
+               ("colsf", 24), ("msum", 4), ("junk", 16), ("yt32", 256), ("yc32", 512), ("mi2", 128), ("q1", 128), ("q2", 128),
+               ("s2", 128), ("s3", 128), ("ge", 64)):
     _b(_n, _c, "float32")
-for _n, _c in (("tsti", 256), ("z", 256), ("ci", 256), ("GKi", (2, 8)), ("DEC", (2, 24)), ("VKi", (2, 8)), ("tki", (2, 8)),
-               ("A1", 256), ("A2", 256), ("thr", 8), ("thb", 8), ("mi", 128), ("ri", 128), ("pc", 8)):
+for _n, _c in (("tsti", 256), ("z", 256), ("ci", 256), ("GKi", (2, 8)), ("DEC", (2, 32)), ("VKi", (2, 8)), ("XI", 16), ("RP", 16),
+               ("thr", 8), ("thb", 8), ("pc", 8)):
     _b(_n, _c, "int32")
-for _n, _c in (("K1", 4096), ("R", 256), ("If", 128), ("nIf", 128), ("hib", 256)):
+for _n, _c in (("got", 4096), ("PK", 2560), ("PX", 4096), ("K1", 4096), ("prx", 256), ("prm", 256), ("pz", 128), ("BLKv", 128), ("nI", 128),
+               ("Ind", 8), ("R", 256), ("If", 128), ("If16", 128), ("nIf", 128), ("If256", 128), ("hib", 256), ("SM", 512), ("ysc", W - YT)):
     _b(_n, _c, "float16")
-for _n, _c in (("off", 256), ("l2u", 16)):
+for _n, _c in (("off", 256), ("l0", 16), ("l1", 16), ("og", 8)):
     _b(_n, _c, "uint16")
-for _n in "ABCDEFGH":
+for _n in ("S0", "S1", "G", "V", "F", "L", "C1"):
     _b("b" + _n, 512, "float32", "psum")
+_b("bC2", (32, 16), "float32", "psum")
 
-SEMAPHORES = ["cv", "cs", "ct", "cg", "loc"] + ["d%d" % k for k in range(10)] + ["a%d" % k for k in range(1, 5)]
+SEMAPHORES = ["cv", "cs", "ct", "cg", "loc"] + ["d%d" % k for k in range(10)] + ["a%d%d" % (k, h) for k in range(1, 5) for h in range(2)]
 
 
 def rank_program(g, core, T, topo):
@@ -54,6 +60,7 @@ def rank_program(g, core, T, topo):
     clk = {}
     wr, rd, bank = {}, {}, {}
     ndma = [0]
+    nloc = [0]
 
     def sem_of(e):
         return T.sem["c" + e] if e in cnt else T.sem[e]
@@ -148,6 +155,9 @@ def rank_program(g, core, T, topo):
     def act(out, in_, func, r, w, **k):
         op("s", lambda: S.activation(out, in_, func, **k), r, w)
 
+    def lin(out, in_, scale, bias, r, w):
+        act(out, in_, F.Identity, r, w, scale=scale, bias=bias)
+
     def mm(out, l, x, st, sp, r, w):
         op("t", lambda: P.matmul(out, l, x, st, sp), r, w)
 
@@ -157,49 +167,122 @@ def rank_program(g, core, T, topo):
     def sel(out, in_, pat, cmp, fill, base, cm, r, w):
         op("g", lambda: g.affine_select(out, in_, pat, cmp, fill, base, cm), r, w)
 
+    def half(h):
+        return slice(128 * h, 128 * h + 128)
+
     dma("y", T.tsti[:], T.tst[:], "", "tsti")
     dma("s", T.prb[:], T.pr[:], "", "prb")
     dma("y", T.thr[0:1, 0:8], T.th[:], "", "thr")
-    dma("y", T.U[:, 0:4096], T.cov[:, 0:4096], "", "Ua")
-    dma("s", T.U[:, 4096:W], T.cov[:, 4096:W], "", "Ub")
+    dma("s", T.U[:, PAD + 4096:TR], T.cov[:, 4096:W], "", "Ub")
+    dma("y", T.U[:, PAD:PAD + 4096], T.cov[:, 0:4096], "", "Ua")
     UALL = "Ua Ub Uc"
 
-    PI, PG, PP, OD, EV, SK, BK, CL, CR, N14, R14, R15, HB, PH = range(14)
-    KC, RC_ = 16, 20
-    BP = [[-1, 8], [0, 16]]
+    PI, PJ, PG, P8, FF, PP, J0, J1, CTA, CQC, K0, KC = range(12)
     FL = {"allow_small_or_imprecise_dtypes": True}
 
     def col(k):
         return T.colsf[:, k:k + 1]
 
+    def oh(f):
+        return T.OH[:, f:f + 1]
+
     def iota(out, pat, base, cm, w, **k):
         op("g", lambda: g.iota(out, pat, base, cm, **k), "", w)
 
-    iota(T.pc[:, 0:1], [[0, 1]], 0, 1, "pc0")
-    iota(T.ri[:], [[1, 128]], 1, 0, "ri")
+    iota(T.pc[:, 0:2], [[15, 2]], 0, 1, "pc0")
     iota(T.mgf[:], [[1, 8], [0, 16]], 0, 0, "mgf", **FL)
-    iota(T.mif[:], [[0, 16], [1, 16]], 0, 0, "mif", **FL)
-    iota(col(PP), [[0, 1]], 0, 1, "f2", **FL)
-    iota(T.mf[:], [[1, 256]], 0, 0, "mf", **FL)
-    iota(T.q1[:], [[0, 8], [-1, 16]], 7, 0, "q1", **FL)
+    iota(T.mif[:], [[0, 8], [1, 16]], 0, 0, "mif", **FL)
     iota(T.w8[:], [[1, 8]], 0, 0, "w8", **FL)
-    iota(col(PH), [[0, 1]], 128, 1, "f13", **FL)
-    op("g", lambda: g.partition_broadcast(T.thb[:], T.thr[0:1, 0:8], 128), "thr", "thb")
+    iota(T.mf[:], [[1, 128]], 0, 0, "mf", **FL)
+    iota(T.q1[:], [[0, 8], [-1, 16]], 15, 0, "q1", **FL)
+
+    def codes_in(t, h):
+        src, c = "T%d" % t, half(h)
+        mm(T.bL[:, 128:256], T.onesb[0:1, :], T.onesb[0:1, :], True, False, "onesb", "bL")
+        mm(T.bL[:, 128:256], T.RT[:, 128 * t:128 * t + 128], T[src][:, c], False, True, "RT%d %s%d" % (t, src, h), "bL")
+        lin(T.xx[:, c], T[src][:, c], -2.0, -1.0, "%s%d" % (src, h), "xx%d" % h)
+
+    def codes(t, h, k):
+        c = half(h)
+        if k == 0:
+            tt(T.pd[:, c], T.bL[:, 128:256], T.xx[:, c], A.mult, "bL xx%d" % h, "pd%d" % h)
+        if k == 1:
+            ts(T.z[:, c], T.pd[:, c], col(KC + t), -2.0 ** 30, A.add, A.max, "pd%d fk" % h, "z%d" % h)
+        if k == 2:
+            ts(T.ci[:, c], T.z[:, c], 4, (W - 1) | 0x7FFF8000, A.arith_shift_right, A.bitwise_and, "z%d" % h, "ci%d" % h)
+        if k == 3:
+            ts(T.off[:, c], T.ci[:, c], -1.0, float(TOP), A.mult, A.add, "ci%d" % h, "off%d" % h)
+        if k == 4:
+            ts(T.hib[:, c], T.off[:, c], 1.0 / 32, 1280.0 - 0.484375 - PAD / 32, A.mult, A.add, "off%d" % h, "hib%d" % h)
+
+    def empties(t, h):
+        src, c = "T%d" % t, half(h)
+        act(T.Nn[:, c], T[src][:, c], F.Relu, "%s%d" % (src, h), "Nn%d" % h, bias=1.0 - NONE)
+        lin(T.Tt[:, c], T[src][:, c], 1.0, T.OHN[:, RHO[t]:RHO[t] + 1], "%s%d OHN" % (src, h), "Tt%d" % h)
+
+    def prices(h, i):
+        cp(T.PX[:, 2048 * h + i:2048 * h + 2048:16], T.prx[:, half(h)], "prx", "PX%d+" % h)
 
     ms(T.onesb[:], 1.0, "onesb")
+    ms(T.PK[:], 1.0 / 16, "PK")
+    ts(T.pc[:, 2:4], T.pc[:, 0:2], 15, None, A.bitwise_and, None, "pc0", "pc1+")
+    for k, (sh, msk) in enumerate(((4, 7), (0, 7), (3, 15))):
+        ts(T.pc[:, 4 + k:5 + k], T.pc[:, 0:1], sh, msk, A.arith_shift_right, A.bitwise_and, "pc0", "pc1+")
+    cp(col(PP), T.pc[:, 0:1], "pc0", "fp")
+    cp(T.colsf[:, PI:PI + 5], T.pc[:, 2:7], "pc1", "f")
     ms(T.zb[:], 0.0, "zb")
-    ms(T.CTa[:], 0.0, "CTa")
-    ms(T.CC[:], 0.0, "CC")
-    ts(T.pc[:, 1:2], T.pc[:, 0:1], 15, None, A.bitwise_and, None, "pc0", "pc1")
-    ts(T.pc[:, 2:3], T.pc[:, 0:1], 4, None, A.arith_shift_right, None, "pc0", "pc2")
-    ts(T.pc[:, 3:4], T.pc[:, 0:1], 4, 1, A.arith_shift_right, A.bitwise_and, "pc0", "pc3")
-    cp(col(PI), T.pc[:, 1:2], "pc1", "f0")
-    cp(col(PG), T.pc[:, 2:3], "pc2", "f1")
-    cp(col(OD), T.pc[:, 3:4], "pc3", "f3")
-    ts(T.BLK[:], T.mgf[:], col(PG), None, A.is_equal, None, "mgf f1", "BLK")
-    ts(T.mi[:], T.ri[:], 15, None, A.bitwise_and, None, "ri", "mi")
-    ts(T.mi2[:], T.mi[:], col(PI), 2.0, A.is_equal, A.mult, "mi f0", "mi2")
+    for a, b in ((0, 64), (64, 192), (192, 256)):
+        v = RAW[a // 32] == "v"
+        lin(T.prx[:, a:b], T.prb[:, a:b], 1.0, -512.0 if v else 384.0, "prb", "prx+")
+    for a, b in ((0, 64), (64, 192), (192, 256)):
+        v = RAW[a // 32] == "v"
+        lin(T.prm[:, a:b], T.prb[:, a:b], 1.0 if v else 0.0, -640.0 if v else -512.0, "prb", "prm+")
+    ts(T.BLK[:], T.mgf[:], col(PG), None, A.is_equal, None, "mgf f", "BLK")
+    ts(T.mi2[:], T.mif[:], col(PJ), 2.0, A.is_equal, A.mult, "mif f", "mi2")
+    ts(T.pd[:, half(1)], T.tsti[:, half(1)], 256.0, NONE, A.is_ge, A.mult, "tsti", "pd1")
+    ts(col(K0), col(PI), -16.0 * 613, 2.0 ** 20 - 1, A.mult, A.add, "f", "fk0")
     tt(T.RT[:, 0:128], T.mi2[:], T.BLK[:], A.mult, "mi2 BLK", "RT0")
+    tt(T.T0[:, half(1)], T.pd[:, half(1)], T.tsti[:, half(1)], A.max, "pd1 tsti", "T01")
+    ts(T.colsf[:, KC:KC + 4], T.w8[:, 0:4], -16.0 * 77, col(K0), A.mult, A.add, "w8 fk0", "fk")
+    ts(T.pd[:, half(0)], T.tsti[:, half(0)], 256.0, NONE, A.is_ge, A.mult, "tsti", "pd0")
+    ts(T.I1[:], T.mf[:], col(PP), None, A.is_equal, None, "mf fp", "I1")
+    codes_in(0, 1)
+    tt(T.T0[:, half(0)], T.pd[:, half(0)], T.tsti[:, half(0)], A.max, "pd0 tsti", "T00")
+    ms(T.U[:, 0:PAD], -128.0, "Uc+")
+    ms(T.U[:, TR:UW], 0.0, "Uc+")
+    for n, v in (("If", 1.0), ("nI", -1.0), ("I256", 256.0), ("If16", 16.0), ("nIf", -16.0)):
+        act(T[n][:], T.I1[:], F.Copy, "I1", n, scale=v)
+    act(T.BLKN[:], T.BLK[:], F.Copy, "BLK", "BLKN", scale=NONE)
+    for k in range(4):
+        codes(0, 1, k)
+        for i in range(4 * k, 4 * k + 4):
+            prices(1, i)
+    codes_in(0, 0)
+    ms(T.PK[:, 2048 + 15:2560:16], -512.0, "PK")
+    cp(T.PK[:, 15:2048:16], T.prm[:, 64:192], "prm", "PK+")
+    ts(T.segm[:], T.mif[:], 0.0, None, A.is_gt, None, "mif", "segm")
+    codes(0, 1, 4)
+    for k in range(4):
+        codes(0, 0, k)
+        for i in range(4 * k, 4 * k + 4):
+            prices(0, i)
+    ts(T.DKp[:], T.mif[:], col(PI), 8192.0, A.is_equal, A.mult, "mif f", "DKp")
+    codes(0, 0, 4)
+    ts(T.OH[:], T.w8[:], col(FF), None, A.is_equal, None, "w8 f", "OH")
+    ts(T.GM[:], T.mgf[:], col(P8), None, A.is_equal, None, "mgf f", "GM")
+    ts(T.Ind[:], T.w8[:], col(PG), 4096.0, A.is_equal, A.mult, "w8 f", "Ind")
+    ts(T.OHN[:], T.mif[:, 0:16], col(PI), NONE, A.is_equal, A.mult, "mif f", "OHN")
+    ts(T.ge[:], T.mif[:, 0:64], col(PI), -64.0, A.is_ge, A.mult, "mif f", "ge")
+    cp(T.og[:], T.w8[:], "w8", "og")
+    ms(T.c15[0:1, :], (TOP % 8192) / 16384.0, "c15")
+    ms(T.Z[:, :, 2, :], 0.0, "Z0 Z1")
+    ms(T.FE[:, :, 48:56], 1.0, "E6")
+    ms(T.DK[:], 0.0, "DK")
+    ms(T.M2[:], 2.5, "M2")
+
+    op("g", lambda: g.partition_broadcast(T.thb[:], T.thr[0:1, 0:8], 128), "thr", "thb")
+    sel(T.TNb[:], T.BLKN[:], [[1, 128]], A.is_gt, 0.0, 0, -1, "BLKN", "TNb")
+    sel(T.TNb[:], T.TNb[:], [[1, 128]], A.not_equal, -NONE, 0, -1, "TNb", "TNb")
 
     def rot(t):
         s, n = 1 + t, "RT%d" % t
@@ -209,333 +292,297 @@ def rank_program(g, core, T, topo):
         sel(b, b, [[-16, 8], [0, 16]], A.is_ge, 0.0, 0, 1, n, n)
         sel(b, b, [[16, 8], [0, 16]], A.is_ge, 0.0, 15, -1, n, n)
 
-    def codes_start():
-        mm(T.bA[:, 0:256], T.onesb[0:1, 0:128], T.onesb[0:1, 0:256], True, False, "onesb", "bA")
-
-    def codes_y(t):
-        src = "T%d" % t
-        mm(T.bA[:, 0:256], T.RT[:, 128 * t:128 * t + 128], T[src][:], False, True, "RT%d %s" % (t, src), "bA")
-
-    def codes_x(t):
-        src = "T%d" % t
-        act(T.xx[:], T[src][:], F.Identity, src, "xx", scale=2.0, bias=1.0)
-
-    HALVES = [(h, slice(128 * h, 128 * h + 128)) for h in range(2)]
-
-    def codes(t):
-        for h, c in HALVES:
-            tt(T.pd[:, c], T.bA[:, c], T.xx[:, c], A.mult, "bA xx", "pd%d" % h)
-        for h, c in HALVES:
-            ts(T.z[:, c], T.pd[:, c], col(KC + t), 2.0 ** 30, A.add, A.min, "pd%d fk%d" % (h, t), "z%d" % h)
-        for h, c in HALVES:
-            ts(T.ci[:, c], T.z[:, c], 4, 8191 | 0x7FFF8000, A.arith_shift_right, A.bitwise_and, "z%d" % h, "ci%d" % h)
-
-    def offsets():
-        for h, c in HALVES:
-            ts(T.off[:, c], T.ci[:, c], float(VOID), None, A.min, None, "ci%d" % h, "off+")
-
-    codes_start()
-    m128 = T.mf[:, 0:128]
-    ts(T.segm[:], T.mif[:], 0.0, None, A.is_gt, None, "mif", "segm")
-    ts(col(KC), col(PI), 16.0 * 613, None, A.mult, None, "f0", "fk0")
-    ts(T.I1[:], m128, col(PP), None, A.is_equal, None, "mf f2", "I1")
-    ts(T.If[:], m128, col(PP), None, A.is_equal, None, "mf f2", "If")
-    ts(T.nIf[:], m128, col(PP), -1.0, A.is_equal, A.mult, "mf f2", "nIf")
-    act(T.BLKN[:], T.BLK[:], F.Copy, "BLK", "BLKN", scale=NONE)
-    for k in range(2):
-        act(T.D0C[:, 256 * k:256 * k + 256], T.segm[:], F.Identity, "segm", "D0C+", scale=2.0 ** 20 + 1, bias=-2.0 ** 20)
-    act(T.s0[:], T.q1[:], F.Copy, "q1", "s0", scale=16384.0)
-    act(T.q2[:], T.q1[:], F.Square, "q1", "q2", bias=8.0)
-    act(T.s2[:], T.q1[:], F.Copy, "q1", "s2", scale=-512.0)
-    act(T.s1[:], T.q2[:], F.Identity, "q2", "s1", scale=-8192.0, bias=8192.0 * 65)
-    ts(T.pd[:], T.tsti[:], 256.0, NONE, A.is_ge, A.mult, "tsti", "pd0 pd1")
-    tt(T.T0[:], T.pd[:], T.tsti[:], A.max, "pd0 pd1 tsti", "T0")
-    codes_y(0)
-    codes_x(0)
-    act(T.s3[:], T.q2[:], F.Identity, "q2", "s3", scale=256.0, bias=-16384.0)
-    act(T.dm[:], T.mf[:], F.Copy, "mf", "dm", scale=1.0 / 1024)
-    act(T.I256[:], T.I1[:], F.Copy, "I1", "I256", scale=256.0)
-    act(T.nI[:], T.I1[:], F.Copy, "I1", "nI", scale=-4096.0)
-    codes(0)
-    offsets()
-    for i in range(16):
-        if i < 6:
-            act(T.PX[:, i:4096:16], T.prb[:], F.Copy, "prb", "PXs+")
-        else:
-            cp(T.PX[:, i:4096:16], T.prb[:], "prb", "PXv+")
-    act(T.nI16[:], T.I1[:], F.Copy, "I1", "nI16", scale=-16.0)
-    act(T.D0G[:], T.segm[:, 0:128], F.Identity, "segm", "D0G", scale=2.0 ** 25 + 16, bias=-2.0 ** 25)
-    act(T.D0V[:], T.segm[:, 0:128], F.Identity, "segm", "D0V", scale=2.0 ** 27 + 256, bias=-2.0 ** 27)
-    ms(T.U[:, W:VOID], 0.0, "Uc+")
-    ms(T.U[:, VOID:UW], -128.0, "Uc+")
-    cp(T.prb2[:, 0:128 - NS], T.prb[:, 128:256 - NS], "prb", "prb2+")
-    ms(T.prb2[:, 128 - NS:128], 0.0, "prb2+")
-    ts(T.Ind[:], T.w8[:], col(PG), 256.0, A.is_equal, A.mult, "w8 f1", "Ind")
-    for h in range(2):
-        ts(T.TH0[:, h, :], T.thb[:], 256.0, -SQ, A.mult, A.add, "thb", "TH0+")
-    act(T.TH20[:], T.TH0[:], F.Identity, "TH0", "TH20", bias=SQ)
-    ts(col(RC_), col(PI), float(RHO[0]), NONE, A.is_equal, A.mult, "f0", "fr0")
-    ms(T.FE[:, :, 48:56], 1.0, "F6")
-    ms(T.FE2[:, :, 40:48], 1.0, "E5")
-
-    def fills(n, rows, items):
-        for f, v in items:
-            sel(T[n][0:rows, :], T[n][0:rows, :], BP, A.not_equal, v, -8 * f, 1, n, n)
-
     def tn(t):
         sel(T.TN[:, 128 * t:128 * t + 128], T.TNb[:], [[0, 8], [1, 16]], A.not_equal, 0.0, -RHO[t], 0, "TNb", "TN%d" % t)
 
     def ct(t):
         n, a = "CT%d" % t, 128 * t
-        sel(T.CT[0:K2R, a:a + 128], T.CTa[0:K2R, :], [[0, 8], [1, 16]], A.not_equal, 0.0, -RHO[t], 0, "CTa", n)
-        c = T.CT[0:K2R, a + RHO[t]:a + 128:16]
-        for f, v in ((0, -16.0), (1, 1.0), (2, NONE), (5, 240.0)):
+        sel(T.CT[0:KR, a:a + 128], T.CTa[0:KR, :], [[0, 8], [1, 16]], A.not_equal, 0.0, -RHO[t], 0, "CTa", n)
+        c = T.CT[0:KR, a + RHO[t]:a + 128:16]
+        for f, v in ((1, -16.0), (2, 1.0), (4, NONE), (6, 240.0)):
             sel(c, c, [[-1, 8]], A.not_equal, v, -8 * f, 1, n, n)
 
-    sel(T.s0[0:K1R, :], T.s0[0:K1R, :], BP, A.is_equal, 0.0, 0, 1, "s0", "s0")
-    sel(T.s1[0:K1R, :], T.s1[0:K1R, :], BP, A.is_equal, 0.0, -8 * 6, 1, "s1", "s1")
-    sel(T.s2[0:K1R, :], T.s2[0:K1R, :], BP, A.is_equal, 0.0, -8, 1, "s2", "s2")
-    sel(T.s3[0:K1R, :], T.s3[0:K1R, :], BP, A.is_equal, 0.0, -8 * 6, 1, "s3", "s3")
-    fills("s0", K1R, [(2, -8192.0)])
-    fills("s2", K1R, [(3, 256.0)])
-    fills("CTa", K2R, [(4, 1.0)])
-    fills("s0", K1R, [(4, -8192.0)])
-    fills("CTa", K2R, [(2, -NONE)])
-    fills("CC", K1R, [(2, 2.0 ** 17)])
-    fills("CTa", K2R, [(3, NONE)])
-    fills("CC", K1R, [(0, 2.0 ** 17)])
-    fills("CTa", K2R, [(5, 2 * NONE)])
-    fills("CC", K1R, [(4, 2.0 ** 17)])
-    sel(T.TNb[:], T.BLKN[:], [[1, 128]], A.is_gt, 0.0, 0, -1, "BLKN", "TNb")
-    sel(T.TNb[:], T.TNb[:], [[1, 128]], A.not_equal, -NONE, 0, -1, "TNb", "TNb")
+    lin(T.D0G[:], T.segm[:], 2.0 ** 25 + 16, -2.0 ** 25, "segm", "D0G")
+    act(T.BLKv[:], T.BLK[:], F.Copy, "BLK", "BLKv", scale=4096.0)
+    act(T.I64k[:], T.I1[:], F.Copy, "I1", "I64k", scale=65536.0)
+    act(T.BLKs[:], T.BLK[:], F.Copy, "BLK", "BLKs", scale=-2.0 ** -14)
+    act(T.If256[:], T.I1[:], F.Copy, "I1", "If256", scale=256.0)
+    lin(T.D0V[:], T.segm[:], 2.0 ** 27 + 256, -2.0 ** 27, "segm", "D0V")
+    act(T.q2[:], T.q1[:], F.Square, "q1", "q2")
+    act(T.s2[:], T.q1[:], F.Copy, "q1", "s2", scale=-2.0)
+    act(T.c16[0:1, :], T.mf[0:1, :], F.Copy, "mf", "c16", scale=16.0)
+    lin(T.pz[:], T.prm[:, 0:128], 1.0, 640.0, "prm", "pz")
+    lin(col(J0), col(PI), 1.0, float(TR), "f", "fj+")
+    lin(col(J1), col(PI), 1.0, float(TR + 16), "f", "fj+")
+    for k in range(4):
+        act(T.DK[:, 48 * k:48 * k + 32], T.DKp[:, 0:32], F.Copy, "DKp", "DK+", scale=1.0 / 128)
+        f, v = ((3, 1.0), (4, -NONE), (5, -NONE / 2), (6, 2.5 * NONE))[k]
+        lin(col(CTA), oh(f), v, col(CTA) if k else 0.0, "OH fa", "fa")
+        if k < 2:
+            lin(col(CQC), oh(6 * k), (-1.0, 15.0)[k], col(CQC) if k else 0.0, "OH fq", "fq")
+            lin(T.M2[:, 2 * k:12:3, :], T.ge[:], 1.0, 2.5, "ge", "M2+")
+    lin(T.M1[:], T.DK[:], -0.5, 34.5, "DK", "M1")
+    act(T.CTa[:], T.GM[:], F.Copy, "GM fa", "CTa", scale=col(CTA))
+    lin(T.s2[:], T.s2[:], oh(1), oh(7), "s2 OH", "s2")
+    act(T.s3[:], T.q2[:], F.Copy, "q2 OH", "s3", scale=oh(6))
+    lin(T.MP[:], T.DKp[:], -0.5, 4096.0, "DKp", "MP")
+    act(T.CQ[:], T.GM[:], F.Copy, "GM fq", "CQ", scale=col(CQC))
+    ts(T.TH0[:], T.thb[:], 256.0, -SQ, A.mult, A.add, "thb", "TH0")
+    ts(T.TH20[:], T.thb[:], 256.0, None, A.mult, None, "thb", "TH20")
+    for h in range(2):
+        ms(T["DD%d" % h][:], 0.0, "DD%d" % h)
+    tt(T.s2[:], T.s2[:], T.s3[:], A.add, "s2 s3", "s2")
+    for k in range(4):
+        ms(T["DD%d" % (k % 2)][:, 16 * (k // 2):192:48], -64.0, "DD%d%s" % (k % 2, "+" if k > 1 else ""))
+    tt(T.CX[:], T.s2[:], T.GM[:], A.mult, "s2 GM", "CX")
+    empties(0, 1)
+    empties(0, 0)
     tn(0)
-    fills("CC", K1R, [(5, 1.0)])
     ct(0)
-    fills("CC", K1R, [(6, 201.0 * 8192)])
+    rot(1)
+    iota(T.one8[:], [[0, 512]], 1, 0, "one8", **FL)
+    sel(T.seg8[:], T.one8[:], [[0, 64], [1, 8]], A.is_gt, 0.0, 0, 0, "one8", "seg8")
+    tn(1)
+    ct(1)
 
-    def late_columns():
-        ms(T.half[:], 0.5, "half")
-        ms(T.pw2[:], 0.0, "pw2")
-        ts(col(R14), col(PI), 14.0, None, A.is_equal, None, "f0", "f10")
-        ts(col(R15), col(PI), 15.0, None, A.is_equal, None, "f0", "f11")
-        ts(col(HB), col(PI), 14.0, 0.5, A.is_lt, A.mult, "f0", "f12")
-        scan(T.pw[:], T.half[:], T.pw2[:], A.mult, A.add, "half pw2", "pw", 2.0)
-        tt(col(CL), col(HB), col(R14), A.subtract, "f12 f10", "f7")
-        tt(col(CR), col(HB), col(R15), A.subtract, "f12 f11", "f8")
-        ts(T.pw2[:], T.mif[:, 0:16], col(PI), None, A.is_equal, None, "mif f0", "pw2")
-        ts(col(N14), col(R14), -1.0, None, A.mult, None, "f10", "f9")
-        tt(T.pw[:], T.pw[:], T.pw2[:], A.mult, "pw pw2", "pw")
-        op("v", lambda: V.tensor_reduce(col(SK), T.pw[:, 0:14], AxisListType.X, A.add), "pw", "f5")
-        ts(T.bH[:, 0:256], T.dm[:], col(R15), col(CL), A.mult, A.add, "dm f11 f7", "bH")
-        ts(T.bH[:, 256:512], T.dm[:], col(N14), col(CR), A.mult, A.add, "dm f9 f8", "bH")
-        ts(col(BK), col(SK), 0.5, -0.5, A.mult, A.add, "f5", "f6")
-
-    def late_tiles():
-        for k in range(1, 4):
-            ts(col(KC + k), col(PI), 16.0 * 613, 16.0 * 77 * k, A.mult, A.add, "f0", "fk%d" % k)
-            ts(col(RC_ + k), col(PI), float(RHO[k]), NONE, A.is_equal, A.mult, "f0", "fr%d" % k)
-        ts(T.MQ[:], T.mif[:], col(PI), None, A.is_equal, None, "mif f0", "MQ")
-        ts(T.TM[:], T.mf[:], float(TR), None, A.add, None, "mf", "TM")
-        ms(T.SEL[:, 0:112], 0.0, "SEL+")
-        ms(T.SEL[:, 128:240], 0.0, "SEL+")
-        ms(T.SEL[:, 112:128], 2.0 ** 24, "SEL+")
-        tt(T.TM[:], T.TM[:], T.MQ[:], A.mult, "TM MQ", "TM")
-
-    late_columns()
-
-    def fe(f, n=1):
-        return T.FE[:, :, 8 * f:8 * (f + n)]
-
-    def fe2(f, n=1):
-        return T.FE2[:, :, 8 * f:8 * (f + n)]
-
-    ALLF = " ".join("F%d" % k for k in range(7)) + " I1"
-    ALLE = " ".join("E%d" % k for k in range(6)) + " I1"
-    GB, VB = [T.bA, T.bB], [T.bC, T.bD]
-    GN, VN = ["bA", "bB"], ["bC", "bD"]
     win = T.U[:, 0:UW]
-    FT, FT2 = T.FT[0:K1R, :], T.FT2[0:K2R, :]
-    X0 = 4096 - 16 * NS
 
-    def gains(h, t):
-        a, b = 2048 * h, 2048 * h + 2048
-        mm(GB[h][:, 0:128], T.prb[:, 0:128] if h == 0 else T.prb2[:], T.nI[:], True, False, ("prb" if h == 0 else "prb2") + " nI", GN[h])
-        for i in range(16):
-            mm(GB[h][:, 0:128], T.Mx[:, a + i:b:16], T.I256[:], False, False, ("Mx0" if h == 0 else "Mx1 Mx2") + " I256", GN[h])
-
-    def votes(h):
-        a, b = 2048 * h, 2048 * h + 2048
-        mm(VB[h][:, 0:128], T.hib[:, 128 * h:128 * h + 128], T.If[:], True, False, "hib If", VN[h])
-        for i in range(16):
-            mm(VB[h][:, i:128:16], T.got[:, a + i:b:16], T.Ind[:], False, i == 15, ("got0" if h == 0 else "got1 got2") + " Ind", VN[h])
-
-    for t in range(4):
-        src = "T%d" % t
-        for k, a, b in ((2, X0, 4096), (0, 0, 2048), (1, 2048, X0)):
-            act(T.got[:, a:b], win.indirect(T.off[:, a // 16:b // 16]), F.Identity, "off " + UALL, "got%d" % k, scale=16.0, bias=-2048.0)
-            if k == 0:
-                mm(T.bG[:], T.nI16[:], T.PX[:, X0:4096], True, False, "nI16 PXs PXv", "bG")
-                mm(T.bG[:], T.I1[:], T.got[:, X0:4096], False, True, "I1 got2", "bG")
-                act(T.Mx[:, X0:4096], T.bG[:], F.Relu, "bG", "Mx2", scale=1.0 / 16, bias=128.0)
-        op("v", lambda: V.tensor_tensor(T.Mx[:, 0:2048], win.indirect(T.off[:, 0:128]), T.PX[:, 0:2048], A.max),
-           "off PXs PXv " + UALL, "Mx0")
-        ts(T.hib[:], T.off[:], 1.0 / 32, 1024.0 - 0.484375, A.mult, A.add, "off", "hib")
-        op("v", lambda: V.tensor_tensor(T.Mx[:, 2048:X0], win.indirect(T.off[:, 128:256 - NS]), T.PX[:, 2048:X0], A.max),
-           "off PXs PXv " + UALL, "Mx1")
-        gains(0, t)
-        votes(0)
-        gains(1, t)
-        votes(1)
-        act(T.Nn[:], T[src][:], F.Relu, src, "Nn", bias=1.0 - NONE)
-        act(T.Tt[:], T[src][:], F.Identity, src + " fr%d" % t, "Tt", bias=col(RC_ + t))
-        def payload(h):
-            c = slice(2048 * h + 15, 2048 * h + 2048, 16)
-            ts(T.R[:, 128 * h:128 * h + 128], T.K1[:, c], SQ - 7.5, SQ - 2288.0, A.add, A.max, "K1%d" % h, "R%d" % h)
-            mm(GB[h][:, 0:128], T.K1[:, c], T.If[:], False, False, "K1%d If" % h, GN[h])
-            mm(GB[h][:, 0:128], T.R[:, 128 * h:128 * h + 128], T.nIf[:], False, True, "R%d nIf" % h, GN[h])
-
-        def best(h):
-            scan(T.GKs[:, h, :], T.D0G[:], GB[h][:, 0:128], A.add, A.max, "D0G " + GN[h], "GKs+")
-
-        for h in (0, 1, 2, 3, 7, 4, 5, 6):
-            a, b = 512 * h, 512 * h + 512
-            scan(T.K1[:, a:b], T.D0C[:], T.got[:, a:b], A.add, A.max, "D0C got%d" % (2 if h == 7 else h // 4), "K1%d+" % (h // 4))
-            if h == 7:
-                payload(0)
-        best(0)
-        payload(1)
-        mm(T.bF[:, 0:256], T.TN[:, 128 * t:128 * t + 128], T.Nn[:], True, False, "TN%d Nn" % t, "bF")
-        best(1)
-        gk = T.GKs[:, :, 15:128:16]
+    def visit(t):
         th, thn = (T.TH0, "TH0") if t == 0 else (T.TH, "TH")
         th2, thn2 = (T.TH20, "TH20") if t == 0 else (T.TH2, "TH2")
-        ts(T.GKi[:], gk, SQ, 240.0, A.add, A.max, "GKs", "GKi")
-        tt(fe(4), gk, th[:], A.is_lt, "GKs " + thn, "F4")
-        ts(T.DEC[:, :, 0:8], T.GKi[:], 15, None, A.bitwise_and, None, "GKi", "DEC0")
-        ts(T.DEC[:, :, 8:16], T.GKi[:], 4, 15, A.arith_shift_right, A.bitwise_and, "GKi", "DEC1")
-        cp(fe(0, 2), T.DEC[:, :, 0:16], "DEC0 DEC1", "F0 F1")
-        act(T.FE[:, 0, 40:48], T.FE[:, 0, 32:40], F.Copy, "F4 f2", "F5+", scale=col(PP))
-        act(T.FE[:, 1, 40:48], T.FE[:, 1, 32:40], F.Copy, "F4 f13", "F5+", scale=col(PH))
-        act(fe(2, 2), fe(0, 2), F.Square, "F0 F1", "F2 F3", bias=-8.0)
-        mm(T.bE[0:K1R, 0:128], T.FE[:, 0, :], T.I1[:], True, True, ALLF, "bE")
-        mm(T.bB[0:K1R, 0:128], T.FE[:, 1, :], T.I1[:], True, True, ALLF, "bB")
-        act(T.FT[0:K1R, 0:128], T.bE[0:K1R, 0:128], F.Copy, "bE", "FTa")
-        for h in range(2):
-            scan(T.VKs[:, h, :], T.D0V[:], VB[h][:, 0:128], A.add, A.max, "D0V " + VN[h], "VKs+")
-        vk = T.VKs[:, :, 15:128:16]
-        cp(T.FT[0:K1R, 128:256], T.bB[0:K1R, 0:128], "bB", "FTb")
-        if t == 0:
-            tt(T.CP[0:K1R, :], T.s0[0:K1R, :], T.s1[0:K1R, :], A.add, "s0 s1", "CP")
-            tt(T.CX[0:K1R, :], T.s2[0:K1R, :], T.s3[0:K1R, :], A.add, "s2 s3", "CX")
-        tt(fe2(2), T.GKi[:], th2[:], A.is_lt, "GKi " + thn2, "E2")
-        ts(fe2(3), vk, -2.0 ** 23, None, A.is_lt, None, "VKs", "E3")
-        ts(T.VKi[:], vk, 2.0 ** 23 - 1024, None, A.add, None, "VKs", "VKi")
-        ts(T.DEC[:, :, 16:24], T.GKi[:], 8, 15, A.arith_shift_right, A.bitwise_and, "GKi", "DEC2")
-        ts(T.tki[:], T.VKi[:], 255, None, A.bitwise_and, None, "VKi", "tki")
-        cp(fe2(0, 2), T.DEC[:, :, 8:24], "DEC1 DEC2", "E0 E1")
-        cp(fe2(4), T.tki[:], "tki", "E4")
-        mm(T.bA[:, 0:256], T.CP[0:K1R, :], FT, True, True, "CP FTa FTb", "bA")
-        colA = [(T.bG[:, 256:384], "bG"), (T.bD[:, 0:128], "bD")]
-        for h, c in HALVES:
-            mm(colA[h][0], T.CC[0:K1R, :], T.FT[0:K1R, c], True, False, "CC FT" + "ab"[h], colA[h][1])
-        for h in range(2):
-            mm(T.bC[0:K2R, 128 * h:128 * h + 128], T.FE2[:, h, :], T.I1[:], True, True, ALLE, "bC")
-        if t < 3:
-            for h in range(2):
-                mm(T.bC[:, 256 + 8 * h:264 + 8 * h], T.onesb[:, 0:128], T.FE2[:, h, 16:24], True, True, "onesb E2", "bC")
-        act(FT2, T.bC[0:K2R, 0:256], F.Copy, "bC", "FT2")
-        for h, c in HALVES:
-            tt(T.Z[:, c], T.bA[:, c], T.ci[:, c], A.min, "bA ci%d" % h, "Z%d" % h)
-            mm(colA[h][0], T.BLK[:], T.Z[:, c], False, True, "BLK Z%d" % h, colA[h][1])
-        mm(T.bF[:, 0:256], T.CT[0:K2R, 128 * t:128 * t + 128], FT2, False, True, "CT%d FT2" % t, "bF")
-        mm(T.bE[:, 256:512], T.CX[0:K1R, :], FT, True, True, "CX FTa FTb", "bE")
-        for h, c in HALVES:
-            ts(T.A1[:, c], colA[h][0], col(SK), col(BK), A.mult, A.add, colA[h][1] + " f5 f6", "A1%d" % h)
-        mm(T.bG[:, 0:256], T.CC[0:K1R, :], FT, True, False, "CC FTa FTb", "bG")
-        mm(T.bG[:, 0:256], T.BLK[:], T.Z[:], False, False, "BLK Z0 Z1", "bG")
-        tt(T["Tn%d" % t][:], T.bF[:, 0:256], T.Tt[:], A.min, "bF Tt", "Tn%d" % t)
-        if t < 3:
-            act(T.junk[:], T.bC[:, 256:272], F.Copy, "bC", "junk msum", accum_out=T.msum[:, 0:1])
-        act(T.Xs[:], T.bE[:, 256:512], F.Copy, "bE", "Xs")
-        dst = T.cores[(rank + 1) % N] if t < 3 else T.cores[(rank - 3) % N]
-        es = topo.engines(core, dst)[::2]
-        need("g", deps_of("g", ["Tn%d" % t], []))
-        rid, pid, _s = topo.addr(dst)
-        g.remote_dma(T["T%d" % (t + 1)][:], T["Tn%d" % t][:], T.sem["a%d" % (t + 1)], T.sem.loc, pid, rid, sum(1 << e for e in es))
-        wr["T%d" % (t + 1)] = ("a%d" % (t + 1), len(es))
-        nloc = len(es)
-        if t < 3:
-            rot(t + 1)
-            tn(t + 1)
-            ct(t + 1)
-        for h, c in HALVES:
-            ts(T.A2[:, c], T.A1[:, c], 1, None, A.bitwise_and, None, "A1%d" % h, "A2%d" % h)
-        for h, c in HALVES:
-            tt(T.lhs[:, c], T.A2[:, c], T.bH[:, c], A.subtract, "A2%d bH" % h, "lhs+")
-        tt(T.rhs[:], T.A2[:], T.bH[:, 256:512], A.subtract, "A20 A21 bH", "rhs")
-        ts(T.lhsO[:], T.lhs[:], col(OD), None, A.mult, None, "lhs f3", "lhsO")
 
-        def gram(bn, pos, gr, half):
-            ba = 32 * (gr // 2)
-            l, ln, k = (T.lhs, "lhs", 16) if gr % 2 == 0 else (T.lhsO, "lhsO", 32)
-            n, c0 = (256, 0) if half == 0 else (128, 128)
-            mm(T[bn][:, pos:pos + n], l[ba:ba + k, c0:c0 + 128], T.rhs[ba:ba + k, c0:256], True, True, ln + " rhs", bn)
+        def piece(p):
+            return slice(512 * p, 512 * p + 512)
 
-        for gr in (0, 2, 1, 3, 4, 5, 6, 7):
-            gram("b" + "ABCD"[gr // 2], 256 * (gr % 2), gr, 0)
-        last = {}
-        for bn, pair in (("bE", 0), ("bF", 2), ("bE", 1), ("bF", 3)):
-            if bn in last:
-                need("t", [("t", last[bn])])
-            for k in range(2):
-                gram(bn, 256 * (pair % 2) + 128 * k, 2 * pair + k, 1)
-            last[bn] = cnt["t"]
-        if t == 0:
-            late_tiles()
-        for k, bn, q in ((0, "bA", "v"), (1, "bB", "s"), (2, "bC", "v"), (3, "bD", "s"), (4, "bE", "v"), (5, "bF", "s")):
-            mt = T["mt%d" % k]
-            if k == 5 and t < 3:
-                codes_x(t + 1)
-            if q == "s":
-                act(mt[:], T[bn][:], F.Relu, bn, "mt%d" % k, bias=-3.5)
+        def raw(p):
+            c, o, r = piece(p), T.off[:, 32 * p:32 * p + 32], "off%d " % (p // 4) + UALL
+            if RAW[p] == "s":
+                act(T.got[:, c], win.indirect(o), F.Identity, r, "got%d" % p, bias=384.0)
             else:
-                ts(mt[:], T[bn][:], -3.5, 0.0, A.add, A.max, bn, "mt%d" % k)
-        for gr in range(8):
-            if gr == 4 and t < 3:
-                codes_start()
-                codes_y(t + 1)
-            mm(T.bG[:, 0:256], T.SEL[:, 112 - 16 * gr:240 - 16 * gr], T["mt%d" % (gr // 2)][:, 256 * (gr % 2):256 * (gr % 2) + 256],
-               False, False, "SEL mt%d" % (gr // 2), "bG")
-        for gr in range(8):
-            mm(T.bG[:, 128:256], T.SEL[:, 112 - 16 * gr:240 - 16 * gr], T["mt%d" % (4 + gr // 4)][:, 128 * (gr % 4):128 * (gr % 4) + 128],
-               False, gr == 7, "SEL mt%d" % (4 + gr // 4), "bG")
-        if t < 3:
-            codes(t + 1)
-            act(T.m16[:, 0:1], T.msum[:, 0:1], F.Identity, "msum", "m16", bias=49152.0 - 127.5)
-            act(T.msum[:, 1:2], T.msum[:, 0:1], F.Identity, "msum", "mb", scale=256.0, bias=256.0 * 49152)
-            act(T.msum[:, 2:3], T.m16[:, 0:1], F.Identity, "m16 mb", "mc", scale=-256.0, bias=T.msum[:, 1:2])
-            act(T.TH[:], T.TH0[:], F.Identity, "TH0 mc", "TH", bias=T.msum[:, 2:3])
-            act(T.TH2[:], T.TH20[:], F.Identity, "TH20 mc", "TH2", bias=T.msum[:, 2:3])
-        for h, c in HALVES:
-            tt(T.dm[:, c], T.bG[:, c], T.TM[:, c], A.min, "bG TM", "dm%d" % h)
-        if t < 3:
-            offsets()
-        for h, c in HALVES:
-            scan(T.D1[:, c], T.segm[:, c], T.dm[:, c], A.mult, A.add, "segm dm%d" % h, "D1%d" % h)
-        for h in range(2):
-            cp(T.l2u[:, 8 * h:8 * h + 8], T.D1[:, 128 * h + 15:128 * h + 128:16], "D1%d" % h, "l2u+")
-        op("v", lambda: V.tensor_tensor(T.vals[:], win.indirect(T.l2u[:]), T.Xs[:], A.min), "l2u Xs " + UALL, "vals")
-        op("v", lambda: V.tensor_copy(win.indirect(T.l2u[:]), T.vals[:]), "l2u vals", UALL)
+                tt(T.got[:, c], win.indirect(o), T.PX[:, c], A.subtract, "PX%d " % (p // 4) + r, "got%d" % p)
 
+        def price(p):
+            bn = "bS%d" % BANK[p]
+            mm(T[bn][:], T.nI[:], T.PX[:, piece(p)], True, False, "nI PX%d" % (p // 4), bn)
+
+        def diff(p):
+            bn = "bS%d" % BANK[p]
+            mm(T[bn][:], T.If[:], T.got[:, piece(p)], False, True, "If got%d" % p, bn)
+
+        def term(p):
+            c, bn = piece(p), "bS%d" % BANK.get(p, 0)
+            if RAW[p] == "s":
+                act(T.Mx[:, c], T[bn][:], F.Relu, bn, "Mx%d" % p)
+            elif TERM[p] == "s":
+                act(T.Mx[:, c], T.got[:, c], F.Relu, "got%d" % p, "Mx%d" % p, bias=-512.0)
+            else:
+                ts(T.Mx[:, c], T.got[:, c], -512.0, 0.0, A.add, A.max, "got%d" % p, "Mx%d" % p)
+
+        def names(n, a, b):
+            return " ".join("%s%d" % (n, p) for p in range(a, b))
+
+        def gains(h):
+            n = 4 if h else 3
+            if not h:
+                mm(T.bG[:, 0:128], T.zb[0:1, :], T.zb[0:1, :], True, False, "zb", "bG")
+            for i in range(16):
+                mm(T.bG[0:32 * n, 0:128], T.Mx[:, 2048 * h + i:2048 * h + 512 * n:16], T.I256[:], h == 1 and i == 0, False,
+                   names("Mx", 4 * h, 4 * h + n) + " I256", "bG")
+
+        def last(p):
+            scan(T.SM[:], T.seg8[:], T.Mx[:, piece(p)], A.mult, A.add, "seg8 Mx%d" % p, "SM")
+            for k in range(2):
+                mm(T.bG[96:128, 0:128], T.SM[:, 7 + 8 * k:512:16], T.If256[:], False, False, "SM If256", "bG")
+
+        def votes(h):
+            mm(T.bV[:, 0:128], T.prm[:, half(h)], T.BLKv[:], True, False, "prm BLKv", "bV")
+            for i in range(16):
+                mm(T.bV[:, i:128:16], T.got[:, 2048 * h + i:2048 * h + 2048:16], T.Ind[:], False, False,
+                   names("got", 4 * h, 4 * h + 4) + " Ind", "bV")
+            mm(T.bV[:, 0:128], T.hib[:, half(h)], T.If[:], False, True, "hib%d If" % h, "bV")
+
+        def tuples(p):
+            a = 2048 if RAW[p] == "s" else 512 * (p - 2)
+            scan(T.K1[:, piece(p)], T.got[:, piece(p)], T.PK[:, a:a + 512], A.max, A.add, "PK got%d" % p, "K1%d" % p)
+
+        def payload(h):
+            k1, n = T.K1[:, 2048 * h + 15:2048 * h + 2048:16], names("K1", 4 * h, 4 * h + 4)
+            ts(T.R[:, half(h)], k1, SQ / 16 - 15.0 / 32, SQ / 16 - 143.0, A.add, A.max, n, "R%d" % h)
+            mm(T.bG[:, 0:128], k1, T.If16[:], False, False, n + " If16", "bG")
+            mm(T.bG[:, 0:128], T.R[:, half(h)], T.nIf[:], False, True, "R%d nIf" % h, "bG")
+
+        def level(h):
+            scan(T.GKs[:, h, :], T.D0G[:], T.bG[:, 0:128], A.add, A.max, "D0G bG", "GKs%d" % h)
+
+        def over(h):
+            tt(T.XI[:, 8 * h:8 * h + 8], T.GKs[:, h, 15:128:16], th[:], A.subtract, "GKs%d %s" % (h, thn), "XI%d" % h)
+
+        def claim(h):
+            ts(T.RP[:, 8 * h:8 * h + 8], T.XI[:, 8 * h:8 * h + 8], 15 | 0x40000000, None, A.bitwise_and, None, "XI%d" % h, "RP%d" % h)
+
+        def place(h):
+            tt(T.hot[:, half(h)], T.RP[:, 8 * h:8 * h + 8].indirect(T.og[:]), T.q1[:], A.is_equal, "RP%d og q1" % h, "hot%d" % h)
+            mm(T.bC1[:, 0:208], T.I1[:], T.M1[:], True, False, "I1 M1", "bC1")
+            mm(T.bC1[:, 0:208], T.onesb[0:1, :], T.c15[0:1, :], False, False, "onesb c15", "bC1")
+            mm(T.bC2[:, 0:12, :], T.I1[:], T.M2[:], True, False, "I1 M2", "bC2")
+            mm(T.bC2[:, 0:12, :], T.onesb[0:1, :], T.c15[0:1, 0:192], False, False, "onesb c15", "bC2")
+            mm(T.bF[:, 0:128], T.hot[:, half(h)], T.I64k[:], True, True, "hot%d I64k" % h, "bF")
+
+        def column(h):
+            b = slice(4 * h, 4 * h + 4)
+            tt(T.Z[:, b, 0:2, :], T.bF[:, 0:128], T.ci[:, half(h)], A.min, "bF ci%d" % h, "Z%d" % h)
+            mm(T.bC1[:, 0:192], T.BLKs[:], T.Z[:, b, :, :], False, True, "BLKs Z%d" % h, "bC1")
+            for s, u in ((0, 0), (1, 0), (2, 1)):
+                mm(T.bC2[:, s:12:3, :], T.BLKs[:], T.Z[:, b, u, :], False, s == 2, "BLKs Z%d" % h, "bC2")
+
+        def own(h):
+            scan(T["S1%d" % h][:], T.DK[:], T.bC1[:, 0:208], A.add, A.min, "DK bC1", "S1%d" % h, 64.0)
+
+        def equal(h):
+            s1, dd = T["S1%d" % h], T["DD%d" % h]
+            for u in range(2):
+                act(dd[:, 15 + 32 * u:192:48], s1[:, 15 + 16 * u:192:48], F.Copy, "S1%d" % h, "DD%d+" % h)
+            tt(T.E[:, h, :], s1[:, 16:208], T.bC2[:, 0:12, :], A.is_equal, "S1%d bC2" % h, "E%d" % h)
+
+        def before(h):
+            for u in range(2):
+                ts(T.l0[:, 8 * h + u:8 * h + 8:2], T["S1%d" % h][:, 15 + 16 * u:192:48], 16384.0, float(TR), A.mult, A.min, "S1%d" % h, "l0%d+" % h)
+            act(T.old[:, half(h)], win.indirect(T.l0[:, 8 * h:8 * h + 8]), F.Copy, "l0%d " % h + UALL, "old%d" % h)
+
+        def where(h):
+            mm(T.bF[:, 256:384], T.I1[:], T.MP[:], True, False, "I1 MP", "bF")
+            mm(T.bF[:, 256:384], T.onesb[0:1, :], T.c16[0:1, :], False, False, "onesb c16", "bF")
+            mm(T.bF[:, 256:384], T.CQ[0:KR, :], T.FT[0:KR, half(h)], False, True, "CQ FT%d" % h, "bF")
+            scan(T.SP[:], T.DKp[:], T.bF[:, 256:384], A.add, A.min, "DKp bF", "SP", 8192.0)
+
+        def wlist(h):
+            cp(T.l0[:, 0:8], T.SP[:, 15:128:16], "SP", "l00")
+
+        def kept(h):
+            tt(T.old[:, half(h)], T.gb[:].indirect(T.l0[:, 0:8]), T.pz[:], A.add, "l00 pz " + names("gb", 0, 4), "old0")
+
+        def keep(p):
+            lin(T.gb[:, piece(p)], T.got[:, piece(p)], 1.0, -512.0, "got%d" % p, "gb%d" % p)
+
+        def lower(h):
+            scan(T["S2%d" % h][:], T["DD%d" % h][:], T.E[:, h, :], A.add, A.max, "DD%d E%d" % (h, h), "S2%d" % h)
+
+        def lists(h):
+            for u in range(2):
+                ts(T.l1[:, 8 * h + u:8 * h + 8:2], T["S2%d" % h][:, 15 + 32 * u:192:48], 16384.0, col(J0 + u), A.mult, A.min,
+                   "S2%d fj" % h, "l1%d+" % h)
+
+        def credit(p):
+            c, h = slice(32 * p, 32 * p + 32), p // 4
+            tt(win.indirect(T.l1[:, 2 * p:2 * p + 2]), T.old[:, c], T.Xs[:, c], A.mult, "l1%d old%d Xs%d" % (h, h, h), UALL)
+
+        def vote(h):
+            scan(T.VKs[:, h, :], T.D0V[:], T.bV[:, 0:128], A.add, A.max, "D0V bV", "VKs%d" % h)
+
+        def keys(h):
+            vk = T.VKs[:, h, 15:128:16]
+            ts(T.GKi[:, h, :], T.GKs[:, h, 15:128:16], SQ, 240.0, A.add, A.max, "GKs%d" % h, "GKi%d" % h)
+            ts(T.VKi[:, h, :], vk, 2.0 ** 23 - 1280, None, A.add, None, "VKs%d" % h, "VKi%d" % h)
+            act(T.FE[:, h, 40:48], vk, F.Sign, "VKs%d" % h, "Es%d" % h, bias=2.0 ** 23)
+
+        def fields(h):
+            for k in range(h, 3):
+                ts(T.DEC[:, h, 8 * k:8 * k + 8], T.GKi[:, h, :], 4 * k, 15, A.arith_shift_right, A.bitwise_and, "GKi%d" % h, "DEC%d+" % h)
+            ts(T.DEC[:, h, 24:32], T.VKi[:, h, :], 255, None, A.bitwise_and, None, "VKi%d" % h, "DEC%d+" % h)
+            tt(T.FE[:, h, 32:40], T.GKi[:, h, :], th2[:], A.is_lt, "GKi%d %s" % (h, thn2), "Ea%d+" % h)
+
+        def features(h):
+            c = half(h)
+            cp(T.FE[:, h, 8 * h:32], T.DEC[:, h, 8 * h:32], "DEC%d" % h, "Ea%d+" % h)
+            tt(T.FE[:, h, 56:64], T.DEC[:, h, 8:16], T.DEC[:, h, 8:16], A.mult, "DEC%d" % h, "Ea%d+" % h)
+            mm(T.bV[0:KR, 128:256], T.FE[:, h, :], T.I1[:], True, True, "Ea%d Es%d E6 I1" % (h, h), "bV")
+            act(T.FT[0:KR, c], T.bV[0:KR, 128:256], F.Copy, "bV", "FT%d" % h)
+
+        def mask(h):
+            mm(T.bF[:, 128:256], T.CX[0:KR, :], T.FT[0:KR, half(h)], True, True, "CX FT%d" % h, "bF")
+            act(T.Xs[:, half(h)], T.bF[:, 128:256], F.Sign, "bF", "Xs%d" % h)
+
+        def change(h):
+            c = half(h)
+            mm(T.bL[:, 0:128], T.TN[:, 128 * t:128 * t + 128], T.Nn[:, c], True, False, "TN%d Nn%d" % (t, h), "bL")
+            mm(T.bL[:, 0:128], T.CT[0:KR, 128 * t:128 * t + 128], T.FT[0:KR, c], False, True, "CT%d FT%d" % (t, h), "bL")
+
+        def walk(h):
+            c, n = half(h), "Tn%d%d" % (t, h)
+            tt(T["Tn%d" % t][:, c], T.bL[:, 0:128], T.Tt[:, c], A.min, "bL Tt%d" % h, n)
+            dst = T.cores[(rank + 1) % N] if t < 3 else T.cores[(rank - 3) % N]
+            es = topo.engines(core, dst)[::2]
+            need("g", deps_of("g", [n], []))
+            rid, pid, _s = topo.addr(dst)
+            a = "a%d%d" % (t + 1, h)
+            g.remote_dma(T["T%d" % (t + 1)][:, c], T["Tn%d" % t][:, c], T.sem[a], T.sem.loc, pid, rid, sum(1 << e for e in es))
+            wr["T%d%d" % (t + 1, h)] = (a, len(es))
+            nloc[0] += len(es)
+            if h == 0 and t < 2:
+                rot(t + 2)
+                tn(t + 2)
+                ct(t + 2)
+
+        def count(k):
+            if t == 3:
+                return
+            for h in range(2):
+                mm(T.bV[:, 256 + 8 * h:264 + 8 * h], T.onesb[:], T.FE[:, h, 32:40], True, True, "onesb Ea%d" % h, "bV")
+            act(T.junk[:], T.bV[:, 256:272], F.Copy, "bV", "junk msum", accum_out=T.msum[:, 0:1])
+            lin(T.m16[:, 0:1], T.msum[:, 0:1], 1.0, 49152.0 - 127.5, "msum", "m16")
+            lin(T.msum[:, 1:2], T.msum[:, 0:1], 256.0, 256.0 * 49152, "msum", "mb")
+            lin(T.msum[:, 2:3], T.m16[:, 0:1], -256.0, T.msum[:, 1:2], "m16 mb", "mc")
+            lin(T.TH[:], T.TH0[:], 1.0, T.msum[:, 2:3], "TH0 mc", "TH")
+            lin(T.TH2[:], T.TH20[:], 1.0, T.msum[:, 2:3], "TH20 mc", "TH2")
+
+        def mine(k):
+            if t and k < 5:
+                codes(t, 0, k)
+            if t and k == 5:
+                codes_in(t, 0)
+            if t and k == 6:
+                empties(t, 0)
+
+        def next_(k):
+            if t < 3 and k < 5:
+                codes(t + 1, 1, k)
+            if t < 3 and k == 5:
+                codes_in(t + 1, 1)
+            if t < 3 and k == 6:
+                empties(t + 1, 1)
+
+        steps = {"raw": raw, "price": price, "diff": diff, "term": term, "gains": gains, "last": last, "votes": votes, "tuples": tuples,
+                 "payload": payload, "level": level, "over": over, "claim": claim, "place": place, "column": column, "own": own,
+                 "equal": equal, "before": before, "where": where, "wlist": wlist, "kept": kept, "keep": keep, "lower": lower, "lists": lists,
+                 "credit": credit, "vote": vote, "keys": keys, "fields": fields, "features": features, "mask": mask, "change": change,
+                 "walk": walk, "count": count, "mine": mine, "next": next_}
+        for word in ORDER.split():
+            steps[word[:-1]](int(word[-1]))
+
+    ms(T.FE[:, 1, 0:8], 0.0, "Ea1")
+    for t in range(4):
+        visit(t)
+
+    nb = YT // 16
     for k in range(16):
-        mm(T.bA[:, 0:384], T.I1[:], T.U[:, k:6144:16], k == 0, k == 15, "I1 " + UALL, "bA")
-    for k in range(8):
-        scan(T.ysc[:, 256 * k:256 * k + 256], T.segm[:], T.U[:, 6144 + 256 * k:6400 + 256 * k], A.mult, A.add, "segm " + UALL, "ysc+")
-    cp(T.yc32[:, 384:512], T.ysc[:, 15:2048:16], "ysc", "yc1")
-    ts(T.yt32[:], T.T4[:], 256.0, None, A.min, None, "T4", "yt32")
-    act(T.yc32[:, 0:384], T.bA[:, 0:384], F.Copy, "bA", "yc0")
-    dma("s", T.yt[:], T.yt32[:], "yt32", "yt")
+        mm(T.bS0[:, 0:nb], T.I1[:], T.U[:, PAD + k:PAD + YT:16], k == 0, k == 15, "I1 " + UALL, "bS0")
+    for a in range(YT, W, 512):
+        scan(T.ysc[:, a - YT:a - YT + 512], T.seg8[:], T.U[:, PAD + a:PAD + a + 512], A.mult, A.add, "seg8 " + UALL, "ysc+")
+    tt(T.yc32[:, nb:512], T.ysc[:, 7:W - YT:16], T.ysc[:, 15:W - YT:16], A.add, "ysc", "yc1")
+    act(T.yc32[:, 0:nb], T.bS0[:, 0:nb], F.Copy, "bS0", "yc0")
+    ts(T.yt32[:], T.T4[:], 256.0, None, A.min, None, "T40 T41", "yt32")
     dma("y", T.yc[:], T.yc32[:], "yc0 yc1", "yc")
+    dma("s", T.yt[:], T.yt32[:], "yt32", "yt")
     fin = [(q, n) for q, n in cnt.items() if n] + [("d%d" % k, 16) for k in range(ndma[0])]
     need("g", fin)
-    g.wait_ge(T.sem.loc, 4 * nloc)
+    g.wait_ge(T.sem.loc, nloc[0])
+
+
+ORDER = """
+raw6 mine5 price7 price6 raw4 raw7 diff6 raw5 mine0 term6 tuples6 mine1 diff7 term5 price0 mine2 tuples5 term4 mine3 term7
+votes1 raw0 gains1 tuples4 tuples7 raw2 payload1 mine4 term2 diff0 tuples2 level1 price1 raw1 term0 diff1 vote1 term1 over1 tuples0
+claim1 tuples1 keep1 place1 raw3 gains0 keep3 column1 keys1 term3 tuples3 last3 payload0 fields1 keep0 own1 votes0 features1 level0
+equal1 mask1 over0 mine6 change1 before1 claim0 keep2 vote0 place0 walk1 lower1 keys0 column0 fields0 lists1 features0 credit7 own0
+credit6 equal0 credit5 lower0 where0 change0 walk0 credit4 wlist0 next5 lists0 mask0 kept0 next0 credit3 next1 credit2 next6 next2
+credit1 next3 credit0 next4 count0
+"""

@@ -9,10 +9,9 @@ TOP = 32768 + W - 1 + PAD
 SQ = 20480.0
 KR = 64
 RHO = [0, 5, 10, 15]
-RAW = "ssvvvvss"
-TERM = "ssvvsvss"
-BANK = {0: 0, 1: 1, 6: 0, 7: 1}
-YT = 4608
+PIECES = [(0, 32, "s", "s"), (32, 32, "s", "s"), (64, 32, "v", "s"), (96, 16, "v", "v"), (112, 16, "v", "v"),
+          (128, 32, "v", "s"), (160, 32, "v", "v"), (192, 32, "s", "s"), (224, 32, "s", "s")]
+YT = 4224
 
 SCRATCH = {}
 
@@ -22,22 +21,22 @@ def _b(name, cols, dtype, where="sbuf"):
 
 
 for _n, _c in (("U", UW), ("Mx", 4096), ("gb", 2048), ("D0G", 128), ("D0V", 128), ("segm", 128), ("seg8", 512), ("one8", 512),
-               ("T0", 256), ("T1", 256), ("T2", 256), ("T3", 256), ("T4", 256), ("Tn0", 256), ("Tn1", 256), ("Tn2", 256), ("Tn3", 256),
+               ("T0", 256), ("T1", 256), ("T2", 256), ("T3", 256), ("Tn0", 256), ("Tn1", 256), ("Tn2", 256), ("nI4k", 128), ("prq", 128),
                ("Tt", 256), ("Nn", 256), ("prb", 256), ("FT", 256), ("Xs", 256), ("old", 256), ("hot", 256),
                ("onesb", 128), ("I1", 128), ("I256", 128), ("I64k", 128), ("BLKN", 128), ("TNb", 128), ("CTa", 128),
                ("CQ", 128), ("CX", 128), ("zb", 128), ("m16", 4), ("M1", 208), ("M2", (12, 16)), ("DK", 208), ("DKp", 128), ("MP", 128),
                ("c15", 208), ("c16", 128), ("E", (2, 192)), ("RT", 512), ("TN", 512), ("CT", 512), ("FE", (2, KR))):
     _b(_n, _c, "bfloat16")
-for _n, _c in (("xx", 256), ("pd", 256), ("GKs", (2, 128)), ("VKs", (2, 128)), ("TH0", 8), ("TH", 8), ("TH20", 8), ("TH2", 8),
+for _n, _c in (("xx", 256), ("pd", 256), ("KS", (2, 256)), ("TH0", 8), ("TH", 8), ("TH20", 8), ("TH2", 8),
                ("Z", (8, 3, 16)), ("S10", 208), ("S11", 208), ("DD0", 192), ("DD1", 192), ("S20", 192), ("S21", 192), ("SP", 128),
                ("BLK", 128), ("BLKs", 128), ("GM", 128), ("mif", 128), ("mf", 128), ("mgf", 128), ("w8", 8), ("OH", 8), ("OHN", 16),
-               ("colsf", 24), ("msum", 4), ("junk", 16), ("yt32", 256), ("yc32", 512), ("mi2", 128), ("q1", 128), ("q2", 128),
+               ("colsf", 24), ("msum", 4), ("junk", 16), ("T4", 256), ("Tn3", 256), ("rho3", 4), ("yc32", 512), ("mi2", 128), ("q1", 128), ("q2", 128),
                ("s2", 128), ("s3", 128), ("ge", 64)):
     _b(_n, _c, "float32")
-for _n, _c in (("tsti", 256), ("z", 256), ("ci", 256), ("GKi", (2, 8)), ("DEC", (2, 32)), ("VKi", (2, 8)), ("XI", 16), ("RP", 16),
+for _n, _c in (("tsti", 256), ("z", 256), ("ci", 256), ("KI", (2, 16)), ("DEC", 64), ("XI", 16),
                ("thr", 8), ("thb", 8), ("pc", 8)):
     _b(_n, _c, "int32")
-for _n, _c in (("got", 4096), ("PK", 2560), ("PX", 4096), ("K1", 4096), ("prx", 256), ("prm", 256), ("pz", 128), ("BLKv", 128), ("nI", 128),
+for _n, _c in (("got", 4096), ("PK", 3072), ("PX", 4096), ("K1", 4096), ("prx", 256), ("prm", 256), ("pz", 256), ("pb", 128), ("BLKv", 128), ("nI", 128),
                ("Ind", 8), ("R", 256), ("If", 128), ("If16", 128), ("nIf", 128), ("If256", 128), ("hib", 256), ("SM", 512), ("ysc", W - YT)):
     _b(_n, _c, "float16")
 for _n, _c in (("off", 256), ("l0", 16), ("l1", 16), ("og", 8)):
@@ -177,7 +176,10 @@ def rank_program(g, core, T, topo):
     dma("y", T.U[:, PAD:PAD + 4096], T.cov[:, 0:4096], "", "Ua")
     UALL = "Ua Ub Uc"
 
-    PI, PJ, PG, P8, FF, PP, J0, J1, CTA, CQC, K0, KC = range(12)
+    PI, PJ, PG, P8, FF, PP, J0, J1, CTA, CQC, M2C, K0, KC = range(13)
+    SUB = [p for p in range(len(PIECES)) if PIECES[p][2:] == ("s", "s")]
+    VA = min(a for a, n, who, how in PIECES if who == "v")
+    VB = max(a + n for a, n, who, how in PIECES if who == "v")
     FL = {"allow_small_or_imprecise_dtypes": True}
 
     def col(k):
@@ -218,25 +220,33 @@ def rank_program(g, core, T, topo):
     def empties(t, h):
         src, c = "T%d" % t, half(h)
         act(T.Nn[:, c], T[src][:, c], F.Relu, "%s%d" % (src, h), "Nn%d" % h, bias=1.0 - NONE)
-        lin(T.Tt[:, c], T[src][:, c], 1.0, T.OHN[:, RHO[t]:RHO[t] + 1], "%s%d OHN" % (src, h), "Tt%d" % h)
+        if t < 3:
+            lin(T.Tt[:, c], T[src][:, c], 1.0, T.OHN[:, RHO[t]:RHO[t] + 1], "%s%d OHN" % (src, h), "Tt%d" % h)
+        else:
+            act(T.Tt[:, c], T[src][:, c], F.Relu, "%s%d rho3" % (src, h), "Tt%d" % h, scale=-1.0, bias=T.rho3[:, 0:1])
+            lin(T.Tt[:, c], T.Tt[:, c], -1.0, 256.0, "Tt%d" % h, "Tt%d" % h)
 
     def prices(h, i):
         cp(T.PX[:, 2048 * h + i:2048 * h + 2048:16], T.prx[:, half(h)], "prx", "PX%d+" % h)
 
     ms(T.onesb[:], 1.0, "onesb")
-    ms(T.PK[:], 1.0 / 16, "PK")
+    ms(T.PK[:, 0:512 + 16 * (VB - VA)], 1.0 / 16, "PK")
     ts(T.pc[:, 2:4], T.pc[:, 0:2], 15, None, A.bitwise_and, None, "pc0", "pc1+")
     for k, (sh, msk) in enumerate(((4, 7), (0, 7), (3, 15))):
         ts(T.pc[:, 4 + k:5 + k], T.pc[:, 0:1], sh, msk, A.arith_shift_right, A.bitwise_and, "pc0", "pc1+")
     cp(col(PP), T.pc[:, 0:1], "pc0", "fp")
     cp(T.colsf[:, PI:PI + 5], T.pc[:, 2:7], "pc1", "f")
-    ms(T.zb[:], 0.0, "zb")
-    for a, b in ((0, 64), (64, 192), (192, 256)):
-        v = RAW[a // 32] == "v"
-        lin(T.prx[:, a:b], T.prb[:, a:b], 1.0, -512.0 if v else 384.0, "prb", "prx+")
-    for a, b in ((0, 64), (64, 192), (192, 256)):
-        v = RAW[a // 32] == "v"
-        lin(T.prm[:, a:b], T.prb[:, a:b], 1.0 if v else 0.0, -640.0 if v else -512.0, "prb", "prm+")
+    runs = []
+    for a, n, who, how in PIECES:
+        kind = "m" if how == "m" else who
+        if runs and runs[-1][2] == kind:
+            runs[-1][1] = a + n
+        else:
+            runs.append([a, a + n, kind])
+    for a, b, kind in runs[::-1]:
+        lin(T.prx[:, a:b], T.prb[:, a:b], 1.0, {"v": -512.0, "s": 384.0, "m": 0.0}[kind], "prb", "prx+")
+    for a, b, kind in runs:
+        lin(T.prm[:, a:b], T.prb[:, a:b], 1.0 if kind == "v" else 0.0, -640.0 if kind == "v" else -512.0, "prb", "prm+")
     ts(T.BLK[:], T.mgf[:], col(PG), None, A.is_equal, None, "mgf f", "BLK")
     ts(T.mi2[:], T.mif[:], col(PJ), 2.0, A.is_equal, A.mult, "mif f", "mi2")
     ts(T.pd[:, half(1)], T.tsti[:, half(1)], 256.0, NONE, A.is_ge, A.mult, "tsti", "pd1")
@@ -248,8 +258,10 @@ def rank_program(g, core, T, topo):
     ts(T.I1[:], T.mf[:], col(PP), None, A.is_equal, None, "mf fp", "I1")
     codes_in(0, 1)
     tt(T.T0[:, half(0)], T.pd[:, half(0)], T.tsti[:, half(0)], A.max, "pd0 tsti", "T00")
-    ms(T.U[:, 0:PAD], -128.0, "Uc+")
-    ms(T.U[:, TR:UW], 0.0, "Uc+")
+    ts(T.segm[:], T.mif[:], 0.0, None, A.is_gt, None, "mif", "segm")
+    ts(T.DKp[:], T.mif[:], col(PI), 8192.0, A.is_equal, A.mult, "mif f", "DKp")
+    ts(T.OH[:], T.w8[:], col(FF), None, A.is_equal, None, "w8 f", "OH")
+    ts(T.GM[:], T.mgf[:], col(P8), None, A.is_equal, None, "mgf f", "GM")
     for n, v in (("If", 1.0), ("nI", -1.0), ("I256", 256.0), ("If16", 16.0), ("nIf", -16.0)):
         act(T[n][:], T.I1[:], F.Copy, "I1", n, scale=v)
     act(T.BLKN[:], T.BLK[:], F.Copy, "BLK", "BLKN", scale=NONE)
@@ -257,30 +269,29 @@ def rank_program(g, core, T, topo):
         codes(0, 1, k)
         for i in range(4 * k, 4 * k + 4):
             prices(1, i)
-    codes_in(0, 0)
-    ms(T.PK[:, 2048 + 15:2560:16], -512.0, "PK")
-    cp(T.PK[:, 15:2048:16], T.prm[:, 64:192], "prm", "PK+")
-    ts(T.segm[:], T.mif[:], 0.0, None, A.is_gt, None, "mif", "segm")
+    ms(T.U[:, 0:PAD], -128.0, "Uc+")
+    ms(T.U[:, TR:UW], 0.0, "Uc+")
+    ms(T.PK[:, 15:512:16], -512.0, "PK")
+    cp(T.PK[:, 512 + 15:512 + 16 * (VB - VA):16], T.prm[:, VA:VB], "prm", "PK+")
     codes(0, 1, 4)
-    for k in range(4):
-        codes(0, 0, k)
-        for i in range(4 * k, 4 * k + 4):
-            prices(0, i)
-    ts(T.DKp[:], T.mif[:], col(PI), 8192.0, A.is_equal, A.mult, "mif f", "DKp")
-    codes(0, 0, 4)
-    ts(T.OH[:], T.w8[:], col(FF), None, A.is_equal, None, "w8 f", "OH")
-    ts(T.GM[:], T.mgf[:], col(P8), None, A.is_equal, None, "mgf f", "GM")
-    ts(T.Ind[:], T.w8[:], col(PG), 4096.0, A.is_equal, A.mult, "w8 f", "Ind")
     ts(T.OHN[:], T.mif[:, 0:16], col(PI), NONE, A.is_equal, A.mult, "mif f", "OHN")
     ts(T.ge[:], T.mif[:, 0:64], col(PI), -64.0, A.is_ge, A.mult, "mif f", "ge")
+    ms(T.M2[:], 2.5, "M2")
+    ts(T.Ind[:], T.w8[:], col(PG), 4096.0, A.is_equal, A.mult, "w8 f", "Ind")
     cp(T.og[:], T.w8[:], "w8", "og")
     ms(T.c15[0:1, :], (TOP % 8192) / 16384.0, "c15")
-    ms(T.Z[:, :, 2, :], 0.0, "Z0 Z1")
-    ms(T.FE[:, :, 48:56], 1.0, "E6")
-    ms(T.DK[:], 0.0, "DK")
-    ms(T.M2[:], 2.5, "M2")
+    for i in range(16):
+        prices(0, i)
 
+    iota(T.DK[:], [[0, 208]], 0, 0, "DK", **FL)
     op("g", lambda: g.partition_broadcast(T.thb[:], T.thr[0:1, 0:8], 128), "thr", "thb")
+    iota(T.Z[:, :, 2, :], [[0, 8], [0, 16]], 0, 0, "Z0 Z1", **FL)
+    iota(T.FE[:, :, 48:56], [[0, 2], [0, 8]], 1, 0, "E6", **FL)
+    for h in range(2):
+        iota(T["DD%d" % h][:], [[0, 192]], 0, 0, "DD%d" % h, **FL)
+    for k in range(4):
+        iota(T["DD%d" % (k % 2)][:, 16 * (k // 2):192:48], [[0, 4]], -64, 0, "DD%d%s" % (k % 2, "+" if k > 1 else ""), **FL)
+    iota(T.zb[:], [[0, 128]], 0, 0, "zb", **FL)
     sel(T.TNb[:], T.BLKN[:], [[1, 128]], A.is_gt, 0.0, 0, -1, "BLKN", "TNb")
     sel(T.TNb[:], T.TNb[:], [[1, 128]], A.not_equal, -NONE, 0, -1, "TNb", "TNb")
 
@@ -308,10 +319,16 @@ def rank_program(g, core, T, topo):
     act(T.BLKs[:], T.BLK[:], F.Copy, "BLK", "BLKs", scale=-2.0 ** -14)
     act(T.If256[:], T.I1[:], F.Copy, "I1", "If256", scale=256.0)
     lin(T.D0V[:], T.segm[:], 2.0 ** 27 + 256, -2.0 ** 27, "segm", "D0V")
-    act(T.q2[:], T.q1[:], F.Square, "q1", "q2")
-    act(T.s2[:], T.q1[:], F.Copy, "q1", "s2", scale=-2.0)
+    act(T.nI4k[:], T.I1[:], F.Copy, "I1", "nI4k", scale=-4096.0)
+    for a, b, kind in runs:
+        if a < 128:
+            act(T.prq[:, a:min(b, 128)], T.prb[:, a:min(b, 128)], F.Copy, "prb", "prq+", scale=1.0 if kind == "m" else 0.0)
+    lin(col(M2C), oh(1), -2.0, 0.0, "OH", "fm")
+    act(T.s2[32:64, :], T.q1[32:64, :], F.Square, "q1 OH", "s2+", scale=T.OH[32:64, 6:7], bias=T.OH[32:64, 7:8])
+    act(T.s2[0:32, :], T.q1[0:32, :], F.Copy, "q1 fm", "s2+", scale=T.colsf[0:32, M2C:M2C + 1])
     act(T.c16[0:1, :], T.mf[0:1, :], F.Copy, "mf", "c16", scale=16.0)
-    lin(T.pz[:], T.prm[:, 0:128], 1.0, 640.0, "prm", "pz")
+    lin(T.pz[:], T.prm[:], 1.0, 128.0, "prm", "pz")
+    lin(T.pb[:], T.prm[:, 0:128], 1.0, 640.0, "prm", "pb")
     lin(col(J0), col(PI), 1.0, float(TR), "f", "fj+")
     lin(col(J1), col(PI), 1.0, float(TR + 16), "f", "fj+")
     for k in range(4):
@@ -323,25 +340,18 @@ def rank_program(g, core, T, topo):
             lin(T.M2[:, 2 * k:12:3, :], T.ge[:], 1.0, 2.5, "ge", "M2+")
     lin(T.M1[:], T.DK[:], -0.5, 34.5, "DK", "M1")
     act(T.CTa[:], T.GM[:], F.Copy, "GM fa", "CTa", scale=col(CTA))
-    lin(T.s2[:], T.s2[:], oh(1), oh(7), "s2 OH", "s2")
-    act(T.s3[:], T.q2[:], F.Copy, "q2 OH", "s3", scale=oh(6))
     lin(T.MP[:], T.DKp[:], -0.5, 4096.0, "DKp", "MP")
     act(T.CQ[:], T.GM[:], F.Copy, "GM fq", "CQ", scale=col(CQC))
+    lin(T.rho3[:, 0:1], T.OHN[:, RHO[3]:RHO[3] + 1], -1.0, 256.0, "OHN", "rho3")
     ts(T.TH0[:], T.thb[:], 256.0, -SQ, A.mult, A.add, "thb", "TH0")
     ts(T.TH20[:], T.thb[:], 256.0, None, A.mult, None, "thb", "TH20")
-    for h in range(2):
-        ms(T["DD%d" % h][:], 0.0, "DD%d" % h)
-    tt(T.s2[:], T.s2[:], T.s3[:], A.add, "s2 s3", "s2")
-    for k in range(4):
-        ms(T["DD%d" % (k % 2)][:, 16 * (k // 2):192:48], -64.0, "DD%d%s" % (k % 2, "+" if k > 1 else ""))
-    tt(T.CX[:], T.s2[:], T.GM[:], A.mult, "s2 GM", "CX")
+    tt(T.CX[0:KR, :], T.s2[0:KR, :], T.GM[0:KR, :], A.mult, "s2 GM", "CX")
     empties(0, 1)
-    empties(0, 0)
     tn(0)
-    ct(0)
-    rot(1)
     iota(T.one8[:], [[0, 512]], 1, 0, "one8", **FL)
     sel(T.seg8[:], T.one8[:], [[0, 64], [1, 8]], A.is_gt, 0.0, 0, 0, "one8", "seg8")
+    ct(0)
+    rot(1)
     tn(1)
     ct(1)
 
@@ -352,81 +362,97 @@ def rank_program(g, core, T, topo):
         th2, thn2 = (T.TH20, "TH20") if t == 0 else (T.TH2, "TH2")
 
         def piece(p):
-            return slice(512 * p, 512 * p + 512)
+            a, n = PIECES[p][0:2]
+            return slice(16 * a, 16 * (a + n))
+
+        def gather(p):
+            a, n = PIECES[p][0:2]
+            return win.indirect(T.off[:, a:a + n]), "off%d PX%d " % (a // 128, a // 128) + UALL
 
         def raw(p):
-            c, o, r = piece(p), T.off[:, 32 * p:32 * p + 32], "off%d " % (p // 4) + UALL
-            if RAW[p] == "s":
-                act(T.got[:, c], win.indirect(o), F.Identity, r, "got%d" % p, bias=384.0)
+            c, (w, r) = piece(p), gather(p)
+            if PIECES[p][2] == "s":
+                act(T.got[:, c], w, F.Identity, r, "got%d" % p, bias=384.0)
             else:
-                tt(T.got[:, c], win.indirect(o), T.PX[:, c], A.subtract, "PX%d " % (p // 4) + r, "got%d" % p)
+                tt(T.got[:, c], w, T.PX[:, c], A.subtract, r, "got%d" % p)
+
+        def bank_of(p):
+            bn = "bS%d" % (SUB.index(p) % 2)
+            return T[bn][:, 0:16 * PIECES[p][1]], bn
 
         def price(p):
-            bn = "bS%d" % BANK[p]
-            mm(T[bn][:], T.nI[:], T.PX[:, piece(p)], True, False, "nI PX%d" % (p // 4), bn)
+            b, bn = bank_of(p)
+            mm(b, T.nI[:], T.PX[:, piece(p)], True, False, "nI PX%d" % (PIECES[p][0] // 128), bn)
 
         def diff(p):
-            bn = "bS%d" % BANK[p]
-            mm(T[bn][:], T.If[:], T.got[:, piece(p)], False, True, "If got%d" % p, bn)
+            b, bn = bank_of(p)
+            mm(b, T.If[:], T.got[:, piece(p)], False, True, "If got%d" % p, bn)
 
         def term(p):
-            c, bn = piece(p), "bS%d" % BANK.get(p, 0)
-            if RAW[p] == "s":
-                act(T.Mx[:, c], T[bn][:], F.Relu, bn, "Mx%d" % p)
-            elif TERM[p] == "s":
+            c, kind = piece(p), PIECES[p][2] + PIECES[p][3]
+            if kind == "ss":
+                act(T.Mx[:, c], bank_of(p)[0], F.Relu, bank_of(p)[1], "Mx%d" % p)
+            elif kind == "sm":
+                tt(T.Mx[:, c], gather(p)[0], T.PX[:, c], A.max, gather(p)[1], "Mx%d" % p)
+            elif kind == "vs":
                 act(T.Mx[:, c], T.got[:, c], F.Relu, "got%d" % p, "Mx%d" % p, bias=-512.0)
             else:
                 ts(T.Mx[:, c], T.got[:, c], -512.0, 0.0, A.add, A.max, "got%d" % p, "Mx%d" % p)
 
         def names(n, a, b):
-            return " ".join("%s%d" % (n, p) for p in range(a, b))
+            return " ".join("%s%d" % (n, p) for p in range(len(PIECES)) if a <= PIECES[p][0] < b)
 
         def gains(h):
-            n = 4 if h else 3
+            a, n = 128 * h, 128 if h else 96
             if not h:
-                mm(T.bG[:, 0:128], T.zb[0:1, :], T.zb[0:1, :], True, False, "zb", "bG")
+                mm(T.bG[:, 0:128], T.prq[:], T.nI4k[:], True, False, "prq nI4k", "bG")
             for i in range(16):
-                mm(T.bG[0:32 * n, 0:128], T.Mx[:, 2048 * h + i:2048 * h + 512 * n:16], T.I256[:], h == 1 and i == 0, False,
-                   names("Mx", 4 * h, 4 * h + n) + " I256", "bG")
+                mm(T.bG[0:n, 0:128], T.Mx[:, 16 * a + i:16 * (a + n):16], T.I256[:], h == 1 and i == 0, False,
+                   names("Mx", a, a + n) + " I256", "bG")
 
         def last(p):
-            scan(T.SM[:], T.seg8[:], T.Mx[:, piece(p)], A.mult, A.add, "seg8 Mx%d" % p, "SM")
+            a, n = PIECES[p][0:2]
+            scan(T.SM[:, 16 * (a - 96):16 * (a - 96 + n)], T.seg8[:, 0:16 * n], T.Mx[:, piece(p)], A.mult, A.add, "seg8 Mx%d" % p, "SM%d" % p)
+
+        def turn(h):
             for k in range(2):
-                mm(T.bG[96:128, 0:128], T.SM[:, 7 + 8 * k:512:16], T.If256[:], False, False, "SM If256", "bG")
+                mm(T.bG[96:128, 0:128], T.SM[:, 7 + 8 * k:512:16], T.If256[:], False, False, names("SM", 96, 128) + " If256", "bG")
 
         def votes(h):
-            mm(T.bV[:, 0:128], T.prm[:, half(h)], T.BLKv[:], True, False, "prm BLKv", "bV")
+            mm(T.bV[:, 0:128], T.pz[:, half(h)], T.BLKv[:], True, False, "pz BLKv", "bV")
             for i in range(16):
                 mm(T.bV[:, i:128:16], T.got[:, 2048 * h + i:2048 * h + 2048:16], T.Ind[:], False, False,
-                   names("got", 4 * h, 4 * h + 4) + " Ind", "bV")
+                   names("got", 128 * h, 128 * h + 128) + " Ind", "bV")
             mm(T.bV[:, 0:128], T.hib[:, half(h)], T.If[:], False, True, "hib%d If" % h, "bV")
 
         def tuples(p):
-            a = 2048 if RAW[p] == "s" else 512 * (p - 2)
-            scan(T.K1[:, piece(p)], T.got[:, piece(p)], T.PK[:, a:a + 512], A.max, A.add, "PK got%d" % p, "K1%d" % p)
+            a = 0 if PIECES[p][2] == "s" else 512 + 16 * (PIECES[p][0] - VA)
+            scan(T.K1[:, piece(p)], T.got[:, piece(p)], T.PK[:, a:a + 16 * PIECES[p][1]], A.max, A.add, "PK got%d" % p, "K1%d" % p)
 
         def payload(h):
-            k1, n = T.K1[:, 2048 * h + 15:2048 * h + 2048:16], names("K1", 4 * h, 4 * h + 4)
+            k1, n = T.K1[:, 2048 * h + 15:2048 * h + 2048:16], names("K1", 128 * h, 128 * h + 128)
             ts(T.R[:, half(h)], k1, SQ / 16 - 15.0 / 32, SQ / 16 - 143.0, A.add, A.max, n, "R%d" % h)
             mm(T.bG[:, 0:128], k1, T.If16[:], False, False, n + " If16", "bG")
             mm(T.bG[:, 0:128], T.R[:, half(h)], T.nIf[:], False, True, "R%d nIf" % h, "bG")
 
         def level(h):
-            scan(T.GKs[:, h, :], T.D0G[:], T.bG[:, 0:128], A.add, A.max, "D0G bG", "GKs%d" % h)
+            scan(T.KS[:, h, 0:128], T.D0G[:], T.bG[:, 0:128], A.add, A.max, "D0G bG", "GKs%d" % h)
 
         def over(h):
-            tt(T.XI[:, 8 * h:8 * h + 8], T.GKs[:, h, 15:128:16], th[:], A.subtract, "GKs%d %s" % (h, thn), "XI%d" % h)
+            tt(T.XI[:, 8 * h:8 * h + 8], T.KS[:, h, 15:128:16], th[:], A.subtract, "GKs%d %s" % (h, thn), "XI%d" % h)
 
         def claim(h):
-            ts(T.RP[:, 8 * h:8 * h + 8], T.XI[:, 8 * h:8 * h + 8], 15 | 0x40000000, None, A.bitwise_and, None, "XI%d" % h, "RP%d" % h)
+            ts(T.DEC[:, 32 * h:32 * h + 8], T.XI[:, 8 * h:8 * h + 8], 15 | 0x40000000, None, A.bitwise_and, None, "XI%d" % h, "RP%d" % h)
 
         def place(h):
-            tt(T.hot[:, half(h)], T.RP[:, 8 * h:8 * h + 8].indirect(T.og[:]), T.q1[:], A.is_equal, "RP%d og q1" % h, "hot%d" % h)
+            tt(T.hot[:, half(h)], T.DEC[:, 32 * h:32 * h + 8].indirect(T.og[:]), T.q1[:], A.is_equal, "RP%d og q1" % h, "hot%d" % h)
+            mm(T.bF[:, 0:128], T.hot[:, half(h)], T.I64k[:], True, True, "hot%d I64k" % h, "bF")
+
+        def streams(h):
             mm(T.bC1[:, 0:208], T.I1[:], T.M1[:], True, False, "I1 M1", "bC1")
             mm(T.bC1[:, 0:208], T.onesb[0:1, :], T.c15[0:1, :], False, False, "onesb c15", "bC1")
             mm(T.bC2[:, 0:12, :], T.I1[:], T.M2[:], True, False, "I1 M2", "bC2")
             mm(T.bC2[:, 0:12, :], T.onesb[0:1, :], T.c15[0:1, 0:192], False, False, "onesb c15", "bC2")
-            mm(T.bF[:, 0:128], T.hot[:, half(h)], T.I64k[:], True, True, "hot%d I64k" % h, "bF")
 
         def column(h):
             b = slice(4 * h, 4 * h + 4)
@@ -459,10 +485,11 @@ def rank_program(g, core, T, topo):
             cp(T.l0[:, 0:8], T.SP[:, 15:128:16], "SP", "l00")
 
         def kept(h):
-            tt(T.old[:, half(h)], T.gb[:].indirect(T.l0[:, 0:8]), T.pz[:], A.add, "l00 pz " + names("gb", 0, 4), "old0")
+            tt(T.old[:, half(h)], T.gb[:].indirect(T.l0[:, 0:8]), T.pb[:], A.add, "l00 pb gb0 gb1 gb2 gb3", "old0")
 
-        def keep(p):
-            lin(T.gb[:, piece(p)], T.got[:, piece(p)], 1.0, -512.0, "got%d" % p, "gb%d" % p)
+        def keep(k):
+            c = slice(512 * k, 512 * k + 512)
+            lin(T.gb[:, c], T.got[:, c], 1.0, -512.0, names("got", 32 * k, 32 * k + 32), "gb%d" % k)
 
         def lower(h):
             scan(T["S2%d" % h][:], T["DD%d" % h][:], T.E[:, h, :], A.add, A.max, "DD%d E%d" % (h, h), "S2%d" % h)
@@ -477,24 +504,24 @@ def rank_program(g, core, T, topo):
             tt(win.indirect(T.l1[:, 2 * p:2 * p + 2]), T.old[:, c], T.Xs[:, c], A.mult, "l1%d old%d Xs%d" % (h, h, h), UALL)
 
         def vote(h):
-            scan(T.VKs[:, h, :], T.D0V[:], T.bV[:, 0:128], A.add, A.max, "D0V bV", "VKs%d" % h)
+            scan(T.KS[:, h, 128:256], T.D0V[:], T.bV[:, 0:128], A.add, A.max, "D0V bV", "VKs%d" % h)
 
         def keys(h):
-            vk = T.VKs[:, h, 15:128:16]
-            ts(T.GKi[:, h, :], T.GKs[:, h, 15:128:16], SQ, 240.0, A.add, A.max, "GKs%d" % h, "GKi%d" % h)
-            ts(T.VKi[:, h, :], vk, 2.0 ** 23 - 1280, None, A.add, None, "VKs%d" % h, "VKi%d" % h)
-            act(T.FE[:, h, 40:48], vk, F.Sign, "VKs%d" % h, "Es%d" % h, bias=2.0 ** 23)
+            ts(T.KI[:, h, :], T.KS[:, h, 15:256:16], SQ, 240.0, A.add, A.max, "GKs%d VKs%d" % (h, h), "KI%d" % h)
+            act(T.FE[:, h, 40:48], T.KS[:, h, 128 + 15:256:16], F.Sign, "VKs%d" % h, "Es%d" % h)
 
         def fields(h):
-            for k in range(h, 3):
-                ts(T.DEC[:, h, 8 * k:8 * k + 8], T.GKi[:, h, :], 4 * k, 15, A.arith_shift_right, A.bitwise_and, "GKi%d" % h, "DEC%d+" % h)
-            ts(T.DEC[:, h, 24:32], T.VKi[:, h, :], 255, None, A.bitwise_and, None, "VKi%d" % h, "DEC%d+" % h)
-            tt(T.FE[:, h, 32:40], T.GKi[:, h, :], th2[:], A.is_lt, "GKi%d %s" % (h, thn2), "Ea%d+" % h)
+            a = 32 * h
+            for k in range(1, 3):
+                ts(T.DEC[:, a + 8 * k:a + 8 * k + 8], T.KI[:, h, 0:8], 4 * k, 15, A.arith_shift_right, A.bitwise_and, "KI%d" % h, "DEC%d+" % h)
+            ts(T.DEC[:, a + 24:a + 32], T.KI[:, h, 8:16], 255, None, A.bitwise_and, None, "KI%d" % h, "DEC%d+" % h)
+            tt(T.FE[:, h, 32:40], T.KI[:, h, 0:8], th2[:], A.is_lt, "KI%d %s" % (h, thn2), "Ea%d+" % h)
 
         def features(h):
             c = half(h)
-            cp(T.FE[:, h, 8 * h:32], T.DEC[:, h, 8 * h:32], "DEC%d" % h, "Ea%d+" % h)
-            tt(T.FE[:, h, 56:64], T.DEC[:, h, 8:16], T.DEC[:, h, 8:16], A.mult, "DEC%d" % h, "Ea%d+" % h)
+            ts(T.FE[:, h, 0:32], T.DEC[:, 32 * h:32 * h + 32], 255.0, None, A.min, None, "RP%d DEC%d" % (h, h), "Ea%d+" % h)
+            w1 = T.DEC[:, 32 * h + 8:32 * h + 16]
+            tt(T.FE[:, h, 56:64], w1, w1, A.mult, "DEC%d" % h, "Ea%d+" % h)
             mm(T.bV[0:KR, 128:256], T.FE[:, h, :], T.I1[:], True, True, "Ea%d Es%d E6 I1" % (h, h), "bV")
             act(T.FT[0:KR, c], T.bV[0:KR, 128:256], F.Copy, "bV", "FT%d" % h)
 
@@ -518,6 +545,8 @@ def rank_program(g, core, T, topo):
             g.remote_dma(T["T%d" % (t + 1)][:, c], T["Tn%d" % t][:, c], T.sem[a], T.sem.loc, pid, rid, sum(1 << e for e in es))
             wr["T%d%d" % (t + 1, h)] = (a, len(es))
             nloc[0] += len(es)
+            if t == 3:
+                dma("y", T.yt[:, c], T.T4[:, c], "T4%d" % h, "yt%d" % h)
             if h == 0 and t < 2:
                 rot(t + 2)
                 tn(t + 2)
@@ -536,11 +565,11 @@ def rank_program(g, core, T, topo):
             lin(T.TH2[:], T.TH20[:], 1.0, T.msum[:, 2:3], "TH20 mc", "TH2")
 
         def mine(k):
-            if t and k < 5:
+            if k < 5:
                 codes(t, 0, k)
-            if t and k == 5:
+            if k == 5:
                 codes_in(t, 0)
-            if t and k == 6:
+            if k == 6:
                 empties(t, 0)
 
         def next_(k):
@@ -552,37 +581,38 @@ def rank_program(g, core, T, topo):
                 empties(t + 1, 1)
 
         steps = {"raw": raw, "price": price, "diff": diff, "term": term, "gains": gains, "last": last, "votes": votes, "tuples": tuples,
-                 "payload": payload, "level": level, "over": over, "claim": claim, "place": place, "column": column, "own": own,
+                 "payload": payload, "level": level, "over": over, "claim": claim, "place": place, "streams": streams, "turn": turn, "column": column, "own": own,
                  "equal": equal, "before": before, "where": where, "wlist": wlist, "kept": kept, "keep": keep, "lower": lower, "lists": lists,
                  "credit": credit, "vote": vote, "keys": keys, "fields": fields, "features": features, "mask": mask, "change": change,
                  "walk": walk, "count": count, "mine": mine, "next": next_}
         for word in ORDER.split():
             steps[word[:-1]](int(word[-1]))
 
-    ms(T.FE[:, 1, 0:8], 0.0, "Ea1")
     for t in range(4):
         visit(t)
 
     nb = YT // 16
-    for k in range(16):
-        mm(T.bS0[:, 0:nb], T.I1[:], T.U[:, PAD + k:PAD + YT:16], k == 0, k == 15, "I1 " + UALL, "bS0")
+    for j, (a, b) in enumerate(((0, nb - 64), (nb - 64, nb))):
+        bn = "bS%d" % j
+        for k in range(16):
+            mm(T[bn][:, a:b], T.I1[:], T.U[:, PAD + 16 * a + k:PAD + 16 * b:16], k == 0, k == 15, "I1 " + UALL, bn)
+        act(T.yc32[:, a:b], T[bn][:, a:b], F.Copy, bn, "yc0+")
     for a in range(YT, W, 512):
-        scan(T.ysc[:, a - YT:a - YT + 512], T.seg8[:], T.U[:, PAD + a:PAD + a + 512], A.mult, A.add, "seg8 " + UALL, "ysc+")
+        b = min(a + 512, W)
+        scan(T.ysc[:, a - YT:b - YT], T.seg8[:, 0:b - a], T.U[:, PAD + a:PAD + b], A.mult, A.add, "seg8 " + UALL, "ysc+")
     tt(T.yc32[:, nb:512], T.ysc[:, 7:W - YT:16], T.ysc[:, 15:W - YT:16], A.add, "ysc", "yc1")
-    act(T.yc32[:, 0:nb], T.bS0[:, 0:nb], F.Copy, "bS0", "yc0")
-    ts(T.yt32[:], T.T4[:], 256.0, None, A.min, None, "T40 T41", "yt32")
-    dma("y", T.yc[:], T.yc32[:], "yc0 yc1", "yc")
-    dma("s", T.yt[:], T.yt32[:], "yt32", "yt")
+    dma("s", T.yc[:, 0:nb], T.yc32[:, 0:nb], "yc0", "yca")
+    dma("y", T.yc[:, nb:512], T.yc32[:, nb:512], "yc1", "ycb")
     fin = [(q, n) for q, n in cnt.items() if n] + [("d%d" % k, 16) for k in range(ndma[0])]
     need("g", fin)
     g.wait_ge(T.sem.loc, nloc[0])
 
 
 ORDER = """
-raw6 mine5 price7 price6 raw4 raw7 diff6 raw5 mine0 term6 tuples6 mine1 diff7 term5 price0 mine2 tuples5 term4 mine3 term7
-votes1 raw0 gains1 tuples4 tuples7 raw2 payload1 mine4 term2 diff0 tuples2 level1 price1 raw1 term0 diff1 vote1 term1 over1 tuples0
-claim1 tuples1 keep1 place1 raw3 gains0 keep3 column1 keys1 term3 tuples3 last3 payload0 fields1 keep0 own1 votes0 features1 level0
-equal1 mask1 over0 mine6 change1 before1 claim0 keep2 vote0 place0 walk1 lower1 keys0 column0 fields0 lists1 features0 credit7 own0
-credit6 equal0 credit5 lower0 where0 change0 walk0 credit4 wlist0 next5 lists0 mask0 kept0 next0 credit3 next1 credit2 next6 next2
-credit1 next3 credit0 next4 count0
+raw7 raw5 raw6 price7 mine5 price8 mine0 raw8 streams1 tuples5 diff7 diff8 mine1 term6 mine2 tuples8 term5 tuples7 term7 votes1 term8
+mine3 price0 tuples6 raw2 gains1 mine4 payload1 raw1 raw3 price1 raw4 diff1 level1 tuples3 raw0 term2 vote1 term1 diff0 over1 tuples0
+votes0 term0 keys1 claim1 tuples1 keep2 place1 term4 tuples2 term3 tuples4 keep1 mine6 fields1 last3 last4 gains0 turn0 payload0 vote0
+features1 column1 level0 over0 keys0 change1 own1 mask1 claim0 fields0 walk1 place0 equal1 streams0 keep0 before1 features0 lower1
+column0 keep3 lists1 credit7 credit6 own0 credit5 where0 equal0 credit4 wlist0 change0 next5 lower0 mask0 kept0 lists0 walk0 next0
+credit3 count0 next6 next1 credit2 next2 credit1 next3 credit0 next4
 """

@@ -7,10 +7,11 @@ TR = PAD + W
 UW = TR + 32
 TOP = 32768 + W - 1 + PAD
 SQ = 20480.0
-KR = 64
+KR = 56
 RHO = [0, 5, 10, 15]
-PIECES = [(0, 32, "s", "s"), (32, 32, "s", "s"), (64, 32, "v", "s"), (96, 16, "v", "v"), (112, 16, "v", "v"),
-          (128, 32, "v", "s"), (160, 32, "v", "v"), (192, 32, "s", "s"), (224, 32, "s", "s")]
+GATHER = "ssvvvvss"
+CUT = "sssvsvss"
+VA, VB = 64, 192
 YT = 4224
 
 SCRATCH = {}
@@ -21,23 +22,23 @@ def _b(name, cols, dtype, where="sbuf"):
 
 
 for _n, _c in (("U", UW), ("Mx", 4096), ("gb", 2048), ("D0G", 128), ("D0V", 128), ("segm", 128), ("seg8", 512), ("one8", 512),
-               ("T0", 256), ("T1", 256), ("T2", 256), ("T3", 256), ("Tn0", 256), ("Tn1", 256), ("Tn2", 256), ("nI4k", 128), ("prq", 128),
-               ("Tt", 256), ("Nn", 256), ("prb", 256), ("FT", 256), ("Xs", 256), ("old", 256), ("hot", 256),
-               ("onesb", 128), ("I1", 128), ("I256", 128), ("I64k", 128), ("BLKN", 128), ("TNb", 128), ("CTa", 128),
-               ("CQ", 128), ("CX", 128), ("zb", 128), ("m16", 4), ("M1", 208), ("M2", (12, 16)), ("DK", 208), ("DKp", 128), ("MP", 128),
-               ("c15", 208), ("c16", 128), ("E", (2, 192)), ("RT", 512), ("TN", 512), ("CT", 512), ("FE", (2, KR))):
+               ("T0", 256), ("T1", 256), ("T2", 256), ("T3", 256), ("Tn0", 256), ("Tn1", 256), ("Tn2", 256),
+               ("Tt", 256), ("Nn", 256), ("prb", 256), ("FT", 256), ("Xq", 256), ("Xs", 256), ("old", 256), ("hot", 256),
+               ("onesb", 128), ("minus", 128), ("I1", 128), ("I256", 128), ("I64k", 128), ("BLKN", 128), ("TNb", 128), ("CTa", 128),
+               ("CQ", 144), ("CX", 128), ("zb", 128), ("m16", 4), ("M1", 208), ("M2", (12, 16)), ("DK", 208), ("DKp", 32),
+               ("E", 384), ("RT", 512), ("TN", 512), ("CT", 512), ("FE", (2, KR))):
     _b(_n, _c, "bfloat16")
 for _n, _c in (("xx", 256), ("pd", 256), ("KS", (2, 256)), ("TH0", 8), ("TH", 8), ("TH20", 8), ("TH2", 8),
-               ("Z", (8, 3, 16)), ("S10", 208), ("S11", 208), ("DD0", 192), ("DD1", 192), ("S20", 192), ("S21", 192), ("SP", 128),
+               ("Z", (8, 3, 16)), ("S10", 208), ("S11", 208), ("DD", 384), ("S2", 384),
                ("BLK", 128), ("BLKs", 128), ("GM", 128), ("mif", 128), ("mf", 128), ("mgf", 128), ("w8", 8), ("OH", 8), ("OHN", 16),
-               ("colsf", 24), ("msum", 4), ("junk", 16), ("T4", 256), ("Tn3", 256), ("rho3", 4), ("yc32", 512), ("mi2", 128), ("q1", 128), ("q2", 128),
-               ("s2", 128), ("s3", 128), ("ge", 64)):
+               ("colsf", 24), ("msum", 4), ("junk", 16), ("T4", 256), ("Tn3", 256), ("yc32", 512), ("mi2", 128), ("q1", 128),
+               ("s2", 128), ("ge", 64)):
     _b(_n, _c, "float32")
-for _n, _c in (("tsti", 256), ("z", 256), ("ci", 256), ("KI", (2, 16)), ("DEC", 64), ("XI", 16),
-               ("thr", 8), ("thb", 8), ("pc", 8)):
+for _n, _c in (("tsti", 256), ("z", 256), ("ci", 256), ("KI", (2, 16)), ("DEC", 64), ("XI", 16), ("thr", 8), ("thb", 8), ("pc", 8)):
     _b(_n, _c, "int32")
-for _n, _c in (("got", 4096), ("PK", 3072), ("PX", 4096), ("K1", 4096), ("prx", 256), ("prm", 256), ("pz", 256), ("pb", 128), ("BLKv", 128), ("nI", 128),
-               ("Ind", 8), ("R", 256), ("If", 128), ("If16", 128), ("nIf", 128), ("If256", 128), ("hib", 256), ("SM", 512), ("ysc", W - YT)):
+for _n, _c in (("got", 4096), ("PK", 512 + 16 * (VB - VA)), ("PX", 4096), ("K1", 4096), ("prx", 256), ("prm", 256), ("pz", 256), ("pb", 128),
+               ("c16", 8), ("BLKv", 128), ("nI", 128), ("Ind", 8), ("R", 256), ("If", 128), ("If16", 128), ("nIf", 128), ("hib", 256),
+               ("ysc", W - YT)):
     _b(_n, _c, "float16")
 for _n, _c in (("off", 256), ("l0", 16), ("l1", 16), ("og", 8)):
     _b(_n, _c, "uint16")
@@ -45,7 +46,7 @@ for _n in ("S0", "S1", "G", "V", "F", "L", "C1"):
     _b("b" + _n, 512, "float32", "psum")
 _b("bC2", (32, 16), "float32", "psum")
 
-SEMAPHORES = ["cv", "cs", "ct", "cg", "loc"] + ["d%d" % k for k in range(10)] + ["a%d%d" % (k, h) for k in range(1, 5) for h in range(2)]
+SEMAPHORES = ["cv", "cs", "ct", "cg", "loc"] + ["d%d" % k for k in range(12)] + ["a%d%d" % (k, h) for k in range(1, 5) for h in range(2)]
 
 
 def rank_program(g, core, T, topo):
@@ -176,10 +177,8 @@ def rank_program(g, core, T, topo):
     dma("y", T.U[:, PAD:PAD + 4096], T.cov[:, 0:4096], "", "Ua")
     UALL = "Ua Ub Uc"
 
-    PI, PJ, PG, P8, FF, PP, J0, J1, CTA, CQC, M2C, K0, KC = range(13)
-    SUB = [p for p in range(len(PIECES)) if PIECES[p][2:] == ("s", "s")]
-    VA = min(a for a, n, who, how in PIECES if who == "v")
-    VB = max(a + n for a, n, who, how in PIECES if who == "v")
+    PI, PJ, PG, P8, FF, PP, J0, J1, CTA, CQC, NW, R3, K0, KC = range(14)
+    RUNS = ((0, VA, False), (VA, VB, True), (VB, 256, False))
     FL = {"allow_small_or_imprecise_dtypes": True}
 
     def col(k):
@@ -223,30 +222,23 @@ def rank_program(g, core, T, topo):
         if t < 3:
             lin(T.Tt[:, c], T[src][:, c], 1.0, T.OHN[:, RHO[t]:RHO[t] + 1], "%s%d OHN" % (src, h), "Tt%d" % h)
         else:
-            act(T.Tt[:, c], T[src][:, c], F.Relu, "%s%d rho3" % (src, h), "Tt%d" % h, scale=-1.0, bias=T.rho3[:, 0:1])
+            act(T.Tt[:, c], T[src][:, c], F.Relu, "%s%d fr" % (src, h), "Tt%d" % h, scale=-1.0, bias=col(R3))
             lin(T.Tt[:, c], T.Tt[:, c], -1.0, 256.0, "Tt%d" % h, "Tt%d" % h)
 
     def prices(h, i):
         cp(T.PX[:, 2048 * h + i:2048 * h + 2048:16], T.prx[:, half(h)], "prx", "PX%d+" % h)
 
     ms(T.onesb[:], 1.0, "onesb")
-    ms(T.PK[:, 0:512 + 16 * (VB - VA)], 1.0 / 16, "PK")
+    ms(T.PK[:], 1.0 / 16, "PK")
     ts(T.pc[:, 2:4], T.pc[:, 0:2], 15, None, A.bitwise_and, None, "pc0", "pc1+")
     for k, (sh, msk) in enumerate(((4, 7), (0, 7), (3, 15))):
         ts(T.pc[:, 4 + k:5 + k], T.pc[:, 0:1], sh, msk, A.arith_shift_right, A.bitwise_and, "pc0", "pc1+")
     cp(col(PP), T.pc[:, 0:1], "pc0", "fp")
     cp(T.colsf[:, PI:PI + 5], T.pc[:, 2:7], "pc1", "f")
-    runs = []
-    for a, n, who, how in PIECES:
-        kind = "m" if how == "m" else who
-        if runs and runs[-1][2] == kind:
-            runs[-1][1] = a + n
-        else:
-            runs.append([a, a + n, kind])
-    for a, b, kind in runs[::-1]:
-        lin(T.prx[:, a:b], T.prb[:, a:b], 1.0, {"v": -512.0, "s": 384.0, "m": 0.0}[kind], "prb", "prx+")
-    for a, b, kind in runs:
-        lin(T.prm[:, a:b], T.prb[:, a:b], 1.0 if kind == "v" else 0.0, -640.0 if kind == "v" else -512.0, "prb", "prm+")
+    for a, b, v in RUNS[::-1]:
+        lin(T.prx[:, a:b], T.prb[:, a:b], 1.0, -512.0 if v else 384.0, "prb", "prx+")
+    for a, b, v in RUNS:
+        lin(T.prm[:, a:b], T.prb[:, a:b], 1.0 if v else 0.0, -640.0 if v else -512.0, "prb", "prm+")
     ts(T.BLK[:], T.mgf[:], col(PG), None, A.is_equal, None, "mgf f", "BLK")
     ts(T.mi2[:], T.mif[:], col(PJ), 2.0, A.is_equal, A.mult, "mif f", "mi2")
     ts(T.pd[:, half(1)], T.tsti[:, half(1)], 256.0, NONE, A.is_ge, A.mult, "tsti", "pd1")
@@ -259,8 +251,10 @@ def rank_program(g, core, T, topo):
     codes_in(0, 1)
     tt(T.T0[:, half(0)], T.pd[:, half(0)], T.tsti[:, half(0)], A.max, "pd0 tsti", "T00")
     ts(T.segm[:], T.mif[:], 0.0, None, A.is_gt, None, "mif", "segm")
-    ts(T.DKp[:], T.mif[:], col(PI), 8192.0, A.is_equal, A.mult, "mif f", "DKp")
+    ts(T.DKp[:], T.mif[:, 0:32], col(PI), 64.0, A.is_equal, A.mult, "mif f", "DKp")
     ts(T.OH[:], T.w8[:], col(FF), None, A.is_equal, None, "w8 f", "OH")
+    ts(T.ge[:], T.mif[:, 0:64], col(PI), -64.0, A.is_ge, A.mult, "mif f", "ge")
+    ms(T.M2[:], 2.5, "M2")
     ts(T.GM[:], T.mgf[:], col(P8), None, A.is_equal, None, "mgf f", "GM")
     for n, v in (("If", 1.0), ("nI", -1.0), ("I256", 256.0), ("If16", 16.0), ("nIf", -16.0)):
         act(T[n][:], T.I1[:], F.Copy, "I1", n, scale=v)
@@ -275,85 +269,73 @@ def rank_program(g, core, T, topo):
     cp(T.PK[:, 512 + 15:512 + 16 * (VB - VA):16], T.prm[:, VA:VB], "prm", "PK+")
     codes(0, 1, 4)
     ts(T.OHN[:], T.mif[:, 0:16], col(PI), NONE, A.is_equal, A.mult, "mif f", "OHN")
-    ts(T.ge[:], T.mif[:, 0:64], col(PI), -64.0, A.is_ge, A.mult, "mif f", "ge")
-    ms(T.M2[:], 2.5, "M2")
     ts(T.Ind[:], T.w8[:], col(PG), 4096.0, A.is_equal, A.mult, "w8 f", "Ind")
     cp(T.og[:], T.w8[:], "w8", "og")
-    ms(T.c15[0:1, :], (TOP % 8192) / 16384.0, "c15")
     for i in range(16):
         prices(0, i)
 
     iota(T.DK[:], [[0, 208]], 0, 0, "DK", **FL)
-    op("g", lambda: g.partition_broadcast(T.thb[:], T.thr[0:1, 0:8], 128), "thr", "thb")
     iota(T.Z[:, :, 2, :], [[0, 8], [0, 16]], 0, 0, "Z0 Z1", **FL)
     iota(T.FE[:, :, 48:56], [[0, 2], [0, 8]], 1, 0, "E6", **FL)
-    for h in range(2):
-        iota(T["DD%d" % h][:], [[0, 192]], 0, 0, "DD%d" % h, **FL)
-    for k in range(4):
-        iota(T["DD%d" % (k % 2)][:, 16 * (k // 2):192:48], [[0, 4]], -64, 0, "DD%d%s" % (k % 2, "+" if k > 1 else ""), **FL)
-    iota(T.zb[:], [[0, 128]], 0, 0, "zb", **FL)
+    iota(T.DD[:], [[0, 384]], 0, 0, "DD0 DD1", **FL)
+    iota(T.minus[0:1, :], [[0, 128]], -1, 0, "minus", **FL)
+    for k in range(2):
+        iota(T.DD[:, 16 * k:384:48], [[0, 8]], -64, 0, "DD0+ DD1+" if k else "DD0 DD1", **FL)
     sel(T.TNb[:], T.BLKN[:], [[1, 128]], A.is_gt, 0.0, 0, -1, "BLKN", "TNb")
+    iota(T.zb[:], [[0, 128]], 0, 0, "zb", **FL)
+    op("g", lambda: g.partition_broadcast(T.thb[:], T.thr[0:1, 0:8], 128), "thr", "thb")
     sel(T.TNb[:], T.TNb[:], [[1, 128]], A.not_equal, -NONE, 0, -1, "TNb", "TNb")
-
-    def rot(t):
-        s, n = 1 + t, "RT%d" % t
-        b = T.RT[:, 128 * t:128 * t + 128]
-        sel(b, T.zb[:], [[-16, 8], [-1, 16]], A.not_equal, 2.0, -s, 1, "zb", n)
-        sel(b, b, [[-16, 8], [-1, 16]], A.not_equal, 2.0, 16 - s, 1, n, n)
-        sel(b, b, [[-16, 8], [0, 16]], A.is_ge, 0.0, 0, 1, n, n)
-        sel(b, b, [[16, 8], [0, 16]], A.is_ge, 0.0, 15, -1, n, n)
+    iota(T.CQ[0:32, :], [[0, 144]], 0, 0, "CQ", **FL)
 
     def tn(t):
         sel(T.TN[:, 128 * t:128 * t + 128], T.TNb[:], [[0, 8], [1, 16]], A.not_equal, 0.0, -RHO[t], 0, "TNb", "TN%d" % t)
 
-    def ct(t):
+    def turns(t, u):
         n, a = "CT%d" % t, 128 * t
         sel(T.CT[0:KR, a:a + 128], T.CTa[0:KR, :], [[0, 8], [1, 16]], A.not_equal, 0.0, -RHO[t], 0, "CTa", n)
         c = T.CT[0:KR, a + RHO[t]:a + 128:16]
-        for f, v in ((1, -16.0), (2, 1.0), (4, NONE), (6, 240.0)):
+        for k, (f, v) in enumerate(((1, -16.0), (2, 1.0), (4, NONE), (6, 240.0))):
+            if u < 4:
+                b, m = T.RT[:, 128 * u:128 * u + 128], "RT%d" % u
+                pat, cmp, fill, base, cm = (([[-16, 8], [-1, 16]], A.not_equal, 2.0, -1 - u, 1), ([[-16, 8], [-1, 16]], A.not_equal, 2.0, 15 - u, 1),
+                                            ([[-16, 8], [0, 16]], A.is_ge, 0.0, 0, 1), ([[16, 8], [0, 16]], A.is_ge, 0.0, 15, -1))[k]
+                sel(b, b if k else T.zb[:], pat, cmp, fill, base, cm, m if k else "zb", m)
             sel(c, c, [[-1, 8]], A.not_equal, v, -8 * f, 1, n, n)
 
     lin(T.D0G[:], T.segm[:], 2.0 ** 25 + 16, -2.0 ** 25, "segm", "D0G")
     act(T.BLKv[:], T.BLK[:], F.Copy, "BLK", "BLKv", scale=4096.0)
     act(T.I64k[:], T.I1[:], F.Copy, "I1", "I64k", scale=65536.0)
     act(T.BLKs[:], T.BLK[:], F.Copy, "BLK", "BLKs", scale=-2.0 ** -14)
-    act(T.If256[:], T.I1[:], F.Copy, "I1", "If256", scale=256.0)
     lin(T.D0V[:], T.segm[:], 2.0 ** 27 + 256, -2.0 ** 27, "segm", "D0V")
-    act(T.nI4k[:], T.I1[:], F.Copy, "I1", "nI4k", scale=-4096.0)
-    for a, b, kind in runs:
-        if a < 128:
-            act(T.prq[:, a:min(b, 128)], T.prb[:, a:min(b, 128)], F.Copy, "prb", "prq+", scale=1.0 if kind == "m" else 0.0)
-    lin(col(M2C), oh(1), -2.0, 0.0, "OH", "fm")
-    act(T.s2[32:64, :], T.q1[32:64, :], F.Square, "q1 OH", "s2+", scale=T.OH[32:64, 6:7], bias=T.OH[32:64, 7:8])
-    act(T.s2[0:32, :], T.q1[0:32, :], F.Copy, "q1 fm", "s2+", scale=T.colsf[0:32, M2C:M2C + 1])
-    act(T.c16[0:1, :], T.mf[0:1, :], F.Copy, "mf", "c16", scale=16.0)
+    lin(col(NW), oh(1), -1.0, 0.0, "OH", "fn")
     lin(T.pz[:], T.prm[:], 1.0, 128.0, "prm", "pz")
-    lin(T.pb[:], T.prm[:, 0:128], 1.0, 640.0, "prm", "pb")
     lin(col(J0), col(PI), 1.0, float(TR), "f", "fj+")
     lin(col(J1), col(PI), 1.0, float(TR + 16), "f", "fj+")
+    lin(T.s2[:], T.q1[:], oh(6), col(NW), "q1 OH fn", "s2")
     for k in range(4):
-        act(T.DK[:, 48 * k:48 * k + 32], T.DKp[:, 0:32], F.Copy, "DKp", "DK+", scale=1.0 / 128)
+        act(T.DK[:, 48 * k:48 * k + 32], T.DKp[:], F.Copy, "DKp", "DK+")
         f, v = ((3, 1.0), (4, -NONE), (5, -NONE / 2), (6, 2.5 * NONE))[k]
         lin(col(CTA), oh(f), v, col(CTA) if k else 0.0, "OH fa", "fa")
         if k < 2:
-            lin(col(CQC), oh(6 * k), (-1.0, 15.0)[k], col(CQC) if k else 0.0, "OH fq", "fq")
             lin(T.M2[:, 2 * k:12:3, :], T.ge[:], 1.0, 2.5, "ge", "M2+")
     lin(T.M1[:], T.DK[:], -0.5, 34.5, "DK", "M1")
     act(T.CTa[:], T.GM[:], F.Copy, "GM fa", "CTa", scale=col(CTA))
-    lin(T.MP[:], T.DKp[:], -0.5, 4096.0, "DKp", "MP")
-    act(T.CQ[:], T.GM[:], F.Copy, "GM fq", "CQ", scale=col(CQC))
-    lin(T.rho3[:, 0:1], T.OHN[:, RHO[3]:RHO[3] + 1], -1.0, 256.0, "OHN", "rho3")
     ts(T.TH0[:], T.thb[:], 256.0, -SQ, A.mult, A.add, "thb", "TH0")
     ts(T.TH20[:], T.thb[:], 256.0, None, A.mult, None, "thb", "TH20")
-    tt(T.CX[0:KR, :], T.s2[0:KR, :], T.GM[0:KR, :], A.mult, "s2 GM", "CX")
-    empties(0, 1)
+
+    def late():
+        tt(T.CX[0:KR, :], T.s2[0:KR, :], T.GM[0:KR, :], A.mult, "s2 GM", "CX")
+        empties(0, 1)
+        lin(col(CQC), col(PI), 16.0, 15.0, "f", "fq")
+        lin(T.pb[:], T.prm[:, 0:128], 1.0, 640.0, "prm", "pb")
+        lin(T.c16[:], T.w8[:], 256.0, col(CQC), "w8 fq", "c16")
+        lin(col(R3), T.OHN[:, RHO[3]:RHO[3] + 1], -1.0, 256.0, "OHN", "fr")
+
     tn(0)
+    turns(0, 1)
     iota(T.one8[:], [[0, 512]], 1, 0, "one8", **FL)
+    sel(T.CQ[0:32, :], T.CQ[0:32, :], [[1, 144]], A.not_equal, -1.0, -15, -16, "CQ", "CQ")
     sel(T.seg8[:], T.one8[:], [[0, 64], [1, 8]], A.is_gt, 0.0, 0, 0, "one8", "seg8")
-    ct(0)
-    rot(1)
-    tn(1)
-    ct(1)
 
     win = T.U[:, 0:UW]
 
@@ -362,75 +344,51 @@ def rank_program(g, core, T, topo):
         th2, thn2 = (T.TH20, "TH20") if t == 0 else (T.TH2, "TH2")
 
         def piece(p):
-            a, n = PIECES[p][0:2]
-            return slice(16 * a, 16 * (a + n))
+            return slice(512 * p, 512 * p + 512)
 
-        def gather(p):
-            a, n = PIECES[p][0:2]
-            return win.indirect(T.off[:, a:a + n]), "off%d PX%d " % (a // 128, a // 128) + UALL
+        def names(n, h):
+            return " ".join("%s%d" % (n, p) for p in range(4 * h, 4 * h + 4))
 
         def raw(p):
-            c, (w, r) = piece(p), gather(p)
-            if PIECES[p][2] == "s":
+            c, w, r = piece(p), win.indirect(T.off[:, 32 * p:32 * p + 32]), "off%d " % (p // 4) + UALL
+            if GATHER[p] == "s":
                 act(T.got[:, c], w, F.Identity, r, "got%d" % p, bias=384.0)
             else:
-                tt(T.got[:, c], w, T.PX[:, c], A.subtract, r, "got%d" % p)
-
-        def bank_of(p):
-            bn = "bS%d" % (SUB.index(p) % 2)
-            return T[bn][:, 0:16 * PIECES[p][1]], bn
+                tt(T.got[:, c], w, T.PX[:, c], A.subtract, "PX%d " % (p // 4) + r, "got%d" % p)
 
         def price(p):
-            b, bn = bank_of(p)
-            mm(b, T.nI[:], T.PX[:, piece(p)], True, False, "nI PX%d" % (PIECES[p][0] // 128), bn)
+            bn = "bS%d" % (p % 2)
+            mm(T[bn][:], T.nI[:], T.PX[:, piece(p)], True, False, "nI PX%d" % (p // 4), bn)
 
         def diff(p):
-            b, bn = bank_of(p)
-            mm(b, T.If[:], T.got[:, piece(p)], False, True, "If got%d" % p, bn)
+            bn = "bS%d" % (p % 2)
+            mm(T[bn][:], T.If[:], T.got[:, piece(p)], False, True, "If got%d" % p, bn)
 
         def term(p):
-            c, kind = piece(p), PIECES[p][2] + PIECES[p][3]
-            if kind == "ss":
-                act(T.Mx[:, c], bank_of(p)[0], F.Relu, bank_of(p)[1], "Mx%d" % p)
-            elif kind == "sm":
-                tt(T.Mx[:, c], gather(p)[0], T.PX[:, c], A.max, gather(p)[1], "Mx%d" % p)
-            elif kind == "vs":
+            c, bn = piece(p), "bS%d" % (p % 2)
+            if GATHER[p] == "s":
+                act(T.Mx[:, c], T[bn][:], F.Relu, bn, "Mx%d" % p)
+            elif CUT[p] == "s":
                 act(T.Mx[:, c], T.got[:, c], F.Relu, "got%d" % p, "Mx%d" % p, bias=-512.0)
             else:
                 ts(T.Mx[:, c], T.got[:, c], -512.0, 0.0, A.add, A.max, "got%d" % p, "Mx%d" % p)
 
-        def names(n, a, b):
-            return " ".join("%s%d" % (n, p) for p in range(len(PIECES)) if a <= PIECES[p][0] < b)
-
         def gains(h):
-            a, n = 128 * h, 128 if h else 96
-            if not h:
-                mm(T.bG[:, 0:128], T.prq[:], T.nI4k[:], True, False, "prq nI4k", "bG")
             for i in range(16):
-                mm(T.bG[0:n, 0:128], T.Mx[:, 16 * a + i:16 * (a + n):16], T.I256[:], h == 1 and i == 0, False,
-                   names("Mx", a, a + n) + " I256", "bG")
-
-        def last(p):
-            a, n = PIECES[p][0:2]
-            scan(T.SM[:, 16 * (a - 96):16 * (a - 96 + n)], T.seg8[:, 0:16 * n], T.Mx[:, piece(p)], A.mult, A.add, "seg8 Mx%d" % p, "SM%d" % p)
-
-        def turn(h):
-            for k in range(2):
-                mm(T.bG[96:128, 0:128], T.SM[:, 7 + 8 * k:512:16], T.If256[:], False, False, names("SM", 96, 128) + " If256", "bG")
+                mm(T.bG[:, 0:128], T.Mx[:, 2048 * h + i:2048 * h + 2048:16], T.I256[:], i == 0, False, names("Mx", h) + " I256", "bG")
 
         def votes(h):
             mm(T.bV[:, 0:128], T.pz[:, half(h)], T.BLKv[:], True, False, "pz BLKv", "bV")
             for i in range(16):
-                mm(T.bV[:, i:128:16], T.got[:, 2048 * h + i:2048 * h + 2048:16], T.Ind[:], False, False,
-                   names("got", 128 * h, 128 * h + 128) + " Ind", "bV")
+                mm(T.bV[:, i:128:16], T.got[:, 2048 * h + i:2048 * h + 2048:16], T.Ind[:], False, False, names("got", h) + " Ind", "bV")
             mm(T.bV[:, 0:128], T.hib[:, half(h)], T.If[:], False, True, "hib%d If" % h, "bV")
 
         def tuples(p):
-            a = 0 if PIECES[p][2] == "s" else 512 + 16 * (PIECES[p][0] - VA)
-            scan(T.K1[:, piece(p)], T.got[:, piece(p)], T.PK[:, a:a + 16 * PIECES[p][1]], A.max, A.add, "PK got%d" % p, "K1%d" % p)
+            a = 0 if GATHER[p] == "s" else 512 + 512 * p - 16 * VA
+            scan(T.K1[:, piece(p)], T.got[:, piece(p)], T.PK[:, a:a + 512], A.max, A.add, "PK got%d" % p, "K1%d" % p)
 
         def payload(h):
-            k1, n = T.K1[:, 2048 * h + 15:2048 * h + 2048:16], names("K1", 128 * h, 128 * h + 128)
+            k1, n = T.K1[:, 2048 * h + 15:2048 * h + 2048:16], names("K1", h)
             ts(T.R[:, half(h)], k1, SQ / 16 - 15.0 / 32, SQ / 16 - 143.0, A.add, A.max, n, "R%d" % h)
             mm(T.bG[:, 0:128], k1, T.If16[:], False, False, n + " If16", "bG")
             mm(T.bG[:, 0:128], T.R[:, half(h)], T.nIf[:], False, True, "R%d nIf" % h, "bG")
@@ -446,58 +404,58 @@ def rank_program(g, core, T, topo):
 
         def place(h):
             tt(T.hot[:, half(h)], T.DEC[:, 32 * h:32 * h + 8].indirect(T.og[:]), T.q1[:], A.is_equal, "RP%d og q1" % h, "hot%d" % h)
-            mm(T.bF[:, 0:128], T.hot[:, half(h)], T.I64k[:], True, True, "hot%d I64k" % h, "bF")
+            mm(T.bF[:, 0:128], T.onesb[0:1, :], T.minus[0:1, :], True, False, "onesb minus", "bF")
+            mm(T.bF[:, 0:128], T.hot[:, half(h)], T.I64k[:], False, True, "hot%d I64k" % h, "bF")
+
+        FIRST = ("bS0", "bC1")
 
         def streams(h):
-            mm(T.bC1[:, 0:208], T.I1[:], T.M1[:], True, False, "I1 M1", "bC1")
-            mm(T.bC1[:, 0:208], T.onesb[0:1, :], T.c15[0:1, :], False, False, "onesb c15", "bC1")
-            mm(T.bC2[:, 0:12, :], T.I1[:], T.M2[:], True, False, "I1 M2", "bC2")
-            mm(T.bC2[:, 0:12, :], T.onesb[0:1, :], T.c15[0:1, 0:192], False, False, "onesb c15", "bC2")
+            mm(T[FIRST[h]][:, 0:208], T.I1[:], T.M1[:], True, False, "I1 M1", FIRST[h])
+            mm(T.bC2[:, 12 * h:12 * h + 12, :], T.I1[:], T.M2[:], True, False, "I1 M2", "bC2")
 
         def column(h):
             b = slice(4 * h, 4 * h + 4)
             tt(T.Z[:, b, 0:2, :], T.bF[:, 0:128], T.ci[:, half(h)], A.min, "bF ci%d" % h, "Z%d" % h)
-            mm(T.bC1[:, 0:192], T.BLKs[:], T.Z[:, b, :, :], False, True, "BLKs Z%d" % h, "bC1")
-            for s, u in ((0, 0), (1, 0), (2, 1)):
-                mm(T.bC2[:, s:12:3, :], T.BLKs[:], T.Z[:, b, u, :], False, s == 2, "BLKs Z%d" % h, "bC2")
+            mm(T[FIRST[h]][:, 0:192], T.BLKs[:], T.Z[:, b, :, :], False, True, "BLKs Z%d" % h, FIRST[h])
+            for e, u in ((0, 0), (1, 0), (2, 1)):
+                mm(T.bC2[:, 12 * h + e:12 * h + 12:3, :], T.BLKs[:], T.Z[:, b, u, :], False, e == 2, "BLKs Z%d" % h, "bC2")
 
         def own(h):
-            scan(T["S1%d" % h][:], T.DK[:], T.bC1[:, 0:208], A.add, A.min, "DK bC1", "S1%d" % h, 64.0)
+            scan(T["S1%d" % h][:], T.DK[:], T[FIRST[h]][:, 0:208], A.add, A.min, "DK " + FIRST[h], "S1%d" % h, 64.0)
 
         def equal(h):
-            s1, dd = T["S1%d" % h], T["DD%d" % h]
+            s1, a = T["S1%d" % h], 192 * h
             for u in range(2):
-                act(dd[:, 15 + 32 * u:192:48], s1[:, 15 + 16 * u:192:48], F.Copy, "S1%d" % h, "DD%d+" % h)
-            tt(T.E[:, h, :], s1[:, 16:208], T.bC2[:, 0:12, :], A.is_equal, "S1%d bC2" % h, "E%d" % h)
-
-        def before(h):
-            for u in range(2):
-                ts(T.l0[:, 8 * h + u:8 * h + 8:2], T["S1%d" % h][:, 15 + 16 * u:192:48], 16384.0, float(TR), A.mult, A.min, "S1%d" % h, "l0%d+" % h)
-            act(T.old[:, half(h)], win.indirect(T.l0[:, 8 * h:8 * h + 8]), F.Copy, "l0%d " % h + UALL, "old%d" % h)
-
-        def where(h):
-            mm(T.bF[:, 256:384], T.I1[:], T.MP[:], True, False, "I1 MP", "bF")
-            mm(T.bF[:, 256:384], T.onesb[0:1, :], T.c16[0:1, :], False, False, "onesb c16", "bF")
-            mm(T.bF[:, 256:384], T.CQ[0:KR, :], T.FT[0:KR, half(h)], False, True, "CQ FT%d" % h, "bF")
-            scan(T.SP[:], T.DKp[:], T.bF[:, 256:384], A.add, A.min, "DKp bF", "SP", 8192.0)
-
-        def wlist(h):
-            cp(T.l0[:, 0:8], T.SP[:, 15:128:16], "SP", "l00")
-
-        def kept(h):
-            tt(T.old[:, half(h)], T.gb[:].indirect(T.l0[:, 0:8]), T.pb[:], A.add, "l00 pb gb0 gb1 gb2 gb3", "old0")
-
-        def keep(k):
-            c = slice(512 * k, 512 * k + 512)
-            lin(T.gb[:, c], T.got[:, c], 1.0, -512.0, names("got", 32 * k, 32 * k + 32), "gb%d" % k)
+                act(T.DD[:, a + 15 + 32 * u:a + 192:48], s1[:, 15 + 16 * u:192:48], F.Copy, "S1%d" % h, "DD%d+" % h)
+            tt(T.E[:, a:a + 192], s1[:, 16:208], T.bC2[:, 12 * h:12 * h + 12, :], A.is_equal, "S1%d bC2" % h, "E%d" % h)
 
         def lower(h):
-            scan(T["S2%d" % h][:], T["DD%d" % h][:], T.E[:, h, :], A.add, A.max, "DD%d E%d" % (h, h), "S2%d" % h)
+            c = slice(192 * h, 192 * h + 192)
+            scan(T.S2[:, c], T.DD[:, c], T.E[:, c], A.add, A.max, "DD%d E%d" % (h, h), "S2%d" % h)
 
         def lists(h):
             for u in range(2):
-                ts(T.l1[:, 8 * h + u:8 * h + 8:2], T["S2%d" % h][:, 15 + 32 * u:192:48], 16384.0, col(J0 + u), A.mult, A.min,
+                ts(T.l1[:, 8 * h + u:8 * h + 8:2], T.S2[:, 192 * h + 15 + 32 * u:192 * h + 192:48], 16384.0, col(J0 + u), A.mult, A.min,
                    "S2%d fj" % h, "l1%d+" % h)
+
+        def before(h):
+            for u in range(2):
+                ts(T.l0[:, 8 + u:16:2], T.S11[:, 15 + 16 * u:192:48], 16384.0, float(TR), A.mult, A.min, "S11", "l01+")
+            act(T.old[:, half(1)], win.indirect(T.l0[:, 8:16]), F.Copy, "l01 " + UALL, "old1")
+
+        def keep(p):
+            lin(T.gb[:, piece(p)], T.got[:, piece(p)], 1.0, -512.0, "got%d" % p, "gb%d" % p)
+
+        def where(h):
+            mm(T.bG[:, 256:264], T.If[:], T.c16[:], True, False, "If c16", "bG")
+            for j in range(16):
+                mm(T.bG[:, 256:264], T.CQ[0:32, 15 - j:143 - j], T.FT[0:32, j:128:16], False, j == 15, "CQ FT0", "bG")
+
+        def wlist(h):
+            cp(T.l0[:, 0:8], T.bG[:, 256:264], "bG", "l00")
+
+        def kept(h):
+            tt(T.old[:, half(0)], T.gb[:].indirect(T.l0[:, 0:8]), T.pb[:], A.add, "l00 pb " + names("gb", 0), "old0")
 
         def credit(p):
             c, h = slice(32 * p, 32 * p + 32), p // 4
@@ -518,16 +476,16 @@ def rank_program(g, core, T, topo):
             tt(T.FE[:, h, 32:40], T.KI[:, h, 0:8], th2[:], A.is_lt, "KI%d %s" % (h, thn2), "Ea%d+" % h)
 
         def features(h):
-            c = half(h)
             ts(T.FE[:, h, 0:32], T.DEC[:, 32 * h:32 * h + 32], 255.0, None, A.min, None, "RP%d DEC%d" % (h, h), "Ea%d+" % h)
-            w1 = T.DEC[:, 32 * h + 8:32 * h + 16]
-            tt(T.FE[:, h, 56:64], w1, w1, A.mult, "DEC%d" % h, "Ea%d+" % h)
             mm(T.bV[0:KR, 128:256], T.FE[:, h, :], T.I1[:], True, True, "Ea%d Es%d E6 I1" % (h, h), "bV")
-            act(T.FT[0:KR, c], T.bV[0:KR, 128:256], F.Copy, "bV", "FT%d" % h)
+            act(T.FT[0:KR, half(h)], T.bV[0:KR, 128:256], F.Copy, "bV", "FT%d" % h)
 
         def mask(h):
-            mm(T.bF[:, 128:256], T.CX[0:KR, :], T.FT[0:KR, half(h)], True, True, "CX FT%d" % h, "bF")
-            act(T.Xs[:, half(h)], T.bF[:, 128:256], F.Sign, "bF", "Xs%d" % h)
+            mm(T.bS1[:, 0:128], T.CX[0:KR, :], T.FT[0:KR, half(h)], True, True, "CX FT%d" % h, "bS1")
+            act(T.Xq[:, half(h)], T.bS1[:, 0:128], F.Abs, "bS1", "Xq%d" % h)
+
+        def sign(h):
+            act(T.Xs[:, half(h)], T.Xq[:, half(h)], F.Sign, "Xq%d" % h, "Xs%d" % h)
 
         def change(h):
             c = half(h)
@@ -547,10 +505,9 @@ def rank_program(g, core, T, topo):
             nloc[0] += len(es)
             if t == 3:
                 dma("y", T.yt[:, c], T.T4[:, c], "T4%d" % h, "yt%d" % h)
-            if h == 0 and t < 2:
-                rot(t + 2)
-                tn(t + 2)
-                ct(t + 2)
+            if h == 0 and t < 3:
+                tn(t + 1)
+                turns(t + 1, t + 2)
 
         def count(k):
             if t == 3:
@@ -570,6 +527,8 @@ def rank_program(g, core, T, topo):
             if k == 5:
                 codes_in(t, 0)
             if k == 6:
+                if t == 0:
+                    late()
                 empties(t, 0)
 
         def next_(k):
@@ -580,11 +539,11 @@ def rank_program(g, core, T, topo):
             if t < 3 and k == 6:
                 empties(t + 1, 1)
 
-        steps = {"raw": raw, "price": price, "diff": diff, "term": term, "gains": gains, "last": last, "votes": votes, "tuples": tuples,
-                 "payload": payload, "level": level, "over": over, "claim": claim, "place": place, "streams": streams, "turn": turn, "column": column, "own": own,
-                 "equal": equal, "before": before, "where": where, "wlist": wlist, "kept": kept, "keep": keep, "lower": lower, "lists": lists,
-                 "credit": credit, "vote": vote, "keys": keys, "fields": fields, "features": features, "mask": mask, "change": change,
-                 "walk": walk, "count": count, "mine": mine, "next": next_}
+        steps = {"raw": raw, "price": price, "diff": diff, "term": term, "gains": gains, "votes": votes, "tuples": tuples, "payload": payload,
+                 "level": level, "over": over, "claim": claim, "place": place, "streams": streams, "column": column, "own": own,
+                 "equal": equal, "lower": lower, "lists": lists, "before": before, "keep": keep, "where": where, "wlist": wlist, "kept": kept,
+                 "credit": credit, "vote": vote, "keys": keys, "fields": fields, "features": features, "mask": mask, "sign": sign,
+                 "change": change, "walk": walk, "count": count, "mine": mine, "next": next_}
         for word in ORDER.split():
             steps[word[:-1]](int(word[-1]))
 
@@ -596,23 +555,27 @@ def rank_program(g, core, T, topo):
         bn = "bS%d" % j
         for k in range(16):
             mm(T[bn][:, a:b], T.I1[:], T.U[:, PAD + 16 * a + k:PAD + 16 * b:16], k == 0, k == 15, "I1 " + UALL, bn)
-        act(T.yc32[:, a:b], T[bn][:, a:b], F.Copy, bn, "yc0+")
-    for a in range(YT, W, 512):
-        b = min(a + 512, W)
-        scan(T.ysc[:, a - YT:b - YT], T.seg8[:, 0:b - a], T.U[:, PAD + a:PAD + b], A.mult, A.add, "seg8 " + UALL, "ysc+")
-    tt(T.yc32[:, nb:512], T.ysc[:, 7:W - YT:16], T.ysc[:, 15:W - YT:16], A.add, "ysc", "yc1")
-    dma("s", T.yc[:, 0:nb], T.yc32[:, 0:nb], "yc0", "yca")
-    dma("y", T.yc[:, nb:512], T.yc32[:, nb:512], "yc1", "ycb")
+        act(T.yc32[:, a:b], T[bn][:, a:b], F.Copy, bn, "ya%d" % j)
+    dma("s", T.yc[:, nb - 64:nb], T.yc32[:, nb - 64:nb], "ya1", "yca1")
+    dma("y", T.yc[:, 0:nb - 64], T.yc32[:, 0:nb - 64], "ya0", "yca0")
+    cuts = list(range(YT, W, 512)) + [W]
+    for a, b in zip(cuts, cuts[1:]):
+        scan(T.ysc[:, a - YT:b - YT], T.seg8[:, 0:b - a], T.U[:, PAD + a:PAD + b], A.mult, A.add, "seg8 " + UALL, "ys%d" % a)
+        if b in (cuts[-2], W):
+            j, (c, d) = b == W, ((YT, cuts[-3]), (cuts[-3], W))[b == W]
+            tt(T.yc32[:, c // 16:d // 16], T.ysc[:, c - YT + 7:d - YT:16], T.ysc[:, c - YT + 15:d - YT:16], A.add,
+               " ".join("ys%d" % x for x in cuts[:-1] if c <= x < d), "yb%d" % j)
+            dma("y", T.yc[:, c // 16:d // 16], T.yc32[:, c // 16:d // 16], "yb%d" % j, "ycb%d" % j)
     fin = [(q, n) for q, n in cnt.items() if n] + [("d%d" % k, 16) for k in range(ndma[0])]
     need("g", fin)
     g.wait_ge(T.sem.loc, nloc[0])
 
 
 ORDER = """
-raw7 raw5 raw6 price7 mine5 price8 mine0 raw8 streams1 tuples5 diff7 diff8 mine1 term6 mine2 tuples8 term5 tuples7 term7 votes1 term8
-mine3 price0 tuples6 raw2 gains1 mine4 payload1 raw1 raw3 price1 raw4 diff1 level1 tuples3 raw0 term2 vote1 term1 diff0 over1 tuples0
-votes0 term0 keys1 claim1 tuples1 keep2 place1 term4 tuples2 term3 tuples4 keep1 mine6 fields1 last3 last4 gains0 turn0 payload0 vote0
-features1 column1 level0 over0 keys0 change1 own1 mask1 claim0 fields0 walk1 place0 equal1 streams0 keep0 before1 features0 lower1
-column0 keep3 lists1 credit7 credit6 own0 credit5 where0 equal0 credit4 wlist0 change0 next5 lower0 mask0 kept0 lists0 walk0 next0
-credit3 count0 next6 next1 credit2 next2 credit1 next3 credit0 next4
+price6 mine5 streams1 price7 mine0 raw4 raw7 mine1 diff7 raw5 mine2 raw6 term7 term4 tuples7 diff6 votes1 price1 mine3 term6 raw1 tuples4
+tuples6 raw0 term5 tuples5 gains1 vote1 raw2 payload1 diff1 raw3 level1 tuples1 over1 tuples3 price0 claim1 term3 mine4 diff0 term2 votes0
+term1 term0 place1 keys1 keep0 tuples2 tuples0 gains0 fields1 vote0 keep3 features1 payload0 column1 mine6 change1 level0 over0 own1 keep2
+claim0 mask1 streams0 keys0 walk1 place0 fields0 equal1 before1 sign1 features0 column0 lower1 lists1 credit7 keep1 own0 credit6 change0
+equal0 mask0 sign0 walk0 credit5 lower0 where0 wlist0 next5 credit4 lists0 kept0 next6 next0 credit3 next1 credit2 next2 count0 credit1
+next3 credit0 next4
 """

from concourse.mybir import AluOpType as A, ActivationFunctionType as F

NONE = 2.0 ** 19
W = 8192
PAD = 16
TR = PAD + W
UW = TR + 32
TOP = 32768 + W - 1 + PAD
SQ = 20480.0
KR = 56
RHO = [0, 5, 10, 15]
GATHER = "ssvvvvss"
CUT = "sssvsvss"
VA, VB = 64, 192
YT = 4224

SCRATCH = {}


def _b(name, cols, dtype, where="sbuf"):
    SCRATCH[name] = (where, [128] + (list(cols) if isinstance(cols, (list, tuple)) else [cols]), dtype)


for _n, _c in (("U", UW), ("Mx", 4096), ("gb", 2048), ("D0G", 128), ("D0V", 128), ("segm", 128), ("seg8", 512), ("one8", 512),
               ("T0", 256), ("T1", 256), ("T2", 256), ("T3", 256), ("Tn0", 256), ("Tn1", 256), ("Tn2", 256),
               ("Tt", 256), ("Nn", 256), ("prb", 256), ("FT", 256), ("Xq", 256), ("Xs", 256), ("old", 256), ("hot", 256),
               ("onesb", 128), ("minus", 128), ("I1", 128), ("I256", 128), ("I64k", 128), ("BLKN", 128), ("TNb", 128), ("CTa", 128),
               ("CQ", 144), ("CX", 128), ("zb", 128), ("m16", 4), ("M1", 208), ("M2", (12, 16)), ("DK", 208), ("DKp", 32),
               ("E", 384), ("RT", 512), ("TN", 512), ("CT", 512), ("FE", (2, KR))):
    _b(_n, _c, "bfloat16")
for _n, _c in (("xx", 256), ("pd", 256), ("KS", (2, 256)), ("TH0", 8), ("TH", 8), ("TH20", 8), ("TH2", 8),
               ("Z", (8, 3, 16)), ("S10", 208), ("S11", 208), ("DD", 384), ("S2", 384),
               ("BLK", 128), ("BLKs", 128), ("GM", 128), ("mif", 128), ("mf", 128), ("mgf", 128), ("w8", 8), ("OH", 8), ("OHN", 16),
               ("colsf", 24), ("msum", 4), ("junk", 16), ("T4", 256), ("Tn3", 256), ("yc32", 512), ("mi2", 128), ("q1", 128),
               ("s2", 128), ("ge", 64)):
    _b(_n, _c, "float32")
for _n, _c in (("tsti", 256), ("z", 256), ("ci", 256), ("KI", (2, 16)), ("DEC", 64), ("XI", 16), ("thr", 8), ("thb", 8), ("pc", 8)):
    _b(_n, _c, "int32")
for _n, _c in (("got", 4096), ("PK", 512 + 16 * (VB - VA)), ("PX", 4096), ("K1", 4096), ("prx", 256), ("prm", 256), ("pz", 256), ("pb", 128),
               ("c16", 8), ("BLKv", 128), ("nI", 128), ("Ind", 8), ("R", 256), ("If", 128), ("If16", 128), ("nIf", 128), ("hib", 256),
               ("ysc", W - YT)):
    _b(_n, _c, "float16")
for _n, _c in (("off", 256), ("l0", 16), ("l1", 16), ("og", 8)):
    _b(_n, _c, "uint16")
for _n in ("S0", "S1", "G", "V", "F", "L", "C1"):
    _b("b" + _n, 512, "float32", "psum")
_b("bC2", (32, 16), "float32", "psum")

SEMAPHORES = ["cv", "cs", "ct", "cg", "loc"] + ["d%d" % k for k in range(12)] + ["a%d%d" % (k, h) for k in range(1, 5) for h in range(2)]


def rank_program(g, core, T, topo):
    rank = T.rank_of(core)
    if rank is None:
        return
    N = len(T.cores)
    eng = {"v": g.vector, "s": g.scalar, "t": g.tensor, "g": g, "y": g.sync}
    cnt = {"v": 0, "s": 0, "t": 0, "g": 0}
    known = {q: {} for q in eng}
    clk = {}
    wr, rd, bank = {}, {}, {}
    ndma = [0]
    nloc = [0]

    def sem_of(e):
        return T.sem["c" + e] if e in cnt else T.sem[e]

    def need(q, deps):
        best = {}
        for e, n in deps:
            if known[q].get(e, 0) < n and best.get(e, 0) < n:
                best[e] = n
        for e in list(best):
            for e2 in list(best):
                if e2 != e and e in best and e2 in best and clk.get((e2, best[e2]), {}).get(e, 0) >= best[e]:
                    del best[e]
        for e, n in best.items():
            eng[q].wait_ge(sem_of(e), n)
            for k, v in clk.get((e, n), {}).items():
                if known[q].get(k, 0) < v:
                    known[q][k] = v
            known[q][e] = n

    def deps_of(q, reads, writes):
        deps = []
        for t in list(reads) + list(writes):
            if t[0] == "b":
                for e, n in bank.get(t, {}).items():
                    if e != q:
                        deps.append((e, n))
        for t in reads:
            w = wr.get(t)
            if w is not None and not (t[0] == "b" and w[0] != q):
                deps.append(w)
        for t in writes:
            if t[0] != "b":
                w = wr.get(t.rstrip("+"))
                if w is not None and not (t[-1] == "+" and w[0] == q):
                    deps.append(w)
                deps.extend(rd.get(t.rstrip("+"), {}).items())
        return deps

    def note(q, e, n, reads, writes):
        c = dict(known[q])
        c[e] = n
        clk[(e, n)] = c
        for t in reads:
            if t[0] == "b":
                bank.setdefault(t, {})[e] = n
            else:
                rd.setdefault(t, {})[e] = n
        for t in writes:
            t = t.rstrip("+")
            if t[0] == "b":
                bank.setdefault(t, {})[e] = n
            else:
                rd[t] = {}
            wr[t] = (e, n)

    def op(q, fn, reads, writes):
        reads = reads.split()
        writes = writes.split()
        need(q, deps_of(q, reads, writes))
        ins = fn()
        cnt[q] += 1
        ins.then_inc(T.sem["c" + q], 1)
        note(q, q, cnt[q], reads, writes)

    def dma(q, out, in_, reads, writes):
        reads = reads.split()
        writes = writes.split()
        need(q, deps_of("dma", reads, writes))
        name = "d%d" % ndma[0]
        ndma[0] += 1
        eng[q].dma_start(out, in_).then_inc(T.sem[name], 16)
        note(q, name, 16, reads, writes)

    V, S, P = g.vector, g.scalar, g.tensor

    def ts(out, in0, s1, s2, op0, op1, r, w):
        if op1 is None:
            op("v", lambda: V.tensor_scalar(out, in0, s1, None, op0), r, w)
        else:
            op("v", lambda: V.tensor_scalar(out, in0, s1, s2, op0, op1), r, w)

    def tt(out, a, b, o, r, w):
        op("v", lambda: V.tensor_tensor(out, a, b, o), r, w)

    def cp(out, in_, r, w):
        op("v", lambda: V.tensor_copy(out, in_), r, w)

    def scan(out, d0, d1, o0, o1, r, w, init=0.0):
        op("v", lambda: V.tensor_tensor_scan(out, d0, d1, init, o0, o1), r, w)

    def act(out, in_, func, r, w, **k):
        op("s", lambda: S.activation(out, in_, func, **k), r, w)

    def lin(out, in_, scale, bias, r, w):
        act(out, in_, F.Identity, r, w, scale=scale, bias=bias)

    def mm(out, l, x, st, sp, r, w):
        op("t", lambda: P.matmul(out, l, x, st, sp), r, w)

    def ms(ap, c, w):
        op("v", lambda: V.memset(ap, c), "", w)

    def sel(out, in_, pat, cmp, fill, base, cm, r, w):
        op("g", lambda: g.affine_select(out, in_, pat, cmp, fill, base, cm), r, w)

    def half(h):
        return slice(128 * h, 128 * h + 128)

    dma("y", T.tsti[:], T.tst[:], "", "tsti")
    dma("s", T.prb[:], T.pr[:], "", "prb")
    dma("y", T.thr[0:1, 0:8], T.th[:], "", "thr")
    dma("s", T.U[:, PAD + 4096:TR], T.cov[:, 4096:W], "", "Ub")
    dma("y", T.U[:, PAD:PAD + 4096], T.cov[:, 0:4096], "", "Ua")
    UALL = "Ua Ub Uc"

    PI, PJ, PG, P8, FF, PP, J0, J1, CTA, CQC, NW, R3, K0, KC = range(14)
    RUNS = ((0, VA, False), (VA, VB, True), (VB, 256, False))
    FL = {"allow_small_or_imprecise_dtypes": True}

    def col(k):
        return T.colsf[:, k:k + 1]

    def oh(f):
        return T.OH[:, f:f + 1]

    def iota(out, pat, base, cm, w, **k):
        op("g", lambda: g.iota(out, pat, base, cm, **k), "", w)

    iota(T.pc[:, 0:2], [[15, 2]], 0, 1, "pc0")
    iota(T.mgf[:], [[1, 8], [0, 16]], 0, 0, "mgf", **FL)
    iota(T.mif[:], [[0, 8], [1, 16]], 0, 0, "mif", **FL)
    iota(T.w8[:], [[1, 8]], 0, 0, "w8", **FL)
    iota(T.mf[:], [[1, 128]], 0, 0, "mf", **FL)
    iota(T.q1[:], [[0, 8], [-1, 16]], 15, 0, "q1", **FL)

    def codes_in(t, h):
        src, c = "T%d" % t, half(h)
        mm(T.bL[:, 128:256], T.onesb[0:1, :], T.onesb[0:1, :], True, False, "onesb", "bL")
        mm(T.bL[:, 128:256], T.RT[:, 128 * t:128 * t + 128], T[src][:, c], False, True, "RT%d %s%d" % (t, src, h), "bL")
        lin(T.xx[:, c], T[src][:, c], -2.0, -1.0, "%s%d" % (src, h), "xx%d" % h)

    def codes(t, h, k):
        c = half(h)
        if k == 0:
            tt(T.pd[:, c], T.bL[:, 128:256], T.xx[:, c], A.mult, "bL xx%d" % h, "pd%d" % h)
        if k == 1:
            ts(T.z[:, c], T.pd[:, c], col(KC + t), -2.0 ** 30, A.add, A.max, "pd%d fk" % h, "z%d" % h)
        if k == 2:
            ts(T.ci[:, c], T.z[:, c], 4, (W - 1) | 0x7FFF8000, A.arith_shift_right, A.bitwise_and, "z%d" % h, "ci%d" % h)
        if k == 3:
            ts(T.off[:, c], T.ci[:, c], -1.0, float(TOP), A.mult, A.add, "ci%d" % h, "off%d" % h)
        if k == 4:
            ts(T.hib[:, c], T.off[:, c], 1.0 / 32, 1280.0 - 0.484375 - PAD / 32, A.mult, A.add, "off%d" % h, "hib%d" % h)

    def empties(t, h):
        src, c = "T%d" % t, half(h)
        act(T.Nn[:, c], T[src][:, c], F.Relu, "%s%d" % (src, h), "Nn%d" % h, bias=1.0 - NONE)
        if t < 3:
            lin(T.Tt[:, c], T[src][:, c], 1.0, T.OHN[:, RHO[t]:RHO[t] + 1], "%s%d OHN" % (src, h), "Tt%d" % h)
        else:
            act(T.Tt[:, c], T[src][:, c], F.Relu, "%s%d fr" % (src, h), "Tt%d" % h, scale=-1.0, bias=col(R3))
            lin(T.Tt[:, c], T.Tt[:, c], -1.0, 256.0, "Tt%d" % h, "Tt%d" % h)

    def prices(h, i):
        cp(T.PX[:, 2048 * h + i:2048 * h + 2048:16], T.prx[:, half(h)], "prx", "PX%d+" % h)

    ms(T.onesb[:], 1.0, "onesb")
    ms(T.PK[:], 1.0 / 16, "PK")
    ts(T.pc[:, 2:4], T.pc[:, 0:2], 15, None, A.bitwise_and, None, "pc0", "pc1+")
    for k, (sh, msk) in enumerate(((4, 7), (0, 7), (3, 15))):
        ts(T.pc[:, 4 + k:5 + k], T.pc[:, 0:1], sh, msk, A.arith_shift_right, A.bitwise_and, "pc0", "pc1+")
    cp(col(PP), T.pc[:, 0:1], "pc0", "fp")
    cp(T.colsf[:, PI:PI + 5], T.pc[:, 2:7], "pc1", "f")
    for a, b, v in RUNS[::-1]:
        lin(T.prx[:, a:b], T.prb[:, a:b], 1.0, -512.0 if v else 384.0, "prb", "prx+")
    for a, b, v in RUNS:
        lin(T.prm[:, a:b], T.prb[:, a:b], 1.0 if v else 0.0, -640.0 if v else -512.0, "prb", "prm+")
    ts(T.BLK[:], T.mgf[:], col(PG), None, A.is_equal, None, "mgf f", "BLK")
    ts(T.mi2[:], T.mif[:], col(PJ), 2.0, A.is_equal, A.mult, "mif f", "mi2")
    ts(T.pd[:, half(1)], T.tsti[:, half(1)], 256.0, NONE, A.is_ge, A.mult, "tsti", "pd1")
    ts(col(K0), col(PI), -16.0 * 613, 2.0 ** 20 - 1, A.mult, A.add, "f", "fk0")
    tt(T.RT[:, 0:128], T.mi2[:], T.BLK[:], A.mult, "mi2 BLK", "RT0")
    tt(T.T0[:, half(1)], T.pd[:, half(1)], T.tsti[:, half(1)], A.max, "pd1 tsti", "T01")
    ts(T.colsf[:, KC:KC + 4], T.w8[:, 0:4], -16.0 * 77, col(K0), A.mult, A.add, "w8 fk0", "fk")
    ts(T.pd[:, half(0)], T.tsti[:, half(0)], 256.0, NONE, A.is_ge, A.mult, "tsti", "pd0")
    ts(T.I1[:], T.mf[:], col(PP), None, A.is_equal, None, "mf fp", "I1")
    codes_in(0, 1)
    tt(T.T0[:, half(0)], T.pd[:, half(0)], T.tsti[:, half(0)], A.max, "pd0 tsti", "T00")
    ts(T.segm[:], T.mif[:], 0.0, None, A.is_gt, None, "mif", "segm")
    ts(T.DKp[:], T.mif[:, 0:32], col(PI), 64.0, A.is_equal, A.mult, "mif f", "DKp")
    ts(T.OH[:], T.w8[:], col(FF), None, A.is_equal, None, "w8 f", "OH")
    ts(T.ge[:], T.mif[:, 0:64], col(PI), -64.0, A.is_ge, A.mult, "mif f", "ge")
    ms(T.M2[:], 2.5, "M2")
    ts(T.GM[:], T.mgf[:], col(P8), None, A.is_equal, None, "mgf f", "GM")
    for n, v in (("If", 1.0), ("nI", -1.0), ("I256", 256.0), ("If16", 16.0), ("nIf", -16.0)):
        act(T[n][:], T.I1[:], F.Copy, "I1", n, scale=v)
    act(T.BLKN[:], T.BLK[:], F.Copy, "BLK", "BLKN", scale=NONE)
    for k in range(4):
        codes(0, 1, k)
        for i in range(4 * k, 4 * k + 4):
            prices(1, i)
    ms(T.U[:, 0:PAD], -128.0, "Uc+")
    ms(T.U[:, TR:UW], 0.0, "Uc+")
    ms(T.PK[:, 15:512:16], -512.0, "PK")
    cp(T.PK[:, 512 + 15:512 + 16 * (VB - VA):16], T.prm[:, VA:VB], "prm", "PK+")
    codes(0, 1, 4)
    ts(T.OHN[:], T.mif[:, 0:16], col(PI), NONE, A.is_equal, A.mult, "mif f", "OHN")
    ts(T.Ind[:], T.w8[:], col(PG), 4096.0, A.is_equal, A.mult, "w8 f", "Ind")
    cp(T.og[:], T.w8[:], "w8", "og")
    for i in range(16):
        prices(0, i)

    iota(T.DK[:], [[0, 208]], 0, 0, "DK", **FL)
    iota(T.Z[:, :, 2, :], [[0, 8], [0, 16]], 0, 0, "Z0 Z1", **FL)
    iota(T.FE[:, :, 48:56], [[0, 2], [0, 8]], 1, 0, "E6", **FL)
    iota(T.DD[:], [[0, 384]], 0, 0, "DD0 DD1", **FL)
    iota(T.minus[0:1, :], [[0, 128]], -1, 0, "minus", **FL)
    for k in range(2):
        iota(T.DD[:, 16 * k:384:48], [[0, 8]], -64, 0, "DD0+ DD1+" if k else "DD0 DD1", **FL)
    sel(T.TNb[:], T.BLKN[:], [[1, 128]], A.is_gt, 0.0, 0, -1, "BLKN", "TNb")
    iota(T.zb[:], [[0, 128]], 0, 0, "zb", **FL)
    op("g", lambda: g.partition_broadcast(T.thb[:], T.thr[0:1, 0:8], 128), "thr", "thb")
    sel(T.TNb[:], T.TNb[:], [[1, 128]], A.not_equal, -NONE, 0, -1, "TNb", "TNb")
    iota(T.CQ[0:32, :], [[0, 144]], 0, 0, "CQ", **FL)

    def tn(t):
        sel(T.TN[:, 128 * t:128 * t + 128], T.TNb[:], [[0, 8], [1, 16]], A.not_equal, 0.0, -RHO[t], 0, "TNb", "TN%d" % t)

    def turns(t, u):
        n, a = "CT%d" % t, 128 * t
        sel(T.CT[0:KR, a:a + 128], T.CTa[0:KR, :], [[0, 8], [1, 16]], A.not_equal, 0.0, -RHO[t], 0, "CTa", n)
        c = T.CT[0:KR, a + RHO[t]:a + 128:16]
        for k, (f, v) in enumerate(((1, -16.0), (2, 1.0), (4, NONE), (6, 240.0))):
            if u < 4:
                b, m = T.RT[:, 128 * u:128 * u + 128], "RT%d" % u
                pat, cmp, fill, base, cm = (([[-16, 8], [-1, 16]], A.not_equal, 2.0, -1 - u, 1), ([[-16, 8], [-1, 16]], A.not_equal, 2.0, 15 - u, 1),
                                            ([[-16, 8], [0, 16]], A.is_ge, 0.0, 0, 1), ([[16, 8], [0, 16]], A.is_ge, 0.0, 15, -1))[k]
                sel(b, b if k else T.zb[:], pat, cmp, fill, base, cm, m if k else "zb", m)
            sel(c, c, [[-1, 8]], A.not_equal, v, -8 * f, 1, n, n)

    lin(T.D0G[:], T.segm[:], 2.0 ** 25 + 16, -2.0 ** 25, "segm", "D0G")
    act(T.BLKv[:], T.BLK[:], F.Copy, "BLK", "BLKv", scale=4096.0)
    act(T.I64k[:], T.I1[:], F.Copy, "I1", "I64k", scale=65536.0)
    act(T.BLKs[:], T.BLK[:], F.Copy, "BLK", "BLKs", scale=-2.0 ** -14)
    lin(T.D0V[:], T.segm[:], 2.0 ** 27 + 256, -2.0 ** 27, "segm", "D0V")
    lin(col(NW), oh(1), -1.0, 0.0, "OH", "fn")
    lin(T.pz[:], T.prm[:], 1.0, 128.0, "prm", "pz")
    lin(col(J0), col(PI), 1.0, float(TR), "f", "fj+")
    lin(col(J1), col(PI), 1.0, float(TR + 16), "f", "fj+")
    lin(T.s2[:], T.q1[:], oh(6), col(NW), "q1 OH fn", "s2")
    for k in range(4):
        act(T.DK[:, 48 * k:48 * k + 32], T.DKp[:], F.Copy, "DKp", "DK+")
        f, v = ((3, 1.0), (4, -NONE), (5, -NONE / 2), (6, 2.5 * NONE))[k]
        lin(col(CTA), oh(f), v, col(CTA) if k else 0.0, "OH fa", "fa")
        if k < 2:
            lin(T.M2[:, 2 * k:12:3, :], T.ge[:], 1.0, 2.5, "ge", "M2+")
    lin(T.M1[:], T.DK[:], -0.5, 34.5, "DK", "M1")
    act(T.CTa[:], T.GM[:], F.Copy, "GM fa", "CTa", scale=col(CTA))
    ts(T.TH0[:], T.thb[:], 256.0, -SQ, A.mult, A.add, "thb", "TH0")
    ts(T.TH20[:], T.thb[:], 256.0, None, A.mult, None, "thb", "TH20")

    def late():
        tt(T.CX[0:KR, :], T.s2[0:KR, :], T.GM[0:KR, :], A.mult, "s2 GM", "CX")
        empties(0, 1)
        lin(col(CQC), col(PI), 16.0, 15.0, "f", "fq")
        lin(T.pb[:], T.prm[:, 0:128], 1.0, 640.0, "prm", "pb")
        lin(T.c16[:], T.w8[:], 256.0, col(CQC), "w8 fq", "c16")
        lin(col(R3), T.OHN[:, RHO[3]:RHO[3] + 1], -1.0, 256.0, "OHN", "fr")

    tn(0)
    turns(0, 1)
    iota(T.one8[:], [[0, 512]], 1, 0, "one8", **FL)
    sel(T.CQ[0:32, :], T.CQ[0:32, :], [[1, 144]], A.not_equal, -1.0, -15, -16, "CQ", "CQ")
    sel(T.seg8[:], T.one8[:], [[0, 64], [1, 8]], A.is_gt, 0.0, 0, 0, "one8", "seg8")

    win = T.U[:, 0:UW]

    def visit(t):
        th, thn = (T.TH0, "TH0") if t == 0 else (T.TH, "TH")
        th2, thn2 = (T.TH20, "TH20") if t == 0 else (T.TH2, "TH2")

        def piece(p):
            return slice(512 * p, 512 * p + 512)

        def names(n, h):
            return " ".join("%s%d" % (n, p) for p in range(4 * h, 4 * h + 4))

        def raw(p):
            c, w, r = piece(p), win.indirect(T.off[:, 32 * p:32 * p + 32]), "off%d " % (p // 4) + UALL
            if GATHER[p] == "s":
                act(T.got[:, c], w, F.Identity, r, "got%d" % p, bias=384.0)
            else:
                tt(T.got[:, c], w, T.PX[:, c], A.subtract, "PX%d " % (p // 4) + r, "got%d" % p)

        def price(p):
            bn = "bS%d" % (p % 2)
            mm(T[bn][:], T.nI[:], T.PX[:, piece(p)], True, False, "nI PX%d" % (p // 4), bn)

        def diff(p):
            bn = "bS%d" % (p % 2)
            mm(T[bn][:], T.If[:], T.got[:, piece(p)], False, True, "If got%d" % p, bn)

        def term(p):
            c, bn = piece(p), "bS%d" % (p % 2)
            if GATHER[p] == "s":
                act(T.Mx[:, c], T[bn][:], F.Relu, bn, "Mx%d" % p)
            elif CUT[p] == "s":
                act(T.Mx[:, c], T.got[:, c], F.Relu, "got%d" % p, "Mx%d" % p, bias=-512.0)
            else:
                ts(T.Mx[:, c], T.got[:, c], -512.0, 0.0, A.add, A.max, "got%d" % p, "Mx%d" % p)

        def gains(h):
            for i in range(16):
                mm(T.bG[:, 0:128], T.Mx[:, 2048 * h + i:2048 * h + 2048:16], T.I256[:], i == 0, False, names("Mx", h) + " I256", "bG")

        def votes(h):
            mm(T.bV[:, 0:128], T.pz[:, half(h)], T.BLKv[:], True, False, "pz BLKv", "bV")
            for i in range(16):
                mm(T.bV[:, i:128:16], T.got[:, 2048 * h + i:2048 * h + 2048:16], T.Ind[:], False, False, names("got", h) + " Ind", "bV")
            mm(T.bV[:, 0:128], T.hib[:, half(h)], T.If[:], False, True, "hib%d If" % h, "bV")

        def tuples(p):
            a = 0 if GATHER[p] == "s" else 512 + 512 * p - 16 * VA
            scan(T.K1[:, piece(p)], T.got[:, piece(p)], T.PK[:, a:a + 512], A.max, A.add, "PK got%d" % p, "K1%d" % p)

        def payload(h):
            k1, n = T.K1[:, 2048 * h + 15:2048 * h + 2048:16], names("K1", h)
            ts(T.R[:, half(h)], k1, SQ / 16 - 15.0 / 32, SQ / 16 - 143.0, A.add, A.max, n, "R%d" % h)
            mm(T.bG[:, 0:128], k1, T.If16[:], False, False, n + " If16", "bG")
            mm(T.bG[:, 0:128], T.R[:, half(h)], T.nIf[:], False, True, "R%d nIf" % h, "bG")

        def level(h):
            scan(T.KS[:, h, 0:128], T.D0G[:], T.bG[:, 0:128], A.add, A.max, "D0G bG", "GKs%d" % h)

        def over(h):
            tt(T.XI[:, 8 * h:8 * h + 8], T.KS[:, h, 15:128:16], th[:], A.subtract, "GKs%d %s" % (h, thn), "XI%d" % h)

        def claim(h):
            ts(T.DEC[:, 32 * h:32 * h + 8], T.XI[:, 8 * h:8 * h + 8], 15 | 0x40000000, None, A.bitwise_and, None, "XI%d" % h, "RP%d" % h)

        def place(h):
            tt(T.hot[:, half(h)], T.DEC[:, 32 * h:32 * h + 8].indirect(T.og[:]), T.q1[:], A.is_equal, "RP%d og q1" % h, "hot%d" % h)
            mm(T.bF[:, 0:128], T.onesb[0:1, :], T.minus[0:1, :], True, False, "onesb minus", "bF")
            mm(T.bF[:, 0:128], T.hot[:, half(h)], T.I64k[:], False, True, "hot%d I64k" % h, "bF")

        FIRST = ("bS0", "bC1")

        def streams(h):
            mm(T[FIRST[h]][:, 0:208], T.I1[:], T.M1[:], True, False, "I1 M1", FIRST[h])
            mm(T.bC2[:, 12 * h:12 * h + 12, :], T.I1[:], T.M2[:], True, False, "I1 M2", "bC2")

        def column(h):
            b = slice(4 * h, 4 * h + 4)
            tt(T.Z[:, b, 0:2, :], T.bF[:, 0:128], T.ci[:, half(h)], A.min, "bF ci%d" % h, "Z%d" % h)
            mm(T[FIRST[h]][:, 0:192], T.BLKs[:], T.Z[:, b, :, :], False, True, "BLKs Z%d" % h, FIRST[h])
            for e, u in ((0, 0), (1, 0), (2, 1)):
                mm(T.bC2[:, 12 * h + e:12 * h + 12:3, :], T.BLKs[:], T.Z[:, b, u, :], False, e == 2, "BLKs Z%d" % h, "bC2")

        def own(h):
            scan(T["S1%d" % h][:], T.DK[:], T[FIRST[h]][:, 0:208], A.add, A.min, "DK " + FIRST[h], "S1%d" % h, 64.0)

        def equal(h):
            s1, a = T["S1%d" % h], 192 * h
            for u in range(2):
                act(T.DD[:, a + 15 + 32 * u:a + 192:48], s1[:, 15 + 16 * u:192:48], F.Copy, "S1%d" % h, "DD%d+" % h)
            tt(T.E[:, a:a + 192], s1[:, 16:208], T.bC2[:, 12 * h:12 * h + 12, :], A.is_equal, "S1%d bC2" % h, "E%d" % h)

        def lower(h):
            c = slice(192 * h, 192 * h + 192)
            scan(T.S2[:, c], T.DD[:, c], T.E[:, c], A.add, A.max, "DD%d E%d" % (h, h), "S2%d" % h)

        def lists(h):
            for u in range(2):
                ts(T.l1[:, 8 * h + u:8 * h + 8:2], T.S2[:, 192 * h + 15 + 32 * u:192 * h + 192:48], 16384.0, col(J0 + u), A.mult, A.min,
                   "S2%d fj" % h, "l1%d+" % h)

        def before(h):
            for u in range(2):
                ts(T.l0[:, 8 + u:16:2], T.S11[:, 15 + 16 * u:192:48], 16384.0, float(TR), A.mult, A.min, "S11", "l01+")
            act(T.old[:, half(1)], win.indirect(T.l0[:, 8:16]), F.Copy, "l01 " + UALL, "old1")

        def keep(p):
            lin(T.gb[:, piece(p)], T.got[:, piece(p)], 1.0, -512.0, "got%d" % p, "gb%d" % p)

        def where(h):
            mm(T.bG[:, 256:264], T.If[:], T.c16[:], True, False, "If c16", "bG")
            for j in range(16):
                mm(T.bG[:, 256:264], T.CQ[0:32, 15 - j:143 - j], T.FT[0:32, j:128:16], False, j == 15, "CQ FT0", "bG")

        def wlist(h):
            cp(T.l0[:, 0:8], T.bG[:, 256:264], "bG", "l00")

        def kept(h):
            tt(T.old[:, half(0)], T.gb[:].indirect(T.l0[:, 0:8]), T.pb[:], A.add, "l00 pb " + names("gb", 0), "old0")

        def credit(p):
            c, h = slice(32 * p, 32 * p + 32), p // 4
            tt(win.indirect(T.l1[:, 2 * p:2 * p + 2]), T.old[:, c], T.Xs[:, c], A.mult, "l1%d old%d Xs%d" % (h, h, h), UALL)

        def vote(h):
            scan(T.KS[:, h, 128:256], T.D0V[:], T.bV[:, 0:128], A.add, A.max, "D0V bV", "VKs%d" % h)

        def keys(h):
            ts(T.KI[:, h, :], T.KS[:, h, 15:256:16], SQ, 240.0, A.add, A.max, "GKs%d VKs%d" % (h, h), "KI%d" % h)
            act(T.FE[:, h, 40:48], T.KS[:, h, 128 + 15:256:16], F.Sign, "VKs%d" % h, "Es%d" % h)

        def fields(h):
            a = 32 * h
            for k in range(1, 3):
                ts(T.DEC[:, a + 8 * k:a + 8 * k + 8], T.KI[:, h, 0:8], 4 * k, 15, A.arith_shift_right, A.bitwise_and, "KI%d" % h, "DEC%d+" % h)
            ts(T.DEC[:, a + 24:a + 32], T.KI[:, h, 8:16], 255, None, A.bitwise_and, None, "KI%d" % h, "DEC%d+" % h)
            tt(T.FE[:, h, 32:40], T.KI[:, h, 0:8], th2[:], A.is_lt, "KI%d %s" % (h, thn2), "Ea%d+" % h)

        def features(h):
            ts(T.FE[:, h, 0:32], T.DEC[:, 32 * h:32 * h + 32], 255.0, None, A.min, None, "RP%d DEC%d" % (h, h), "Ea%d+" % h)
            mm(T.bV[0:KR, 128:256], T.FE[:, h, :], T.I1[:], True, True, "Ea%d Es%d E6 I1" % (h, h), "bV")
            act(T.FT[0:KR, half(h)], T.bV[0:KR, 128:256], F.Copy, "bV", "FT%d" % h)

        def mask(h):
            mm(T.bS1[:, 0:128], T.CX[0:KR, :], T.FT[0:KR, half(h)], True, True, "CX FT%d" % h, "bS1")
            act(T.Xq[:, half(h)], T.bS1[:, 0:128], F.Abs, "bS1", "Xq%d" % h)

        def sign(h):
            act(T.Xs[:, half(h)], T.Xq[:, half(h)], F.Sign, "Xq%d" % h, "Xs%d" % h)

        def change(h):
            c = half(h)
            mm(T.bL[:, 0:128], T.TN[:, 128 * t:128 * t + 128], T.Nn[:, c], True, False, "TN%d Nn%d" % (t, h), "bL")
            mm(T.bL[:, 0:128], T.CT[0:KR, 128 * t:128 * t + 128], T.FT[0:KR, c], False, True, "CT%d FT%d" % (t, h), "bL")

        def walk(h):
            c, n = half(h), "Tn%d%d" % (t, h)
            tt(T["Tn%d" % t][:, c], T.bL[:, 0:128], T.Tt[:, c], A.min, "bL Tt%d" % h, n)
            dst = T.cores[(rank + 1) % N] if t < 3 else T.cores[(rank - 3) % N]
            es = topo.engines(core, dst)[::2]
            need("g", deps_of("g", [n], []))
            rid, pid, _s = topo.addr(dst)
            a = "a%d%d" % (t + 1, h)
            g.remote_dma(T["T%d" % (t + 1)][:, c], T["Tn%d" % t][:, c], T.sem[a], T.sem.loc, pid, rid, sum(1 << e for e in es))
            wr["T%d%d" % (t + 1, h)] = (a, len(es))
            nloc[0] += len(es)
            if t == 3:
                dma("y", T.yt[:, c], T.T4[:, c], "T4%d" % h, "yt%d" % h)
            if h == 0 and t < 3:
                tn(t + 1)
                turns(t + 1, t + 2)

        def count(k):
            if t == 3:
                return
            for h in range(2):
                mm(T.bV[:, 256 + 8 * h:264 + 8 * h], T.onesb[:], T.FE[:, h, 32:40], True, True, "onesb Ea%d" % h, "bV")
            act(T.junk[:], T.bV[:, 256:272], F.Copy, "bV", "junk msum", accum_out=T.msum[:, 0:1])
            lin(T.m16[:, 0:1], T.msum[:, 0:1], 1.0, 49152.0 - 127.5, "msum", "m16")
            lin(T.msum[:, 1:2], T.msum[:, 0:1], 256.0, 256.0 * 49152, "msum", "mb")
            lin(T.msum[:, 2:3], T.m16[:, 0:1], -256.0, T.msum[:, 1:2], "m16 mb", "mc")
            lin(T.TH[:], T.TH0[:], 1.0, T.msum[:, 2:3], "TH0 mc", "TH")
            lin(T.TH2[:], T.TH20[:], 1.0, T.msum[:, 2:3], "TH20 mc", "TH2")

        def mine(k):
            if k < 5:
                codes(t, 0, k)
            if k == 5:
                codes_in(t, 0)
            if k == 6:
                if t == 0:
                    late()
                empties(t, 0)

        def next_(k):
            if t < 3 and k < 5:
                codes(t + 1, 1, k)
            if t < 3 and k == 5:
                codes_in(t + 1, 1)
            if t < 3 and k == 6:
                empties(t + 1, 1)

        steps = {"raw": raw, "price": price, "diff": diff, "term": term, "gains": gains, "votes": votes, "tuples": tuples, "payload": payload,
                 "level": level, "over": over, "claim": claim, "place": place, "streams": streams, "column": column, "own": own,
                 "equal": equal, "lower": lower, "lists": lists, "before": before, "keep": keep, "where": where, "wlist": wlist, "kept": kept,
                 "credit": credit, "vote": vote, "keys": keys, "fields": fields, "features": features, "mask": mask, "sign": sign,
                 "change": change, "walk": walk, "count": count, "mine": mine, "next": next_}
        for word in ORDER.split():
            steps[word[:-1]](int(word[-1]))

    for t in range(4):
        visit(t)

    nb = YT // 16
    for j, (a, b) in enumerate(((0, nb - 64), (nb - 64, nb))):
        bn = "bS%d" % j
        for k in range(16):
            mm(T[bn][:, a:b], T.I1[:], T.U[:, PAD + 16 * a + k:PAD + 16 * b:16], k == 0, k == 15, "I1 " + UALL, bn)
        act(T.yc32[:, a:b], T[bn][:, a:b], F.Copy, bn, "ya%d" % j)
    dma("s", T.yc[:, nb - 64:nb], T.yc32[:, nb - 64:nb], "ya1", "yca1")
    dma("y", T.yc[:, 0:nb - 64], T.yc32[:, 0:nb - 64], "ya0", "yca0")
    cuts = list(range(YT, W, 512)) + [W]
    for a, b in zip(cuts, cuts[1:]):
        scan(T.ysc[:, a - YT:b - YT], T.seg8[:, 0:b - a], T.U[:, PAD + a:PAD + b], A.mult, A.add, "seg8 " + UALL, "ys%d" % a)
        if b in (cuts[-2], W):
            j, (c, d) = b == W, ((YT, cuts[-3]), (cuts[-3], W))[b == W]
            tt(T.yc32[:, c // 16:d // 16], T.ysc[:, c - YT + 7:d - YT:16], T.ysc[:, c - YT + 15:d - YT:16], A.add,
               " ".join("ys%d" % x for x in cuts[:-1] if c <= x < d), "yb%d" % j)
            dma("y", T.yc[:, c // 16:d // 16], T.yc32[:, c // 16:d // 16], "yb%d" % j, "ycb%d" % j)
    fin = [(q, n) for q, n in cnt.items() if n] + [("d%d" % k, 16) for k in range(ndma[0])]
    need("g", fin)
    g.wait_ge(T.sem.loc, nloc[0])


ORDER = """
price6 mine5 streams1 price7 mine0 raw4 raw7 mine1 diff7 raw5 mine2 raw6 term7 term4 tuples7 diff6 votes1 price1 mine3 term6 raw1 tuples4
tuples6 raw0 term5 tuples5 gains1 vote1 raw2 payload1 diff1 raw3 level1 tuples1 over1 tuples3 price0 claim1 term3 mine4 diff0 term2 votes0
term1 term0 place1 keys1 keep0 tuples2 tuples0 gains0 fields1 vote0 keep3 features1 payload0 column1 mine6 change1 level0 over0 own1 keep2
claim0 mask1 streams0 keys0 walk1 place0 fields0 equal1 before1 sign1 features0 column0 lower1 lists1 credit7 keep1 own0 credit6 change0
equal0 mask0 sign0 walk0 credit5 lower0 where0 wlist0 next5 credit4 lists0 kept0 next6 next0 credit3 next1 credit2 next2 count0 credit1
next3 credit0 next4
"""
